import numpy as np
import ml_dtypes


def mxq(x, axis, fmt="e4m3"):
    dtype, down = {"e4m3": (ml_dtypes.float8_e4m3fn, 7), "e5m2": (ml_dtypes.float8_e5m2, 14)}[fmt]
    v = np.moveaxis(np.asarray(x, np.float32).astype(ml_dtypes.bfloat16).astype(np.float64), axis, -1)
    blocks = v.reshape(v.shape[:-1] + (-1, 32))
    amax = np.abs(blocks).max(-1, keepdims=True)
    byte = np.maximum(np.where(amax > 0, np.frexp(amax)[1] - 1 + 127, 0) - down, 1)
    scale = np.exp2(byte - 127.0)
    codes = (blocks / scale).astype(np.float32).astype(dtype).astype(np.float64)
    return np.moveaxis((codes * scale).reshape(v.shape), -1, axis)


WIDE = False


def mx_kscale(k):
    if not WIDE:
        return np.ones(k)
    levels = np.array([10, -10, 5, -5, 0])
    if k % 512:
        return np.exp2(np.random.permutation(np.resize(levels, k // 32))).repeat(32)
    a = np.empty((k // 512, 16))
    for p in range(k // 512):
        a[p, :8] = np.random.permutation(np.resize(levels, 8))
        for g in range(8):
            far = levels[np.abs(levels - a[p, g]) >= 10]
            a[p, g + 8] = far[np.random.randint(len(far))]
    return np.exp2(a.ravel()).repeat(32)


BF16 = ml_dtypes.bfloat16


def bf(x):
    return np.asarray(x, np.float32).astype(BF16)


def f64(x):
    return np.asarray(x).astype(np.float64)


E2M1 = np.array([0.0, 0.5, 1.0, 1.5, 2.0, 3.0, 4.0, 6.0, -0.0, -0.5, -1.0, -1.5, -2.0, -3.0, -4.0, -6.0])


def pack_weight(w, fmt):
    k, n = w.shape
    w = f64(bf(w)).reshape(k // 32, 32, n)
    amax = np.abs(w).max(1)
    if fmt == "e4m3":
        byte = np.frexp(amax)[1] - 1 + 127 - 7
    else:
        mant, ex = np.frexp(amax / 6.0)
        byte = np.where(mant > 0.5, ex, ex - 1) + 127
    byte = np.clip(np.where(amax > 0, byte, 1), 1, 254)
    scaled = (w * np.exp2(127.0 - byte)[:, None, :]).reshape(k, n).astype(np.float32)
    by_word = np.ascontiguousarray(scaled.reshape(k // 512, 128, 4, n).transpose(0, 1, 3, 2))
    if fmt == "e4m3":
        words = by_word.astype(ml_dtypes.float8_e4m3fn).view(np.uint8)
    else:
        c = by_word.astype(ml_dtypes.float4_e2m1fn).view(np.uint8) & 0xF
        words = c[..., 0::2] | (c[..., 1::2] << 4)
    return np.ascontiguousarray(words), np.ascontiguousarray(byte.astype(np.uint8).reshape(k // 512, 16, n))


def unpack_weight(words, scales, fmt):
    g, p, n, _ = words.shape
    if fmt == "e4m3":
        vals = np.ascontiguousarray(words).view(ml_dtypes.float8_e4m3fn).astype(np.float64)
    else:
        nib = np.empty((g, p, n, 4), np.uint8)
        nib[..., 0::2] = words & 0xF
        nib[..., 1::2] = words >> 4
        vals = E2M1[nib]
    vals = vals * np.repeat(np.exp2(scales.astype(np.float64) - 127.0), 8, axis=1)[..., None]
    return vals.transpose(0, 1, 3, 2).reshape(g * 512, n)
def pack4(w):
    words, scales = pack_weight(w, "e2m1")
    return words.reshape(words.shape[0], 128, -1), scales


def unpack4(words, scales):
    return unpack_weight(words.reshape(words.shape[0], 128, -1, 2), scales, "e2m1")


M, N, K, C, F = 1024, 512, 1536, 2048, 1024


def draw0():
    s = mx_kscale(K)
    r = mx_kscale(C)
    u = mx_kscale(C)
    t = mx_kscale(F)
    v = np.random.standard_normal((C, F)) / np.sqrt(C) / r[:, None] * t
    v_words, v_scales = pack4(v)
    return {"act_train": bf(np.random.standard_normal((M, K)) * K ** -0.25 * s),
            "act_query": bf(np.random.standard_normal((N, K)) * K ** -0.25 / s),
            "err_train": bf(np.random.standard_normal((M, C)) * 2.0 * F ** -0.25 * r),
            "err_query": bf(np.random.standard_normal((N, C)) * 2.0 * F ** -0.25 * u),
            "slope_train": bf(1.0 / (1.0 + np.exp(-np.random.standard_normal((M, F))))),
            "slope_query": bf(1.0 / (1.0 + np.exp(-np.random.standard_normal((N, F))))),
            "v_words": v_words,
            "v_scales": v_scales,
            "w": bf(np.random.standard_normal((C, F)) / np.sqrt(C) / u[:, None] / t)}


def core(act_train, act_query, err_train, err_query, slope_train, slope_query, v_words, v_scales, w):
    back_train = mxq(f64(err_train), 1, "e4m3") @ unpack4(v_words, v_scales)
    back_query = mxq(f64(err_query), 1, "e4m3") @ mxq(f64(w), 0, "e4m3")
    d_train = back_train * f64(slope_train)
    d_query = back_query * f64(slope_query)
    gram_err = mxq(d_train, 1, "e4m3") @ mxq(d_query, 1, "e4m3").T
    gram_act = mxq(f64(act_train), 1, "e4m3") @ mxq(f64(act_query), 1, "e4m3").T
    return gram_act * gram_err


def e4m3fn_bytes(y):
    return np.clip(np.asarray(y, np.float64), -448.0, 448.0).astype(np.float32).astype(ml_dtypes.float8_e4m3fn).view(np.uint8)


def e4m3fn_values(b):
    return np.asarray(b, np.uint8).view(ml_dtypes.float8_e4m3fn).astype(np.float64)


def setup_inputs():
    d = draw0()
    x0 = np.asarray(d['err_train']).astype(np.float64)
    s = (np.max(np.abs(x0), axis=(0,), keepdims=True) / 448.0).astype(np.float32)
    out = {}
    for k, v in d.items():
        if k == 'err_train':
            out['err_train_bytes'] = e4m3fn_bytes(x0 / s.astype(np.float64))
            out['err_train_scale'] = s
        else:
            out[k] = v
    return out


def reference(act_train, act_query, err_train_bytes, err_train_scale, err_query, slope_train, slope_query, v_words, v_scales, w):
    return core(act_train, act_query, e4m3fn_values(err_train_bytes) * err_train_scale.astype(np.float64), err_query, slope_train, slope_query, v_words, v_scales, w)

@@ -1,0 +1,349 @@
+from contextlib import ExitStack
+
+import concourse.mybir as mybir
+from concourse.masks import make_identity
+
+M, N, K, C, F = 1024, 512, 1536, 2048, 1024
+P = 128
+FLOPS = 2 * (M * F * C + N * F * C + M * N * F + M * N * K)
+
+F32 = mybir.dt.float32
+BF16 = mybir.dt.bfloat16
+I32 = mybir.dt.int32
+U32 = mybir.dt.uint32
+U8 = mybir.dt.uint8
+FP8 = mybir.dt.float8_e4m3fn
+FP8X4 = mybir.dt.float8_e4m3fn_x4
+FP4X4 = mybir.dt.float4_e2m1fn_x4
+MULT = mybir.AluOpType.mult
+
+
+def tile_gradient_inner_products_s11_kernel(
+    tc, act_train, act_query, err_train_bytes, err_train_scale, err_query, slope_train, slope_query, v_words, v_scales, w, out
+):
+    nc = tc.nc
+    with ExitStack() as ctx:
+        keep = ctx.enter_context(tc.tile_pool(name="keep", bufs=1))
+        work = ctx.enter_context(tc.tile_pool(name="work", bufs=2))
+        psum = ctx.enter_context(tc.psum_pool(name="psum", bufs=4))
+        t = {}
+
+        def small(name, shape, dtype):
+            return keep.tile(shape, dtype, name=name, align_bytes=64)
+
+        ident = keep.tile([P, P], F32, name="ident", align_bytes=64)
+        make_identity(nc, ident[:])
+        v_planes = small("v_planes", [P, 4, F], U8)
+        nc.vector.memset(v_planes[:].rearrange("p g n -> p (g n)").bitcast(I32), 0)
+        v_codes = small("v_codes", [P, 4, 2 * F], U8)
+        scale = small("scale", [P, C], F32)
+        w_codes = small("w_codes", [P, 4, F], U32)
+        w_planes = small("w_planes", [P, 4, F], U8)
+        aq_codes = small("aq_codes", [P, 3, N], U32)
+        aq_planes = small("aq_planes", [P, 3, N], U8)
+        dq_codes = small("dq_codes", [P, 2, N], U32)
+        dq_planes = small("dq_planes", [P, 2, N], U8)
+        dt_codes = small("dt_codes", [P, 8, 2, P], U32)
+        dt_planes = small("dt_planes", [P, 8, 2, P], U8)
+        gram_act = small("gram_act", [P, 8, N], F32)
+
+        def load_act(src, name, i):
+            raw = work.tile([P, 2, K], BF16, tag="act_raw", name="act_raw", bufs=4, align_bytes=64)
+            view = src[256 * i : 256 * (i + 1), :].rearrange("(j p) k -> p j k", p=P)
+            if name == "aq" or i == 0:
+                for g in range(3):
+                    nc.sync.dma_start(out=raw[:, :, 512 * g : 512 * (g + 1)], in_=view[:, :, 512 * g : 512 * (g + 1)])
+            else:
+                nc.sync.dma_start(out=raw[:], in_=view)
+            t[name, i] = raw
+
+        def spread_scale():
+            rows = small("scale_rows", [P, 2, 32], F32)
+            cols = small("scale_cols", [P, 2, 32], F32)
+            for q in range(4):
+                nc.scalar.dma_start(out=rows[32 * q : 32 * q + 32], in_=err_train_scale.rearrange("o (h b j) -> (o b) h j", h=2, b=32))
+            for h in range(2):
+                nc.vector.transpose(out=cols[:, h, :], in_=rows[:, h, :])
+            flat = cols[:].rearrange("p h b -> p (h b)")
+            for c in range(4):
+                x = work.tile([P, 16, 32], F32, tag="wx", name="spread", bufs=4, align_bytes=64)
+                nc.scalar.copy(out=x[:], in_=flat[:, 16 * c : 16 * c + 16].unsqueeze(2).to_broadcast([P, 16, 32]))
+                nc.vector.transpose(out=scale[:, 512 * c : 512 * (c + 1)], in_=x[:].rearrange("p b i -> p (b i)"))
+
+        def load_bytes(i):
+            b = small("bytes%d" % i, [P, 2, C], U8)
+            nc.sync.dma_start(out=b[:], in_=err_train_bytes[256 * i : 256 * (i + 1), :].rearrange("(j p) k -> p j k", p=P))
+            t["bytes", i] = b
+
+        def load_v():
+            for q in range(4):
+                nc.sync.dma_start(
+                    out=v_planes[32 * q : 32 * q + 4, :, :].bitcast(I32),
+                    in_=v_scales[:, 4 * q : 4 * q + 4, :].rearrange("g r n -> r g n").bitcast(I32),
+                )
+            nc.sync.dma_start(out=v_codes[:], in_=v_words.rearrange("g p b -> p g b"))
+
+        def load_w(g):
+            raw = work.tile([P, 4, F], BF16, tag="w_raw", name="w_raw", bufs=3, align_bytes=64)
+            nc.sync.dma_start(out=raw[:], in_=w[512 * g : 512 * (g + 1), :].rearrange("(p t) n -> p t n", t=4))
+            t["w", g] = raw
+
+        def load_err_query(i):
+            raw = small("errq%d" % i, [P, 2, C], BF16)
+            nc.sync.dma_start(out=raw[:], in_=err_query[256 * i : 256 * (i + 1), :].rearrange("(j p) k -> p j k", p=P))
+            t["errq", i] = raw
+
+        def load_slope(name, i):
+            src = slope_train if name == "e" else slope_query
+            s = work.tile([P, 2, F], BF16, tag="slope", name="slope", bufs=4, align_bytes=64)
+            nc.sync.dma_start(out=s[:], in_=src[256 * i : 256 * (i + 1), :].rearrange("(j p) k -> p j k", p=P))
+            t["slope", name, 2 * i] = s[:, 0, :]
+            t["slope", name, 2 * i + 1] = s[:, 1, :]
+
+        def turn(key, parts):
+            bank = psum.tile([P, 4, P], F32, tag="turn", name="turn", bufs=4)
+            for j, words in enumerate(parts):
+                nc.tensor.transpose(bank[:, j, :], words, ident[:])
+            t["bank", key] = bank
+
+        def evac(key):
+            x = work.tile([P, 2, P, 4], BF16, tag="kx", name="kx", bufs=5, align_bytes=64)
+            nc.scalar.copy(out=x[:].bitcast(F32), in_=t["bank", key][:].rearrange("p (g u) r -> p g r u", g=2))
+            t["kx", key] = x
+
+        def quant(key, codes, planes):
+            nc.vector.quantize_mx(out=codes.bitcast(FP8X4), scales=planes, in_=t["kx", key][:].rearrange("p g r t -> p (g r t)"))
+
+        def second(words, g):
+            return [words[:, 256 * g + u : 256 * (g + 1) : 2] for u in range(2)]
+
+        def sorted_words(key):
+            x = t["sorted", key]
+            return [x[:, j, u, :] for j in range(2) for u in range(2)]
+
+        def sort_words(key, src):
+            x = work.tile([P, 2, 2, P], F32, tag="sorted", name="sorted", bufs=3, align_bytes=64)
+            nc.scalar.copy(out=x[:], in_=src)
+            t["sorted", key] = x
+
+        def sort_act(name, i, g):
+            sort_words((name, i, g), t[name, i][:, :, 512 * g : 512 * (g + 1)].bitcast(F32).rearrange("p j (m u) -> p j u m", u=2))
+
+        def sort_err(i, b):
+            sort_words(("r", i, b), t["errq", i // 2][:, i % 2, 1024 * b : 1024 * (b + 1)].bitcast(F32).rearrange("p (g m u) -> p g u m", g=2, u=2))
+
+        def turn_act(name, i, g):
+            raw = t[name, i]
+            if ("sorted", (name, i, g)) in t:
+                turn((name, i, g), sorted_words((name, i, g)))
+            else:
+                turn((name, i, g), second(raw[:, 0, :].bitcast(F32), g) + second(raw[:, 1, :].bitcast(F32), g))
+
+        def evac_act(name, i, g):
+            evac((name, i, g))
+
+        def quant_act(name, i, g):
+            if name == "aq":
+                quant((name, i, g), aq_codes[:, g, 256 * i : 256 * (i + 1)], aq_planes[:, g, 256 * i : 256 * (i + 1)])
+            else:
+                if g == 0:
+                    t["at_codes", i] = work.tile([P, 3, 2 * P], U32, tag="at_codes", name="at_codes", align_bytes=64)
+                    t["at_planes", i] = work.tile([P, 3, 2 * P], U8, tag="at_planes", name="at_planes", align_bytes=64)
+                quant((name, i, g), t["at_codes", i][:, g, :], t["at_planes", i][:, g, :])
+
+        def mm_act(i):
+            acc = psum.tile([P, N], F32, tag="acc", name="acc", bufs=4)
+            half = slice(P * (i % 2), P * (i % 2) + P)
+            for g in range(3):
+                nc.tensor.matmul_mx(
+                    out=acc[:], lhsT=t["at_codes", i // 2][:, g, half].bitcast(FP8X4), lhsT_scale=t["at_planes", i // 2][:, g, half],
+                    rhs=aq_codes[:, g, :].bitcast(FP8X4), rhs_scale=aq_planes[:, g, :], start=g == 0, stop=g == 2,
+                )
+            t["gram", i] = acc
+
+        def keep_gram(i):
+            nc.scalar.copy(out=gram_act[:, i, :], in_=t["gram", i][:])
+
+        def scale_err(i, h):
+            if h == 0:
+                t["err", "e", i] = work.tile([P, C], BF16, tag="err", name="err", bufs=3, align_bytes=64)
+            k = slice(1024 * h, 1024 * (h + 1))
+            nc.vector.tensor_tensor(out=t["err", "e", i][:, k], in0=t["bytes", i // 2][:, i % 2, k].bitcast(FP8), in1=scale[:, k], op=MULT)
+
+        def turn_err(name, i, b):
+            words = t["err", "e", i][:].bitcast(F32) if name == "e" else t["errq", i // 2][:, i % 2, :].bitcast(F32)
+            if ("sorted", (name, i, b)) in t:
+                turn((name, i, b), sorted_words((name, i, b)))
+            else:
+                turn((name, i, b), second(words, 2 * b) + second(words, 2 * b + 1))
+
+        def evac_err(name, i, b):
+            evac((name, i, b))
+
+        def quant_err(name, i, b):
+            if b == 0:
+                t["codes", name, i] = work.tile([P, 4, P], U32, tag="e_codes", name="e_codes", bufs=3, align_bytes=64)
+                t["planes", name, i] = work.tile([P, 4, P], U8, tag="e_planes", name="e_planes", bufs=3, align_bytes=64)
+            quant((name, i, b), t["codes", name, i][:, 2 * b : 2 * b + 2, :].rearrange("p g r -> p (g r)"), t["planes", name, i][:, 2 * b : 2 * b + 2, :].rearrange("p g r -> p (g r)"))
+
+        def mm_err(name, i, h):
+            acc = psum.tile([P, N], F32, tag="acc", name="acc", bufs=4)
+            for g in range(4):
+                if name == "e":
+                    rhs, rhs_scale = v_codes[:, g, 1024 * h : 1024 * (h + 1)].bitcast(FP4X4), v_planes[:, g, 512 * h : 512 * (h + 1)]
+                else:
+                    rhs, rhs_scale = w_codes[:, g, 512 * h : 512 * (h + 1)].bitcast(FP8X4), w_planes[:, g, 512 * h : 512 * (h + 1)]
+                nc.tensor.matmul_mx(
+                    out=acc[:], lhsT=t["codes", name, i][:, g, :].bitcast(FP8X4), lhsT_scale=t["planes", name, i][:, g, :],
+                    rhs=rhs, rhs_scale=rhs_scale, start=g == 0, stop=g == 3,
+                )
+            t["back", name, i, h] = acc
+
+        def slope_mul(name, i, h):
+            if h == 0:
+                t["d", name, i] = work.tile([P, 2, 2, P, 2], BF16, tag="d", name="d", bufs=3, align_bytes=64)
+            nc.vector.tensor_tensor(
+                out=t["d", name, i][:, h],
+                in0=t["back", name, i, h][:].rearrange("p (m u e) -> p u m e", u=2, e=2),
+                in1=t["slope", name, i][:, 512 * h : 512 * (h + 1)].rearrange("p (m u e) -> p u m e", u=2, e=2),
+                op=MULT,
+            )
+
+        def turn_d(name, i):
+            words = t["d", name, i][:].rearrange("p h u m e -> p (h u m e)").bitcast(F32)
+            turn(("d", name, i), [words[:, P * j : P * (j + 1)] for j in range(4)])
+
+        def evac_d(name, i):
+            evac(("d", name, i))
+
+        def quant_d(name, i):
+            if name == "e":
+                quant(("d", name, i), dt_codes[:, i].rearrange("p g r -> p (g r)"), dt_planes[:, i].rearrange("p g r -> p (g r)"))
+            else:
+                x = t["kx", ("d", name, i)]
+                for g in range(2):
+                    nc.vector.quantize_mx(
+                        out=dq_codes[:, g, P * i : P * (i + 1)].bitcast(FP8X4), scales=dq_planes[:, g, P * i : P * (i + 1)],
+                        in_=x[:, g].rearrange("p r t -> p (r t)"),
+                    )
+
+        def w_lay(c, engine):
+            g, n0 = c // 4, 256 * (c % 4)
+            x = work.tile([P, 256, 4], BF16, tag="wx", name="wx", bufs=4, align_bytes=64)
+            dst = x[:].rearrange("p (c i) t -> p c t i", i=4)
+            src = t["w", g][:, :, n0 : n0 + 256].rearrange("p t (c i) -> p c t i", i=4)
+            if engine == "act":
+                nc.scalar.copy(out=dst, in_=src)
+            else:
+                nc.vector.tensor_copy(out=dst, in_=src)
+            t["wx", c] = x
+
+        def w_quant(c):
+            g, n0 = c // 4, 256 * (c % 4)
+            nc.vector.quantize_mx(
+                out=w_codes[:, g, n0 : n0 + 256].bitcast(FP8X4), scales=w_planes[:, g, n0 : n0 + 256],
+                in_=t["wx", c][:].rearrange("p n t -> p (n t)"),
+            )
+
+        def mm_gram(i):
+            acc = psum.tile([P, N], F32, tag="acc", name="acc", bufs=4)
+            for g in range(2):
+                nc.tensor.matmul_mx(
+                    out=acc[:], lhsT=dt_codes[:, i, g, :].bitcast(FP8X4), lhsT_scale=dt_planes[:, i, g, :],
+                    rhs=dq_codes[:, g, :].bitcast(FP8X4), rhs_scale=dq_planes[:, g, :], start=g == 0, stop=g == 1,
+                )
+            t["ge", i] = acc
+
+        def finish(i):
+            res = work.tile([P, N], F32, tag="wx", name="res", bufs=4, align_bytes=64)
+            nc.vector.tensor_tensor(out=res[:], in0=t["ge", i][:], in1=gram_act[:, i, :], op=MULT)
+            nc.sync.dma_start(out=out[P * i : P * (i + 1), :], in_=res[:])
+
+        for fn, a in [
+            (load_act, (act_query, "aq", 0)),
+            (load_bytes, (0,)),
+            (load_act, (act_query, "aq", 1)),
+            (load_act, (act_train, "at", 0)),
+            (load_act, (act_train, "at", 1)),
+            (load_act, (act_train, "at", 2)),
+            (load_w, (0,)),
+            (load_bytes, (1,)),
+            (load_bytes, (2,)),
+            (load_v, ()),
+            (load_w, (1,)),
+            (load_slope, ("e", 0)),
+            (load_err_query, (0,)),
+            (load_slope, ("r", 0)),
+            (load_act, (act_train, "at", 3)),
+            (load_w, (2,)),
+            (load_slope, ("e", 1)),
+            (load_slope, ("r", 1)),
+            (load_err_query, (1,)),
+            (load_slope, ("e", 2)),
+            (load_bytes, (3,)),
+            (load_w, (3,)),
+            (load_slope, ("e", 3)),
+        ]:
+            fn(*a)
+
+        waiting = []
+        count = {"lay": 0, "quant": 0}
+
+        def settle(q, n):
+            while len(q) > n:
+                fn, a = q[0]
+                q.remove(q[0])
+                fn(*a)
+
+        ORDER = """
+            q00 q01 q02 s0a q10 q11 q12 a00 a01 s0b a02 s1a e00 a10 a11 a12 pa s1b s2a a20 e01 wl a21 e10
+            s2b A0 A1 a22 wv wq s3a s3b wl e11 e20 A2 wl A3 B00 wq B01 e21 wl s4a e30 e31 wq wq
+            s4b wl A4 B10 B11 B20 wq wl pr s5a d0 wq s5b e40 e41 B21 wq wv wl wl pr B30 wq B31
+            wq wv wq e50 r00 e51 d1 wq B40 wl wq pr B41 wv r01 wq r10 wl wq wv r11 pr wq d2
+            wl wq A5 B50 B51 r20 r21 d3 pa s6a s6b d4 R00 R01 R10 pr pr R11 r30 r31 e60 pa s7a e61
+            a30 pa R20 R21 a31 d5 s7b a32 x0 R30 R31 B60 x1 e70 x2 e71 x3 A6 B61 B70 G0 B71 G1 G2
+            G3 d6 d7 G4 G5 A7 G6 G7
+        """
+        using = []
+        TURNS = {
+            "q": (turn_act, evac_act, quant_act, ("aq",)), "a": (turn_act, evac_act, quant_act, ("at",)),
+            "e": (turn_err, evac_err, quant_err, ("e",)), "r": (turn_err, evac_err, quant_err, ("r",)),
+            "d": (turn_d, evac_d, quant_d, ("e",)), "x": (turn_d, evac_d, quant_d, ("r",)),
+        }
+        PRODUCTS = {"A": (mm_act, keep_gram, ()), "B": (mm_err, slope_mul, ("e",)), "R": (mm_err, slope_mul, ("r",)), "G": (mm_gram, finish, ())}
+        PREPS = {"q": list(range(6, 6)), "a": list(range(8, 12)), "r": list(range(2, 8))}
+        with tc.manual_schedule():
+            spread_scale()
+            for item in ORDER.split():
+                kind = item[0]
+                if kind == "p":
+                    i = PREPS[item[1]][0]
+                    PREPS[item[1]].remove(i)
+                    if item[1] == "r":
+                        sort_err(i // 2, i % 2)
+                    else:
+                        sort_act("aq" if item[1] == "q" else "at", i // 3, i % 3)
+                elif item in ("wl", "wv"):
+                    w_lay(count["lay"], "act" if item == "wl" else "dve")
+                    count["lay"] += 1
+                elif item == "wq":
+                    w_quant(count["quant"])
+                    count["quant"] += 1
+                elif kind == "s":
+                    scale_err(int(item[1]), "ab".index(item[2]))
+                elif kind in TURNS:
+                    settle(using, 0)
+                    turn_fn, evac_fn, quant_fn, first = TURNS[kind]
+                    a = first + tuple([int(z) for z in item[1:]])
+                    turn_fn(*a)
+                    evac_fn(*a)
+                    waiting.append((quant_fn, a))
+                    settle(waiting, 1)
+                else:
+                    settle(using, 0)
+                    settle(waiting, 0)
+                    mm, use, first = PRODUCTS[kind]
+                    a = first + tuple([int(z) for z in item[1:]])
+                    mm(*a)
+                    using.append((use, a))
+            settle(using, 0)

@@ -16,6 +16,7 @@ FP8 = mybir.dt.float8_e4m3fn
 FP8X4 = mybir.dt.float8_e4m3fn_x4
 FP4X4 = mybir.dt.float4_e2m1fn_x4
 MULT = mybir.AluOpType.mult
+WXB = 5
 
 
 def tile_gradient_inner_products_s11_kernel(
@@ -28,322 +29,315 @@ def tile_gradient_inner_products_s11_kernel(
         psum = ctx.enter_context(tc.psum_pool(name="psum", bufs=4))
         t = {}
 
-        def small(name, shape, dtype):
+        def kept(name, shape, dtype):
             return keep.tile(shape, dtype, name=name, align_bytes=64)
 
-        ident = keep.tile([P, P], F32, name="ident", align_bytes=64)
-        make_identity(nc, ident[:])
-        v_planes = small("v_planes", [P, 4, F], U8)
-        nc.vector.memset(v_planes[:].rearrange("p g n -> p (g n)").bitcast(I32), 0)
-        v_codes = small("v_codes", [P, 4, 2 * F], U8)
-        scale = small("scale", [P, C], F32)
-        w_codes = small("w_codes", [P, 4, F], U32)
-        w_planes = small("w_planes", [P, 4, F], U8)
-        aq_codes = small("aq_codes", [P, 3, N], U32)
-        aq_planes = small("aq_planes", [P, 3, N], U8)
-        dq_codes = small("dq_codes", [P, 2, N], U32)
-        dq_planes = small("dq_planes", [P, 2, N], U8)
-        dt_codes = small("dt_codes", [P, 8, 2, P], U32)
-        dt_planes = small("dt_planes", [P, 8, 2, P], U8)
-        gram_act = small("gram_act", [P, 8, N], F32)
+        def ring(name, shape, dtype, bufs):
+            return work.tile(shape, dtype, tag=name, name=name, bufs=bufs, align_bytes=64)
 
-        def load_act(src, name, i):
-            raw = work.tile([P, 2, K], BF16, tag="act_raw", name="act_raw", bufs=4, align_bytes=64)
-            view = src[256 * i : 256 * (i + 1), :].rearrange("(j p) k -> p j k", p=P)
-            if name == "aq" or i == 0:
-                for g in range(3):
-                    nc.sync.dma_start(out=raw[:, :, 512 * g : 512 * (g + 1)], in_=view[:, :, 512 * g : 512 * (g + 1)])
-            else:
-                nc.sync.dma_start(out=raw[:], in_=view)
-            t[name, i] = raw
+        ident = kept("ident", [P, P], F32)
+        v_planes = kept("v_planes", [P, 4, F], U8)
+        v_codes = [kept("v_codes%d" % h, [P, 4, F], U8) for h in range(2)]
+        scale = kept("scale", [P, 4, 4], F32)
+        w_codes = kept("w_codes", [P, 2, 4, N], U32)
+        w_planes = kept("w_planes", [P, 2, 4, N], U8)
+        aq_codes = kept("aq_codes", [P, 3, N], U32)
+        aq_planes = kept("aq_planes", [P, 3, N], U8)
+        rq_codes = kept("rq_codes", [P, 4, 4, P], U32)
+        rq_planes = kept("rq_planes", [P, 4, 4, P], U8)
+        dq_codes = kept("dq_codes", [P, 2, N], U32)
+        dq_planes = kept("dq_planes", [P, 2, N], U8)
+        dt_codes = kept("dt_codes", [P, 8, 2, P], U32)
+        dt_planes = kept("dt_planes", [P, 8, 2, P], U8)
+        gram_act = kept("gram_act", [P, 8, N], F32)
 
-        def spread_scale():
-            rows = small("scale_rows", [P, 2, 32], F32)
-            cols = small("scale_cols", [P, 2, 32], F32)
-            for q in range(4):
-                nc.scalar.dma_start(out=rows[32 * q : 32 * q + 32], in_=err_train_scale.rearrange("o (h b j) -> (o b) h j", h=2, b=32))
-            for h in range(2):
-                nc.vector.transpose(out=cols[:, h, :], in_=rows[:, h, :])
-            flat = cols[:].rearrange("p h b -> p (h b)")
-            for c in range(4):
-                x = work.tile([P, 16, 32], F32, tag="wx", name="spread", bufs=4, align_bytes=64)
-                nc.scalar.copy(out=x[:], in_=flat[:, 16 * c : 16 * c + 16].unsqueeze(2).to_broadcast([P, 16, 32]))
-                nc.vector.transpose(out=scale[:, 512 * c : 512 * (c + 1)], in_=x[:].rearrange("p b i -> p (b i)"))
+        def train_rows(src, pair):
+            return src[256 * pair : 256 * (pair + 1), :].rearrange("(p j) k -> p j k", j=2)
 
-        def load_bytes(i):
-            b = small("bytes%d" % i, [P, 2, C], U8)
-            nc.sync.dma_start(out=b[:], in_=err_train_bytes[256 * i : 256 * (i + 1), :].rearrange("(j p) k -> p j k", p=P))
-            t["bytes", i] = b
+        def query_rows(src, pair):
+            return src[256 * pair : 256 * (pair + 1), :].rearrange("(j p) k -> p j k", j=2)
 
-        def load_v():
+        RING = {"bytes_pair": (2, 4), "act_raw": (3, 3), "w_raw": (3, 2), "slope_t": (3, 4)}
+        unread = {name: 0 for name in RING}
+        waiting = []
+
+        def streamed(name, shape, dtype):
+            unread[name] += RING[name][1]
+            return ring(name, shape, dtype, RING[name][0])
+
+        def was_read(name):
+            unread[name] -= 1
+
+        def issue_loads():
+            while waiting:
+                name, fn, a = waiting[0]
+                if name in RING and unread[name] > (RING[name][0] - 1) * RING[name][1]:
+                    return
+                waiting.remove(waiting[0])
+                fn(*a)
+
+        def load_first_bytes(j):
+            b = kept("bytes0_%d" % j, [P, C], U8)
+            nc.sync.dma_start(out=b[:], in_=train_rows(err_train_bytes, 0)[:, j, :])
+            t["bytes", j] = b[:]
+
+        def load_bytes(pair):
+            b = streamed("bytes_pair", [P, 2, C], U8)
+            nc.sync.dma_start(out=b[:], in_=train_rows(err_train_bytes, pair))
+            for j in range(2):
+                t["bytes", 2 * pair + j] = b[:, j, :]
+
+        def load_scale():
+            nc.sync.dma_start(out=scale[:], in_=err_train_scale.rearrange("o (g p t) -> p (o g) t", p=P, t=4))
+
+        def load_v_scales():
             for q in range(4):
                 nc.sync.dma_start(
                     out=v_planes[32 * q : 32 * q + 4, :, :].bitcast(I32),
                     in_=v_scales[:, 4 * q : 4 * q + 4, :].rearrange("g r n -> r g n").bitcast(I32),
                 )
-            nc.sync.dma_start(out=v_codes[:], in_=v_words.rearrange("g p b -> p g b"))
 
-        def load_w(g):
-            raw = work.tile([P, 4, F], BF16, tag="w_raw", name="w_raw", bufs=3, align_bytes=64)
-            nc.sync.dma_start(out=raw[:], in_=w[512 * g : 512 * (g + 1), :].rearrange("(p t) n -> p t n", t=4))
-            t["w", g] = raw
+        def load_v(h):
+            nc.sync.dma_start(out=v_codes[h][:], in_=v_words[:, :, F * h : F * (h + 1)].rearrange("g p b -> p g b"))
 
-        def load_err_query(i):
-            raw = small("errq%d" % i, [P, 2, C], BF16)
-            nc.sync.dma_start(out=raw[:], in_=err_query[256 * i : 256 * (i + 1), :].rearrange("(j p) k -> p j k", p=P))
-            t["errq", i] = raw
+        def load_act(side, pair):
+            raw = streamed("act_raw", [P, 2, K], BF16)
+            nc.sync.dma_start(out=raw[:], in_=query_rows(act_query, pair) if side == "q" else train_rows(act_train, pair))
+            for g in range(3):
+                t["act", side, pair, g] = raw[:, :, 512 * g : 512 * (g + 1)]
 
-        def load_slope(name, i):
-            src = slope_train if name == "e" else slope_query
-            s = work.tile([P, 2, F], BF16, tag="slope", name="slope", bufs=4, align_bytes=64)
-            nc.sync.dma_start(out=s[:], in_=src[256 * i : 256 * (i + 1), :].rearrange("(j p) k -> p j k", p=P))
-            t["slope", name, 2 * i] = s[:, 0, :]
-            t["slope", name, 2 * i + 1] = s[:, 1, :]
+        def load_first_act(g):
+            raw = kept("act_first%d" % g, [P, 2, 512], BF16)
+            nc.sync.dma_start(out=raw[:], in_=query_rows(act_query, 0)[:, :, 512 * g : 512 * (g + 1)])
+            t["act", "q", 0, g] = raw[:]
 
-        def turn(key, parts):
-            bank = psum.tile([P, 4, P], F32, tag="turn", name="turn", bufs=4)
-            for j, words in enumerate(parts):
-                nc.tensor.transpose(bank[:, j, :], words, ident[:])
+        def load_w(h, g):
+            raw = streamed("w_raw", [P, 4, N], BF16)
+            nc.sync.dma_start(out=raw[:], in_=w[512 * g : 512 * (g + 1), N * h : N * (h + 1)].rearrange("(p t) n -> p t n", t=4))
+            t["w", h, g] = raw
+
+        def load_err_query(pair):
+            raw = kept("errq%d" % pair, [P, 2, C], BF16)
+            nc.sync.dma_start(out=raw[:], in_=query_rows(err_query, pair))
+            for j in range(2):
+                for b in range(2):
+                    t["err", "q", 2 * pair + j, b] = raw[:, j, 1024 * b : 1024 * (b + 1)]
+
+        def load_slope(side, pair):
+            if side == "t":
+                s = streamed("slope_t", [P, 2, F], BF16)
+                nc.sync.dma_start(out=s[:], in_=train_rows(slope_train, pair))
+            else:
+                s = kept("slope_q%d" % pair, [P, 2, F], BF16)
+                nc.sync.dma_start(out=s[:], in_=query_rows(slope_query, pair))
+            for j in range(2):
+                t["slope", side, 2 * pair + j] = s[:, j, :]
+
+        def widen(i, b):
+            x = ring("wide", [P, 1024], BF16, 4)
+            nc.scalar.copy(out=x[:], in_=t["bytes", i][:, 1024 * b : 1024 * (b + 1)].bitcast(FP8))
+            t["err", "t", i, b] = x[:]
+            if i >= 2:
+                was_read("bytes_pair")
+
+        def words_of(key):
+            if key[0] == "act":
+                return t[key].bitcast(F32)
+            return t[key].bitcast(F32).rearrange("p (a m) -> p a m", a=2)
+
+        def words_read(key):
+            if key[0] == "act" and key[1:3] != ("q", 0):
+                was_read("act_raw")
+
+        def copy_on(engine, out, in_):
+            if engine == "s":
+                nc.scalar.copy(out=out, in_=in_)
+            else:
+                nc.vector.tensor_copy(out=out, in_=in_)
+
+        def sort_words(key, engine):
+            x = ring("sorted", [P, 2, 2, P], F32, 6)
+            copy_on(engine, out=x[:], in_=words_of(key).rearrange("p a (m u) -> p a u m", u=2))
+            t["sorted", key] = x
+            words_read(key)
+
+        def turn(key):
+            bank = psum.tile([P, 2, 2 * P], F32, tag="bank", name="turn", bufs=8)
+            for a in range(2):
+                for u in range(2):
+                    if key[0] == "d":
+                        src = t["d", "t", key[2], a][:, u, :] if key[1] == "t" else t["d", "q", 2 * key[2] + a, key[3]][:, u, :]
+                    elif ("sorted", key) in t:
+                        src = t["sorted", key][:, a, u, :]
+                    else:
+                        src = words_of(key)[:, a, u : 256 : 2]
+                    nc.tensor.transpose(bank[:, u, P * a : P * (a + 1)], src, ident[:])
             t["bank", key] = bank
+            if ("sorted", key) not in t:
+                words_read(key)
 
-        def evac(key):
-            x = work.tile([P, 2, P, 4], BF16, tag="kx", name="kx", bufs=5, align_bytes=64)
-            nc.scalar.copy(out=x[:].bitcast(F32), in_=t["bank", key][:].rearrange("p (g u) r -> p g r u", g=2))
+        def empty(key):
+            x = ring("kx", [P, 2 * P, 4], BF16, 8)
+            if key[:2] == ("err", "t"):
+                g = 2 * key[3]
+                nc.vector.tensor_tensor(
+                    out=x[:].rearrange("p (a m) (u e) -> p a m u e", a=2, u=2),
+                    in0=t["bank", key][:].bitcast(BF16).rearrange("p u (a m e) -> p a m u e", a=2, e=2),
+                    in1=scale[:, g : g + 2, :].rearrange("p a (u e) -> p a u e", u=2).unsqueeze(2).to_broadcast([P, 2, P, 2, 2]),
+                    op=MULT,
+                )
+            else:
+                nc.scalar.copy(out=x[:].bitcast(F32), in_=t["bank", key][:].rearrange("p u r -> p r u"))
             t["kx", key] = x
 
-        def quant(key, codes, planes):
-            nc.vector.quantize_mx(out=codes.bitcast(FP8X4), scales=planes, in_=t["kx", key][:].rearrange("p g r t -> p (g r t)"))
-
-        def second(words, g):
-            return [words[:, 256 * g + u : 256 * (g + 1) : 2] for u in range(2)]
-
-        def sorted_words(key):
-            x = t["sorted", key]
-            return [x[:, j, u, :] for j in range(2) for u in range(2)]
-
-        def sort_words(key, src):
-            x = work.tile([P, 2, 2, P], F32, tag="sorted", name="sorted", bufs=3, align_bytes=64)
-            nc.scalar.copy(out=x[:], in_=src)
-            t["sorted", key] = x
-
-        def sort_act(name, i, g):
-            sort_words((name, i, g), t[name, i][:, :, 512 * g : 512 * (g + 1)].bitcast(F32).rearrange("p j (m u) -> p j u m", u=2))
-
-        def sort_err(i, b):
-            sort_words(("r", i, b), t["errq", i // 2][:, i % 2, 1024 * b : 1024 * (b + 1)].bitcast(F32).rearrange("p (g m u) -> p g u m", g=2, u=2))
-
-        def turn_act(name, i, g):
-            raw = t[name, i]
-            if ("sorted", (name, i, g)) in t:
-                turn((name, i, g), sorted_words((name, i, g)))
-            else:
-                turn((name, i, g), second(raw[:, 0, :].bitcast(F32), g) + second(raw[:, 1, :].bitcast(F32), g))
-
-        def evac_act(name, i, g):
-            evac((name, i, g))
-
-        def quant_act(name, i, g):
-            if name == "aq":
-                quant((name, i, g), aq_codes[:, g, 256 * i : 256 * (i + 1)], aq_planes[:, g, 256 * i : 256 * (i + 1)])
-            else:
+        def quant(key):
+            kind, side, i, g = key
+            if kind == "act" and side == "q":
+                codes, planes = aq_codes[:, g, 256 * i : 256 * (i + 1)], aq_planes[:, g, 256 * i : 256 * (i + 1)]
+            elif kind == "act":
                 if g == 0:
-                    t["at_codes", i] = work.tile([P, 3, 2 * P], U32, tag="at_codes", name="at_codes", align_bytes=64)
-                    t["at_planes", i] = work.tile([P, 3, 2 * P], U8, tag="at_planes", name="at_planes", align_bytes=64)
-                quant((name, i, g), t["at_codes", i][:, g, :], t["at_planes", i][:, g, :])
-
-        def mm_act(i):
-            acc = psum.tile([P, N], F32, tag="acc", name="acc", bufs=4)
-            half = slice(P * (i % 2), P * (i % 2) + P)
-            for g in range(3):
-                nc.tensor.matmul_mx(
-                    out=acc[:], lhsT=t["at_codes", i // 2][:, g, half].bitcast(FP8X4), lhsT_scale=t["at_planes", i // 2][:, g, half],
-                    rhs=aq_codes[:, g, :].bitcast(FP8X4), rhs_scale=aq_planes[:, g, :], start=g == 0, stop=g == 2,
-                )
-            t["gram", i] = acc
-
-        def keep_gram(i):
-            nc.scalar.copy(out=gram_act[:, i, :], in_=t["gram", i][:])
-
-        def scale_err(i, h):
-            if h == 0:
-                t["err", "e", i] = work.tile([P, C], BF16, tag="err", name="err", bufs=3, align_bytes=64)
-            k = slice(1024 * h, 1024 * (h + 1))
-            nc.vector.tensor_tensor(out=t["err", "e", i][:, k], in0=t["bytes", i // 2][:, i % 2, k].bitcast(FP8), in1=scale[:, k], op=MULT)
-
-        def turn_err(name, i, b):
-            words = t["err", "e", i][:].bitcast(F32) if name == "e" else t["errq", i // 2][:, i % 2, :].bitcast(F32)
-            if ("sorted", (name, i, b)) in t:
-                turn((name, i, b), sorted_words((name, i, b)))
+                    t["at_codes", i] = ring("at_codes", [P, 3, 2 * P], U32, 2)
+                    t["at_planes", i] = ring("at_planes", [P, 3, 2 * P], U8, 2)
+                codes, planes = t["at_codes", i][:, g, :], t["at_planes", i][:, g, :]
+            elif kind == "err":
+                if side == "q":
+                    t["codes", "q", i], t["planes", "q", i] = rq_codes[:, i], rq_planes[:, i]
+                elif g == 0:
+                    t["codes", "t", i] = ring("e_codes", [P, 4, P], U32, 3)
+                    t["planes", "t", i] = ring("e_planes", [P, 4, P], U8, 3)
+                codes = t["codes", side, i][:, 2 * g : 2 * g + 2, :].rearrange("p g r -> p (g r)")
+                planes = t["planes", side, i][:, 2 * g : 2 * g + 2, :].rearrange("p g r -> p (g r)")
+            elif side == "q":
+                codes, planes = dq_codes[:, g, 256 * i : 256 * (i + 1)], dq_planes[:, g, 256 * i : 256 * (i + 1)]
             else:
-                turn((name, i, b), second(words, 2 * b) + second(words, 2 * b + 1))
+                codes, planes = dt_codes[:, i].rearrange("p g r -> p (g r)"), dt_planes[:, i].rearrange("p g r -> p (g r)")
+            nc.vector.quantize_mx(out=codes.bitcast(FP8X4), scales=planes, in_=t["kx", key][:].rearrange("p r t -> p (r t)"))
 
-        def evac_err(name, i, b):
-            evac((name, i, b))
-
-        def quant_err(name, i, b):
-            if b == 0:
-                t["codes", name, i] = work.tile([P, 4, P], U32, tag="e_codes", name="e_codes", bufs=3, align_bytes=64)
-                t["planes", name, i] = work.tile([P, 4, P], U8, tag="e_planes", name="e_planes", bufs=3, align_bytes=64)
-            quant((name, i, b), t["codes", name, i][:, 2 * b : 2 * b + 2, :].rearrange("p g r -> p (g r)"), t["planes", name, i][:, 2 * b : 2 * b + 2, :].rearrange("p g r -> p (g r)"))
-
-        def mm_err(name, i, h):
-            acc = psum.tile([P, N], F32, tag="acc", name="acc", bufs=4)
-            for g in range(4):
-                if name == "e":
-                    rhs, rhs_scale = v_codes[:, g, 1024 * h : 1024 * (h + 1)].bitcast(FP4X4), v_planes[:, g, 512 * h : 512 * (h + 1)]
+        def product(key):
+            kind, side, i, h = key
+            acc = psum.tile([P, N], F32, tag="bank", name="acc", bufs=8)
+            passes = {"act": 3, "back": 4, "gram": 2}[kind]
+            for g in range(passes):
+                if kind == "act":
+                    half = slice(P * (i % 2), P * (i % 2) + P)
+                    lhs, lhs_scale = t["at_codes", i // 2][:, g, half], t["at_planes", i // 2][:, g, half]
+                    rhs, rhs_scale = aq_codes[:, g, :].bitcast(FP8X4), aq_planes[:, g, :]
+                elif kind == "gram":
+                    lhs, lhs_scale = dt_codes[:, i, g, :], dt_planes[:, i, g, :]
+                    rhs, rhs_scale = dq_codes[:, g, :].bitcast(FP8X4), dq_planes[:, g, :]
                 else:
-                    rhs, rhs_scale = w_codes[:, g, 512 * h : 512 * (h + 1)].bitcast(FP8X4), w_planes[:, g, 512 * h : 512 * (h + 1)]
+                    lhs, lhs_scale = t["codes", side, i][:, g, :], t["planes", side, i][:, g, :]
+                    if side == "t":
+                        rhs, rhs_scale = v_codes[h][:, g, :].bitcast(FP4X4), v_planes[:, g, N * h : N * (h + 1)]
+                    else:
+                        rhs, rhs_scale = w_codes[:, h, g, :].bitcast(FP8X4), w_planes[:, h, g, :]
                 nc.tensor.matmul_mx(
-                    out=acc[:], lhsT=t["codes", name, i][:, g, :].bitcast(FP8X4), lhsT_scale=t["planes", name, i][:, g, :],
-                    rhs=rhs, rhs_scale=rhs_scale, start=g == 0, stop=g == 3,
+                    out=acc[:], lhsT=lhs.bitcast(FP8X4), lhsT_scale=lhs_scale, rhs=rhs, rhs_scale=rhs_scale, start=g == 0, stop=g == passes - 1
                 )
-            t["back", name, i, h] = acc
+            t["acc", key] = acc
 
-        def slope_mul(name, i, h):
-            if h == 0:
-                t["d", name, i] = work.tile([P, 2, 2, P, 2], BF16, tag="d", name="d", bufs=3, align_bytes=64)
-            nc.vector.tensor_tensor(
-                out=t["d", name, i][:, h],
-                in0=t["back", name, i, h][:].rearrange("p (m u e) -> p u m e", u=2, e=2),
-                in1=t["slope", name, i][:, 512 * h : 512 * (h + 1)].rearrange("p (m u e) -> p u m e", u=2, e=2),
-                op=MULT,
-            )
-
-        def turn_d(name, i):
-            words = t["d", name, i][:].rearrange("p h u m e -> p (h u m e)").bitcast(F32)
-            turn(("d", name, i), [words[:, P * j : P * (j + 1)] for j in range(4)])
-
-        def evac_d(name, i):
-            evac(("d", name, i))
-
-        def quant_d(name, i):
-            if name == "e":
-                quant(("d", name, i), dt_codes[:, i].rearrange("p g r -> p (g r)"), dt_planes[:, i].rearrange("p g r -> p (g r)"))
+        def use(key):
+            kind, side, i, h = key
+            acc = t["acc", key]
+            if kind == "act":
+                nc.scalar.copy(out=gram_act[:, i, :], in_=acc[:])
+            elif kind == "back":
+                d = ring("d", [P, 2, P, 2], BF16, 8)
+                nc.vector.tensor_tensor(
+                    out=d[:],
+                    in0=acc[:].rearrange("p (m u e) -> p u m e", u=2, e=2),
+                    in1=t["slope", side, i][:, N * h : N * (h + 1)].rearrange("p (m u e) -> p u m e", u=2, e=2),
+                    op=MULT,
+                )
+                if side == "t":
+                    was_read("slope_t")
+                t["d", side, i, h] = d[:].rearrange("p u m e -> p u (m e)").bitcast(F32)
             else:
-                x = t["kx", ("d", name, i)]
-                for g in range(2):
-                    nc.vector.quantize_mx(
-                        out=dq_codes[:, g, P * i : P * (i + 1)].bitcast(FP8X4), scales=dq_planes[:, g, P * i : P * (i + 1)],
-                        in_=x[:, g].rearrange("p r t -> p (r t)"),
-                    )
+                nc.vector.tensor_tensor(out=gram_act[:, i, :], in0=acc[:], in1=gram_act[:, i, :], op=MULT)
+                nc.sync.dma_start(out=train_rows(out, i // 2)[:, i % 2, :], in_=gram_act[:, i, :])
 
         def w_lay(c, engine):
-            g, n0 = c // 4, 256 * (c % 4)
-            x = work.tile([P, 256, 4], BF16, tag="wx", name="wx", bufs=4, align_bytes=64)
-            dst = x[:].rearrange("p (c i) t -> p c t i", i=4)
-            src = t["w", g][:, :, n0 : n0 + 256].rearrange("p t (c i) -> p c t i", i=4)
-            if engine == "act":
-                nc.scalar.copy(out=dst, in_=src)
-            else:
-                nc.vector.tensor_copy(out=dst, in_=src)
+            h, g, n0 = c // 8, c % 8 // 2, 256 * (c % 2)
+            x = ring("wx", [P, 256, 4], BF16, WXB)
+            src = t["w", h, g][:, :, n0 : n0 + 256]
+            copy_on(engine, out=x[:].rearrange("p (c i) t -> p c t i", i=4), in_=src.rearrange("p t (c i) -> p c t i", i=4))
             t["wx", c] = x
+            was_read("w_raw")
 
         def w_quant(c):
-            g, n0 = c // 4, 256 * (c % 4)
+            h, g, n0 = c // 8, c % 8 // 2, 256 * (c % 2)
             nc.vector.quantize_mx(
-                out=w_codes[:, g, n0 : n0 + 256].bitcast(FP8X4), scales=w_planes[:, g, n0 : n0 + 256],
+                out=w_codes[:, h, g, n0 : n0 + 256].bitcast(FP8X4), scales=w_planes[:, h, g, n0 : n0 + 256],
                 in_=t["wx", c][:].rearrange("p n t -> p (n t)"),
             )
 
-        def mm_gram(i):
-            acc = psum.tile([P, N], F32, tag="acc", name="acc", bufs=4)
-            for g in range(2):
-                nc.tensor.matmul_mx(
-                    out=acc[:], lhsT=dt_codes[:, i, g, :].bitcast(FP8X4), lhsT_scale=dt_planes[:, i, g, :],
-                    rhs=dq_codes[:, g, :].bitcast(FP8X4), rhs_scale=dq_planes[:, g, :], start=g == 0, stop=g == 1,
-                )
-            t["ge", i] = acc
-
-        def finish(i):
-            res = work.tile([P, N], F32, tag="wx", name="res", bufs=4, align_bytes=64)
-            nc.vector.tensor_tensor(out=res[:], in0=t["ge", i][:], in1=gram_act[:, i, :], op=MULT)
-            nc.sync.dma_start(out=out[P * i : P * (i + 1), :], in_=res[:])
-
-        for fn, a in [
-            (load_act, (act_query, "aq", 0)),
-            (load_bytes, (0,)),
-            (load_act, (act_query, "aq", 1)),
-            (load_act, (act_train, "at", 0)),
-            (load_act, (act_train, "at", 1)),
-            (load_act, (act_train, "at", 2)),
-            (load_w, (0,)),
-            (load_bytes, (1,)),
-            (load_bytes, (2,)),
-            (load_v, ()),
-            (load_w, (1,)),
-            (load_slope, ("e", 0)),
-            (load_err_query, (0,)),
-            (load_slope, ("r", 0)),
-            (load_act, (act_train, "at", 3)),
-            (load_w, (2,)),
-            (load_slope, ("e", 1)),
-            (load_slope, ("r", 1)),
-            (load_err_query, (1,)),
-            (load_slope, ("e", 2)),
-            (load_bytes, (3,)),
-            (load_w, (3,)),
-            (load_slope, ("e", 3)),
-        ]:
-            fn(*a)
-
-        waiting = []
-        count = {"lay": 0, "quant": 0}
-
-        def settle(q, n):
-            while len(q) > n:
-                fn, a = q[0]
-                q.remove(q[0])
-                fn(*a)
-
-        ORDER = """
-            q00 q01 q02 s0a q10 q11 q12 a00 a01 s0b a02 s1a e00 a10 a11 a12 pa s1b s2a a20 e01 wl a21 e10
-            s2b A0 A1 a22 wv wq s3a s3b wl e11 e20 A2 wl A3 B00 wq B01 e21 wl s4a e30 e31 wq wq
-            s4b wl A4 B10 B11 B20 wq wl pr s5a d0 wq s5b e40 e41 B21 wq wv wl wl pr B30 wq B31
-            wq wv wq e50 r00 e51 d1 wq B40 wl wq pr B41 wv r01 wq r10 wl wq wv r11 pr wq d2
-            wl wq A5 B50 B51 r20 r21 d3 pa s6a s6b d4 R00 R01 R10 pr pr R11 r30 r31 e60 pa s7a e61
-            a30 pa R20 R21 a31 d5 s7b a32 x0 R30 R31 B60 x1 e70 x2 e71 x3 A6 B61 B70 G0 B71 G1 G2
-            G3 d6 d7 G4 G5 A7 G6 G7
+        PLAN = """
+L0 c00 c01 c10 c11
+e00 e01 q00 e10 e11 | B00
+q01 | B01 c20 c21 B10 c30 c31
+e20 e21 q02 d0 | sse30 sse31 ssq10 ssq11 B11 ssq12
+e30 e31 q10 q11 | c40 c41 B20 sse40 ssa00 ssa01 B21
+e40 q12 d1 a00 | ssa02 sse41 B30 ws
+e41 a01 a02 d2 | c50 ssa10 sva11 B31 ws c51 A0
+e50 a10 a11 | ssa12 ws wv B40 c60 A1
+e51 a12 d3 | ws wv svr00 svr01 c61 B41 A2
+e60 r00 r01 | ws ssr10 svr11 c70 B50 A3
+e61 r10 d4 r11 | ws c71 ssr20 ssr21 B51 R00
+e70 r20 r21 | ws svr30 ssr31 B60 R10
+e71 d5 r30 r31 | ws wv ws B61 R20 ssa20 ssa21 ssa22 B70 R30
+x00 a20 a21 a22 d6 | ws wv ws ws ssa30 ssa31 ssa32 B71 A4 A5 R01 R11
+x10 a30 a31 a32 d7 | R21 R31
+x01 | A6
+x11 | A7 G0 G1 G2 G3 G4 G5 G6 G7
         """
-        using = []
-        TURNS = {
-            "q": (turn_act, evac_act, quant_act, ("aq",)), "a": (turn_act, evac_act, quant_act, ("at",)),
-            "e": (turn_err, evac_err, quant_err, ("e",)), "r": (turn_err, evac_err, quant_err, ("r",)),
-            "d": (turn_d, evac_d, quant_d, ("e",)), "x": (turn_d, evac_d, quant_d, ("r",)),
-        }
-        PRODUCTS = {"A": (mm_act, keep_gram, ()), "B": (mm_err, slope_mul, ("e",)), "R": (mm_err, slope_mul, ("r",)), "G": (mm_gram, finish, ())}
-        PREPS = {"q": list(range(6, 6)), "a": list(range(8, 12)), "r": list(range(2, 8))}
-        with tc.manual_schedule():
-            spread_scale()
-            for item in ORDER.split():
-                kind = item[0]
-                if kind == "p":
-                    i = PREPS[item[1]][0]
-                    PREPS[item[1]].remove(i)
-                    if item[1] == "r":
-                        sort_err(i // 2, i % 2)
-                    else:
-                        sort_act("aq" if item[1] == "q" else "at", i // 3, i % 3)
-                elif item in ("wl", "wv"):
-                    w_lay(count["lay"], "act" if item == "wl" else "dve")
-                    count["lay"] += 1
-                elif item == "wq":
-                    w_quant(count["quant"])
-                    count["quant"] += 1
-                elif kind == "s":
-                    scale_err(int(item[1]), "ab".index(item[2]))
-                elif kind in TURNS:
-                    settle(using, 0)
-                    turn_fn, evac_fn, quant_fn, first = TURNS[kind]
-                    a = first + tuple([int(z) for z in item[1:]])
-                    turn_fn(*a)
-                    evac_fn(*a)
-                    waiting.append((quant_fn, a))
-                    settle(waiting, 1)
+        LOADS = """
+fb:0 sc fa:0 fb:1 vs v:0 fa:1 v:1 st:0 b:1 fa:2 q:1 st:1 a:0 b:2 w:00 a:1 w:01 st:2 r:0 w:02 b:3 r:1 w:03 sq:0 st:3 w:10 w:11 a:2 w:12 w:13 sq:1 a:3
+        """
+        KEY = {"e": ("err", "t"), "r": ("err", "q"), "q": ("act", "q"), "a": ("act", "t"), "d": ("d", "t"), "x": ("d", "q"),
+               "B": ("back", "t"), "R": ("back", "q"), "A": ("act", "t"), "G": ("gram", "t")}
+
+        def key_of(z):
+            return KEY[z[0]] + (int(z[1]), int(z[2]) if len(z) > 2 else 0)
+
+        LOAD = {"b": load_bytes, "fb": load_first_bytes, "fa": load_first_act, "sc": load_scale, "vs": load_v_scales, "v": load_v, "w": load_w, "r": load_err_query,
+                "q": lambda p: load_act("q", p), "a": lambda p: load_act("t", p), "st": lambda p: load_slope("t", p), "sq": lambda p: load_slope("q", p)}
+        todo_use, todo_quant, todo_wq, laid, fresh = [], [], [], [], []
+
+        def flush(q, fn, leave=0):
+            while len(q) > leave:
+                key = q[0]
+                q.remove(key)
+                fn(key)
+
+        def extra(z):
+            if z[0] == "c":
+                widen(int(z[1]), int(z[2]))
+            elif z[0] == "w":
+                fresh.append(len(laid))
+                w_lay(len(laid), z[1])
+                laid.append(z)
+            elif z[0] == "L":
+                for y in LOADS.split():
+                    name = y.split(":")
+                    waiting.append(({"b": "bytes_pair", "q": "act_raw", "a": "act_raw", "w": "w_raw", "st": "slope_t"}.get(name[0]), LOAD[name[0]], [int(c) for c in (name[1] if len(name) > 1 else "")]))
+                issue_loads()
+            else:
+                sort_words(key_of(z[2:]), z[1])
+
+        with tc.manual_schedule(engines={mybir.EngineType.PE, mybir.EngineType.SP}):
+            make_identity(nc, ident[:])
+            nc.vector.memset(v_planes[:].rearrange("p g n -> p (g n)").bitcast(I32), 0)
+            for z in PLAN.split():
+                if z == "|" or z == "!":
+                    continue
+                if z[0] in "eqardx":
+                    turn(key_of(z))
+                    empty(key_of(z))
+                    quant(key_of(z))
+                elif z[0] in "BRAG":
+                    product(key_of(z))
+                    use(key_of(z))
                 else:
-                    settle(using, 0)
-                    settle(waiting, 0)
-                    mm, use, first = PRODUCTS[kind]
-                    a = first + tuple([int(z) for z in item[1:]])
-                    mm(*a)
-                    using.append((use, a))
-            settle(using, 0)
+                    extra(z)
+                    flush(fresh, w_quant)
+                issue_loads()

@@ -16,7 +16,8 @@ FP8 = mybir.dt.float8_e4m3fn
 FP8X4 = mybir.dt.float8_e4m3fn_x4
 FP4X4 = mybir.dt.float4_e2m1fn_x4
 MULT = mybir.AluOpType.mult
-WXB = 5
+ADD = mybir.AluOpType.add
+WXB = 1
 
 
 def tile_gradient_inner_products_s11_kernel(
@@ -57,7 +58,7 @@ def tile_gradient_inner_products_s11_kernel(
         def query_rows(src, pair):
             return src[256 * pair : 256 * (pair + 1), :].rearrange("(j p) k -> p j k", j=2)
 
-        RING = {"bytes_pair": (2, 4), "act_raw": (3, 3), "w_raw": (3, 2), "slope_t": (3, 4)}
+        RING = {"bytes_pair": (2, 4), "act_raw": (3, 3), "w_raw": (4, 1), "slope_t": (3, 4)}
         unread = {name: 0 for name in RING}
         waiting = []
 
@@ -257,41 +258,37 @@ def tile_gradient_inner_products_s11_kernel(
                 nc.sync.dma_start(out=train_rows(out, i // 2)[:, i % 2, :], in_=gram_act[:, i, :])
 
         def w_lay(c, engine):
-            h, g, n0 = c // 8, c % 8 // 2, 256 * (c % 2)
-            x = ring("wx", [P, 256, 4], BF16, WXB)
-            src = t["w", h, g][:, :, n0 : n0 + 256]
-            copy_on(engine, out=x[:].rearrange("p (c i) t -> p c t i", i=4), in_=src.rearrange("p t (c i) -> p c t i", i=4))
+            x = ring("wx_" + engine, [P, N, 4], BF16, WXB)
+            src = t["w", c // 4, c % 4]
+            if engine == "g":
+                nc.gpsimd.tensor_scalar(out=x[:], in0=src[:].rearrange("p t n -> p n t"), scalar1=1.0, scalar2=0.0, op0=MULT, op1=ADD)
+            else:
+                copy_on(engine, out=x[:].rearrange("p (c i) t -> p c t i", i=4), in_=src[:].rearrange("p t (c i) -> p c t i", i=4))
             t["wx", c] = x
             was_read("w_raw")
 
         def w_quant(c):
-            h, g, n0 = c // 8, c % 8 // 2, 256 * (c % 2)
             nc.vector.quantize_mx(
-                out=w_codes[:, h, g, n0 : n0 + 256].bitcast(FP8X4), scales=w_planes[:, h, g, n0 : n0 + 256],
-                in_=t["wx", c][:].rearrange("p n t -> p (n t)"),
+                out=w_codes[:, c // 4, c % 4, :].bitcast(FP8X4), scales=w_planes[:, c // 4, c % 4, :], in_=t["wx", c][:].rearrange("p n t -> p (n t)")
             )
 
         PLAN = """
-L0 c00 c01 c10 c11
-e00 e01 q00 e10 e11 | B00
-q01 | B01 c20 c21 B10 c30 c31
-e20 e21 q02 d0 | sse30 sse31 ssq10 ssq11 B11 ssq12
-e30 e31 q10 q11 | c40 c41 B20 sse40 ssa00 ssa01 B21
-e40 q12 d1 a00 | ssa02 sse41 B30 ws
-e41 a01 a02 d2 | c50 ssa10 sva11 B31 ws c51 A0
-e50 a10 a11 | ssa12 ws wv B40 c60 A1
-e51 a12 d3 | ws wv svr00 svr01 c61 B41 A2
-e60 r00 r01 | ws ssr10 svr11 c70 B50 A3
-e61 r10 d4 r11 | ws c71 ssr20 ssr21 B51 R00
-e70 r20 r21 | ws svr30 ssr31 B60 R10
-e71 d5 r30 r31 | ws wv ws B61 R20 ssa20 ssa21 ssa22 B70 R30
-x00 a20 a21 a22 d6 | ws wv ws ws ssa30 ssa31 ssa32 B71 A4 A5 R01 R11
-x10 a30 a31 a32 d7 | R21 R31
-x01 | A6
-x11 | A7 G0 G1 G2 G3 G4 G5 G6 G7
+| L0 c00 c01 |
+e00 e01 q00 | c10 c11 |
+e10 e11 | | B00
+q01 | c20 c21 | B01 B10
+e20 e21 q02 d0 | c30 c31 sse30 sse31 ssq10 ssq11 ssq12 wg | B11
+e30 e31 q10 q11 q12 d1 | c40 c41 ssa00 ssa01 ssa02 wg | B20 B21
+e40 e41 a00 a01 a02 d2 | c50 c51 ssa10 ssa11 ssa12 wv wg | B30 B31 A0 A1
+e50 e51 a10 a11 a12 d3 | c60 c61 ssr00 ssr01 ssr10 ssr11 wv wg | B40 B41 A2 A3
+e60 e61 r00 r01 r10 r11 d4 | c70 c71 ssr20 ssr21 ssr30 ssr31 sse70 sse71 wg | B50 B51 R00 R10
+e70 e71 r20 r21 r30 r31 d5 | ssa20 ssa21 ssa22 wg | B60 B61 R20 R30
+x00 a20 a21 a22 d6 | ssa30 ssa31 ssa32 | B70 B71 R01 R11
+x10 a30 a31 a32 d7 | | R21 R31 A4 A5
+x01 x11 | | A6 A7 G0 G1 G2 G3 G4 G5 G6 G7
         """
         LOADS = """
-fb:0 sc fa:0 fb:1 vs v:0 fa:1 v:1 st:0 b:1 fa:2 q:1 st:1 a:0 b:2 w:00 a:1 w:01 st:2 r:0 w:02 b:3 r:1 w:03 sq:0 st:3 w:10 w:11 a:2 w:12 w:13 sq:1 a:3
+fb:0 sc fa:0 fb:1 vs v:0 fa:1 v:1 st:0 b:1 fa:2 w:00 q:1 st:1 a:0 b:2 w:01 a:1 w:02 st:2 w:03 r:0 b:3 w:10 w:11 r:1 sq:0 st:3 w:12 a:2 w:13 sq:1 a:3
         """
         KEY = {"e": ("err", "t"), "r": ("err", "q"), "q": ("act", "q"), "a": ("act", "t"), "d": ("d", "t"), "x": ("d", "q"),
                "B": ("back", "t"), "R": ("back", "q"), "A": ("act", "t"), "G": ("gram", "t")}
@@ -324,20 +321,31 @@ fb:0 sc fa:0 fb:1 vs v:0 fa:1 v:1 st:0 b:1 fa:2 q:1 st:1 a:0 b:2 w:00 a:1 w:01 s
             else:
                 sort_words(key_of(z[2:]), z[1])
 
-        with tc.manual_schedule(engines={mybir.EngineType.PE, mybir.EngineType.SP}):
+        with tc.manual_schedule(engines={mybir.EngineType.PE, mybir.EngineType.SP, mybir.EngineType.DVE, mybir.EngineType.Pool}):
             make_identity(nc, ident[:])
             nc.vector.memset(v_planes[:].rearrange("p g n -> p (g n)").bitcast(I32), 0)
-            for z in PLAN.split():
-                if z == "|" or z == "!":
-                    continue
-                if z[0] in "eqardx":
+            for line in PLAN.split("\n")[1:-1]:
+                turns, extras, products = [part.split() for part in line.split("|")]
+                for z in turns:
                     turn(key_of(z))
                     empty(key_of(z))
+                if "wv" in extras:
+                    extra("wv")
+                for z in turns:
                     quant(key_of(z))
-                elif z[0] in "BRAG":
+                if "wv" in extras:
+                    flush(fresh, w_quant)
+                flush(todo_wq, w_quant)
+                for z in extras:
+                    if z != "wv":
+                        extra(z)
+                todo_wq.extend(fresh)
+                fresh.clear()
+                issue_loads()
+                for z in products:
+                    if z == "!":
+                        flush(todo_wq, w_quant)
+                        continue
                     product(key_of(z))
                     use(key_of(z))
-                else:
-                    extra(z)
-                    flush(fresh, w_quant)
-                issue_loads()
+                    issue_loads()

@@ -5,6 +5,7 @@ from concourse.masks import make_identity
 
 M, N, K, C, F = 1024, 512, 1536, 2048, 1024
 P = 128
+PASS = 512
 FLOPS = 2 * (M * F * C + N * F * C + M * N * F + M * N * K)
 
 F32 = mybir.dt.float32
@@ -17,7 +18,9 @@ FP8X4 = mybir.dt.float8_e4m3fn_x4
 FP4X4 = mybir.dt.float4_e2m1fn_x4
 MULT = mybir.AluOpType.mult
 ADD = mybir.AluOpType.add
-WXB = 1
+
+TRAIN, QUERY = "train", "query"
+STREAMS = {"err_bytes": (2, 4), "act_raw": (3, 3), "w_raw": (4, 1), "slope_train": (3, 4)}
 
 
 def tile_gradient_inner_products_s11_kernel(
@@ -27,7 +30,7 @@ def tile_gradient_inner_products_s11_kernel(
     with ExitStack() as ctx:
         keep = ctx.enter_context(tc.tile_pool(name="keep", bufs=1))
         work = ctx.enter_context(tc.tile_pool(name="work", bufs=2))
-        psum = ctx.enter_context(tc.psum_pool(name="psum", bufs=4))
+        psum = ctx.enter_context(tc.psum_pool(name="psum", bufs=8))
         t = {}
 
         def kept(name, shape, dtype):
@@ -35,6 +38,9 @@ def tile_gradient_inner_products_s11_kernel(
 
         def ring(name, shape, dtype, bufs):
             return work.tile(shape, dtype, tag=name, name=name, bufs=bufs, align_bytes=64)
+
+        def bank(shape):
+            return psum.tile(shape, F32, tag="bank", name="bank", bufs=8)
 
         ident = kept("ident", [P, P], F32)
         v_planes = kept("v_planes", [P, 4, F], U8)
@@ -50,43 +56,40 @@ def tile_gradient_inner_products_s11_kernel(
         dq_planes = kept("dq_planes", [P, 2, N], U8)
         dt_codes = kept("dt_codes", [P, 8, 2, P], U32)
         dt_planes = kept("dt_planes", [P, 8, 2, P], U8)
-        gram_act = kept("gram_act", [P, 8, N], F32)
+        gram = kept("gram", [P, 8, N], F32)
 
-        def train_rows(src, pair):
-            return src[256 * pair : 256 * (pair + 1), :].rearrange("(p j) k -> p j k", j=2)
+        def rows(src, side, pair):
+            pattern = "(p j) k -> p j k" if side == TRAIN else "(j p) k -> p j k"
+            return src[256 * pair : 256 * (pair + 1), :].rearrange(pattern, j=2)
 
-        def query_rows(src, pair):
-            return src[256 * pair : 256 * (pair + 1), :].rearrange("(j p) k -> p j k", j=2)
-
-        RING = {"bytes_pair": (2, 4), "act_raw": (3, 3), "w_raw": (4, 1), "slope_t": (3, 4)}
-        unread = {name: 0 for name in RING}
+        unread = {name: 0 for name in STREAMS}
         waiting = []
 
         def streamed(name, shape, dtype):
-            unread[name] += RING[name][1]
-            return ring(name, shape, dtype, RING[name][0])
+            unread[name] += STREAMS[name][1]
+            return ring(name, shape, dtype, STREAMS[name][0])
 
         def was_read(name):
             unread[name] -= 1
 
         def issue_loads():
             while waiting:
-                name, fn, a = waiting[0]
-                if name in RING and unread[name] > (RING[name][0] - 1) * RING[name][1]:
+                name, load, args = waiting[0]
+                if name in STREAMS and unread[name] > (STREAMS[name][0] - 1) * STREAMS[name][1]:
                     return
                 waiting.remove(waiting[0])
-                fn(*a)
+                load(*args)
 
         def load_first_bytes(j):
-            b = kept("bytes0_%d" % j, [P, C], U8)
-            nc.sync.dma_start(out=b[:], in_=train_rows(err_train_bytes, 0)[:, j, :])
-            t["bytes", j] = b[:]
+            raw = kept("first_bytes%d" % j, [P, C], U8)
+            nc.sync.dma_start(out=raw[:], in_=rows(err_train_bytes, TRAIN, 0)[:, j, :])
+            t["bytes", j] = raw[:]
 
         def load_bytes(pair):
-            b = streamed("bytes_pair", [P, 2, C], U8)
-            nc.sync.dma_start(out=b[:], in_=train_rows(err_train_bytes, pair))
+            raw = streamed("err_bytes", [P, 2, C], U8)
+            nc.sync.dma_start(out=raw[:], in_=rows(err_train_bytes, TRAIN, pair))
             for j in range(2):
-                t["bytes", 2 * pair + j] = b[:, j, :]
+                t["bytes", 2 * pair + j] = raw[:, j, :]
 
         def load_scale():
             nc.sync.dma_start(out=scale[:], in_=err_train_scale.rearrange("o (g p t) -> p (o g) t", p=P, t=4))
@@ -101,45 +104,43 @@ def tile_gradient_inner_products_s11_kernel(
         def load_v(h):
             nc.sync.dma_start(out=v_codes[h][:], in_=v_words[:, :, F * h : F * (h + 1)].rearrange("g p b -> p g b"))
 
+        def load_first_act(g):
+            raw = kept("first_act%d" % g, [P, 2, PASS], BF16)
+            nc.sync.dma_start(out=raw[:], in_=rows(act_query, QUERY, 0)[:, :, PASS * g : PASS * (g + 1)])
+            t["act", QUERY, 0, g] = raw[:]
+
         def load_act(side, pair):
             raw = streamed("act_raw", [P, 2, K], BF16)
-            nc.sync.dma_start(out=raw[:], in_=query_rows(act_query, pair) if side == "q" else train_rows(act_train, pair))
+            nc.sync.dma_start(out=raw[:], in_=rows(act_train if side == TRAIN else act_query, side, pair))
             for g in range(3):
-                t["act", side, pair, g] = raw[:, :, 512 * g : 512 * (g + 1)]
+                t["act", side, pair, g] = raw[:, :, PASS * g : PASS * (g + 1)]
 
-        def load_first_act(g):
-            raw = kept("act_first%d" % g, [P, 2, 512], BF16)
-            nc.sync.dma_start(out=raw[:], in_=query_rows(act_query, 0)[:, :, 512 * g : 512 * (g + 1)])
-            t["act", "q", 0, g] = raw[:]
-
-        def load_w(h, g):
+        def load_w(piece):
+            h, g = divmod(piece, 4)
             raw = streamed("w_raw", [P, 4, N], BF16)
-            nc.sync.dma_start(out=raw[:], in_=w[512 * g : 512 * (g + 1), N * h : N * (h + 1)].rearrange("(p t) n -> p t n", t=4))
-            t["w", h, g] = raw
+            nc.sync.dma_start(out=raw[:], in_=w[PASS * g : PASS * (g + 1), N * h : N * (h + 1)].rearrange("(p t) n -> p t n", t=4))
+            t["w_raw", piece] = raw
 
         def load_err_query(pair):
-            raw = kept("errq%d" % pair, [P, 2, C], BF16)
-            nc.sync.dma_start(out=raw[:], in_=query_rows(err_query, pair))
+            raw = kept("err_query%d" % pair, [P, 2, C], BF16)
+            nc.sync.dma_start(out=raw[:], in_=rows(err_query, QUERY, pair))
             for j in range(2):
                 for b in range(2):
-                    t["err", "q", 2 * pair + j, b] = raw[:, j, 1024 * b : 1024 * (b + 1)]
+                    t["err", QUERY, 2 * pair + j, b] = raw[:, j, 1024 * b : 1024 * (b + 1)]
 
         def load_slope(side, pair):
-            if side == "t":
-                s = streamed("slope_t", [P, 2, F], BF16)
-                nc.sync.dma_start(out=s[:], in_=train_rows(slope_train, pair))
-            else:
-                s = kept("slope_q%d" % pair, [P, 2, F], BF16)
-                nc.sync.dma_start(out=s[:], in_=query_rows(slope_query, pair))
+            raw = streamed("slope_train", [P, 2, F], BF16) if side == TRAIN else kept("slope_query%d" % pair, [P, 2, F], BF16)
+            nc.sync.dma_start(out=raw[:], in_=rows(slope_train if side == TRAIN else slope_query, side, pair))
             for j in range(2):
-                t["slope", side, 2 * pair + j] = s[:, j, :]
+                t["slope", side, 2 * pair + j] = raw[:, j, :]
 
-        def widen(i, b):
-            x = ring("wide", [P, 1024], BF16, 4)
-            nc.scalar.copy(out=x[:], in_=t["bytes", i][:, 1024 * b : 1024 * (b + 1)].bitcast(FP8))
-            t["err", "t", i, b] = x[:]
-            if i >= 2:
-                was_read("bytes_pair")
+        def widen(i):
+            for b in range(2):
+                x = ring("wide", [P, 1024], BF16, 4)
+                nc.scalar.copy(out=x[:], in_=t["bytes", i][:, 1024 * b : 1024 * (b + 1)].bitcast(FP8))
+                t["err", TRAIN, i, b] = x[:]
+                if i >= 2:
+                    was_read("err_bytes")
 
         def words_of(key):
             if key[0] == "act":
@@ -147,53 +148,44 @@ def tile_gradient_inner_products_s11_kernel(
             return t[key].bitcast(F32).rearrange("p (a m) -> p a m", a=2)
 
         def words_read(key):
-            if key[0] == "act" and key[1:3] != ("q", 0):
+            if key[0] == "act" and key[1:3] != (QUERY, 0):
                 was_read("act_raw")
 
-        def copy_on(engine, out, in_):
-            if engine == "s":
-                nc.scalar.copy(out=out, in_=in_)
-            else:
-                nc.vector.tensor_copy(out=out, in_=in_)
-
-        def sort_words(key, engine):
+        def sort_words(key):
             x = ring("sorted", [P, 2, 2, P], F32, 6)
-            copy_on(engine, out=x[:], in_=words_of(key).rearrange("p a (m u) -> p a u m", u=2))
+            nc.scalar.copy(out=x[:], in_=words_of(key).rearrange("p a (m u) -> p a u m", u=2))
             t["sorted", key] = x
             words_read(key)
 
         def turn(key):
-            bank = psum.tile([P, 2, 2 * P], F32, tag="bank", name="turn", bufs=8)
+            kind, side, i, g = key
+            turned = bank([P, 2, 2 * P])
             for a in range(2):
                 for u in range(2):
-                    if key[0] == "d":
-                        src = t["d", "t", key[2], a][:, u, :] if key[1] == "t" else t["d", "q", 2 * key[2] + a, key[3]][:, u, :]
+                    if kind == "d":
+                        src = t["d", side, i, a][:, u, :] if side == TRAIN else t["d", side, 2 * i + a, g][:, u, :]
                     elif ("sorted", key) in t:
                         src = t["sorted", key][:, a, u, :]
                     else:
                         src = words_of(key)[:, a, u : 256 : 2]
-                    nc.tensor.transpose(bank[:, u, P * a : P * (a + 1)], src, ident[:])
-            t["bank", key] = bank
+                    nc.tensor.transpose(turned[:, u, P * a : P * (a + 1)], src, ident[:])
             if ("sorted", key) not in t:
                 words_read(key)
-
-        def empty(key):
-            x = ring("kx", [P, 2 * P, 4], BF16, 8)
-            if key[:2] == ("err", "t"):
-                g = 2 * key[3]
+            x = ring("k_first", [P, 2 * P, 4], BF16, 8)
+            if (kind, side) == ("err", TRAIN):
                 nc.vector.tensor_tensor(
                     out=x[:].rearrange("p (a m) (u e) -> p a m u e", a=2, u=2),
-                    in0=t["bank", key][:].bitcast(BF16).rearrange("p u (a m e) -> p a m u e", a=2, e=2),
-                    in1=scale[:, g : g + 2, :].rearrange("p a (u e) -> p a u e", u=2).unsqueeze(2).to_broadcast([P, 2, P, 2, 2]),
+                    in0=turned[:].bitcast(BF16).rearrange("p u (a m e) -> p a m u e", a=2, e=2),
+                    in1=scale[:, 2 * g : 2 * g + 2, :].rearrange("p a (u e) -> p a u e", u=2).unsqueeze(2).to_broadcast([P, 2, P, 2, 2]),
                     op=MULT,
                 )
             else:
-                nc.scalar.copy(out=x[:].bitcast(F32), in_=t["bank", key][:].rearrange("p u r -> p r u"))
-            t["kx", key] = x
+                nc.scalar.copy(out=x[:].bitcast(F32), in_=turned[:].rearrange("p u r -> p r u"))
+            t["k_first", key] = x
 
-        def quant(key):
+        def quantise(key):
             kind, side, i, g = key
-            if kind == "act" and side == "q":
+            if (kind, side) == ("act", QUERY):
                 codes, planes = aq_codes[:, g, 256 * i : 256 * (i + 1)], aq_planes[:, g, 256 * i : 256 * (i + 1)]
             elif kind == "act":
                 if g == 0:
@@ -201,151 +193,148 @@ def tile_gradient_inner_products_s11_kernel(
                     t["at_planes", i] = ring("at_planes", [P, 3, 2 * P], U8, 2)
                 codes, planes = t["at_codes", i][:, g, :], t["at_planes", i][:, g, :]
             elif kind == "err":
-                if side == "q":
-                    t["codes", "q", i], t["planes", "q", i] = rq_codes[:, i], rq_planes[:, i]
+                if side == QUERY:
+                    t["codes", side, i], t["planes", side, i] = rq_codes[:, i], rq_planes[:, i]
                 elif g == 0:
-                    t["codes", "t", i] = ring("e_codes", [P, 4, P], U32, 3)
-                    t["planes", "t", i] = ring("e_planes", [P, 4, P], U8, 3)
+                    t["codes", side, i] = ring("et_codes", [P, 4, P], U32, 3)
+                    t["planes", side, i] = ring("et_planes", [P, 4, P], U8, 3)
                 codes = t["codes", side, i][:, 2 * g : 2 * g + 2, :].rearrange("p g r -> p (g r)")
                 planes = t["planes", side, i][:, 2 * g : 2 * g + 2, :].rearrange("p g r -> p (g r)")
-            elif side == "q":
+            elif side == QUERY:
                 codes, planes = dq_codes[:, g, 256 * i : 256 * (i + 1)], dq_planes[:, g, 256 * i : 256 * (i + 1)]
             else:
                 codes, planes = dt_codes[:, i].rearrange("p g r -> p (g r)"), dt_planes[:, i].rearrange("p g r -> p (g r)")
-            nc.vector.quantize_mx(out=codes.bitcast(FP8X4), scales=planes, in_=t["kx", key][:].rearrange("p r t -> p (r t)"))
+            nc.vector.quantize_mx(out=codes.bitcast(FP8X4), scales=planes, in_=t["k_first", key][:].rearrange("p r t -> p (r t)"))
 
-        def product(key):
-            kind, side, i, h = key
-            acc = psum.tile([P, N], F32, tag="bank", name="acc", bufs=8)
-            passes = {"act": 3, "back": 4, "gram": 2}[kind]
-            for g in range(passes):
-                if kind == "act":
-                    half = slice(P * (i % 2), P * (i % 2) + P)
-                    lhs, lhs_scale = t["at_codes", i // 2][:, g, half], t["at_planes", i // 2][:, g, half]
-                    rhs, rhs_scale = aq_codes[:, g, :].bitcast(FP8X4), aq_planes[:, g, :]
-                elif kind == "gram":
-                    lhs, lhs_scale = dt_codes[:, i, g, :], dt_planes[:, i, g, :]
-                    rhs, rhs_scale = dq_codes[:, g, :].bitcast(FP8X4), dq_planes[:, g, :]
-                else:
-                    lhs, lhs_scale = t["codes", side, i][:, g, :], t["planes", side, i][:, g, :]
-                    if side == "t":
-                        rhs, rhs_scale = v_codes[h][:, g, :].bitcast(FP4X4), v_planes[:, g, N * h : N * (h + 1)]
-                    else:
-                        rhs, rhs_scale = w_codes[:, h, g, :].bitcast(FP8X4), w_planes[:, h, g, :]
+        def accumulate(acc, operands):
+            for g, (lhs, lhs_scale, rhs, rhs_scale) in enumerate(operands):
                 nc.tensor.matmul_mx(
-                    out=acc[:], lhsT=lhs.bitcast(FP8X4), lhsT_scale=lhs_scale, rhs=rhs, rhs_scale=rhs_scale, start=g == 0, stop=g == passes - 1
+                    out=acc, lhsT=lhs.bitcast(FP8X4), lhsT_scale=lhs_scale, rhs=rhs, rhs_scale=rhs_scale, start=g == 0, stop=g == len(operands) - 1
                 )
-            t["acc", key] = acc
 
-        def use(key):
-            kind, side, i, h = key
-            acc = t["acc", key]
-            if kind == "act":
-                nc.scalar.copy(out=gram_act[:, i, :], in_=acc[:])
-            elif kind == "back":
-                d = ring("d", [P, 2, P, 2], BF16, 8)
-                nc.vector.tensor_tensor(
-                    out=d[:],
-                    in0=acc[:].rearrange("p (m u e) -> p u m e", u=2, e=2),
-                    in1=t["slope", side, i][:, N * h : N * (h + 1)].rearrange("p (m u e) -> p u m e", u=2, e=2),
-                    op=MULT,
-                )
-                if side == "t":
-                    was_read("slope_t")
-                t["d", side, i, h] = d[:].rearrange("p u m e -> p u (m e)").bitcast(F32)
+        def back(side, i, h):
+            acc = bank([P, N])
+            if side == TRAIN:
+                moving = [(v_codes[h][:, g, :].bitcast(FP4X4), v_planes[:, g, N * h : N * (h + 1)]) for g in range(4)]
             else:
-                nc.vector.tensor_tensor(out=gram_act[:, i, :], in0=acc[:], in1=gram_act[:, i, :], op=MULT)
-                nc.sync.dma_start(out=train_rows(out, i // 2)[:, i % 2, :], in_=gram_act[:, i, :])
+                moving = [(w_codes[:, h, g, :].bitcast(FP8X4), w_planes[:, h, g, :]) for g in range(4)]
+            accumulate(acc[:], [(t["codes", side, i][:, g, :], t["planes", side, i][:, g, :]) + moving[g] for g in range(4)])
+            d = ring("d", [P, 2, P, 2], BF16, 8)
+            nc.vector.tensor_tensor(
+                out=d[:],
+                in0=acc[:].rearrange("p (m u e) -> p u m e", u=2, e=2),
+                in1=t["slope", side, i][:, N * h : N * (h + 1)].rearrange("p (m u e) -> p u m e", u=2, e=2),
+                op=MULT,
+            )
+            if side == TRAIN:
+                was_read("slope_train")
+            t["d", side, i, h] = d[:].rearrange("p u m e -> p u (m e)").bitcast(F32)
 
-        def w_lay(c, engine):
-            x = ring("wx_" + engine, [P, N, 4], BF16, WXB)
-            src = t["w", c // 4, c % 4]
-            if engine == "g":
-                nc.gpsimd.tensor_scalar(out=x[:], in0=src[:].rearrange("p t n -> p n t"), scalar1=1.0, scalar2=0.0, op0=MULT, op1=ADD)
+        def gram_act(i):
+            acc = bank([P, N])
+            half = slice(P * (i % 2), P * (i % 2) + P)
+            codes, planes = t["at_codes", i // 2], t["at_planes", i // 2]
+            accumulate(acc[:], [(codes[:, g, half], planes[:, g, half], aq_codes[:, g, :].bitcast(FP8X4), aq_planes[:, g, :]) for g in range(3)])
+            nc.scalar.copy(out=gram[:, i, :], in_=acc[:])
+
+        def finish(i, cols):
+            acc = bank([P, cols.stop - cols.start])
+            accumulate(acc[:], [(dt_codes[:, i, g, :], dt_planes[:, i, g, :], dq_codes[:, g, cols].bitcast(FP8X4), dq_planes[:, g, cols]) for g in range(2)])
+            nc.vector.tensor_tensor(out=gram[:, i, cols], in0=acc[:], in1=gram[:, i, cols], op=MULT)
+            nc.sync.dma_start(out=rows(out, TRAIN, i // 2)[:, i % 2, cols], in_=gram[:, i, cols])
+
+        def lay_w(piece, engine):
+            x = ring("w_laid_gpsimd" if engine == "gpsimd" else "w_laid", [P, N, 4], BF16, 1)
+            raw = t["w_raw", piece]
+            if engine == "gpsimd":
+                nc.gpsimd.tensor_scalar(out=x[:], in0=raw[:].rearrange("p t n -> p n t"), scalar1=1.0, scalar2=0.0, op0=MULT, op1=ADD)
             else:
-                copy_on(engine, out=x[:].rearrange("p (c i) t -> p c t i", i=4), in_=src[:].rearrange("p t (c i) -> p c t i", i=4))
-            t["wx", c] = x
+                copy = nc.scalar.copy if engine == "scalar" else nc.vector.tensor_copy
+                copy(out=x[:].rearrange("p (c i) t -> p c t i", i=4), in_=raw[:].rearrange("p t (c i) -> p c t i", i=4))
+            t["w_laid", piece] = x
             was_read("w_raw")
 
-        def w_quant(c):
-            nc.vector.quantize_mx(
-                out=w_codes[:, c // 4, c % 4, :].bitcast(FP8X4), scales=w_planes[:, c // 4, c % 4, :], in_=t["wx", c][:].rearrange("p n t -> p (n t)")
-            )
+        def quantise_w(piece):
+            h, g = divmod(piece, 4)
+            nc.vector.quantize_mx(out=w_codes[:, h, g, :].bitcast(FP8X4), scales=w_planes[:, h, g, :], in_=t["w_laid", piece][:].rearrange("p n t -> p (n t)"))
 
-        PLAN = """
-| L0 c00 c01 |
-e00 e01 q00 | c10 c11 |
-e10 e11 | | B00
-q01 | c20 c21 | B01 B10
-e20 e21 q02 d0 | c30 c31 sse30 sse31 ssq10 ssq11 ssq12 wg | B11
-e30 e31 q10 q11 q12 d1 | c40 c41 ssa00 ssa01 ssa02 wg | B20 B21
-e40 e41 a00 a01 a02 d2 | c50 c51 ssa10 ssa11 ssa12 wv wg | B30 B31 A0 A1
-e50 e51 a10 a11 a12 d3 | c60 c61 ssr00 ssr01 ssr10 ssr11 wv wg | B40 B41 A2 A3
-e60 e61 r00 r01 r10 r11 d4 | c70 c71 ssr20 ssr21 ssr30 ssr31 sse70 sse71 wg | B50 B51 R00 R10
-e70 e71 r20 r21 r30 r31 d5 | ssa20 ssa21 ssa22 wg | B60 B61 R20 R30
-x00 a20 a21 a22 d6 | ssa30 ssa31 ssa32 | B70 B71 R01 R11
-x10 a30 a31 a32 d7 | | R21 R31 A4 A5
-x01 x11 | | A6 A7 G0 G1 G2 G3 G4 G5 G6 G7
-        """
-        LOADS = """
-fb:0 sc fa:0 fb:1 vs v:0 fa:1 v:1 st:0 b:1 fa:2 w:00 q:1 st:1 a:0 b:2 w:01 a:1 w:02 st:2 w:03 r:0 b:3 w:10 w:11 r:1 sq:0 st:3 w:12 a:2 w:13 sq:1 a:3
-        """
-        KEY = {"e": ("err", "t"), "r": ("err", "q"), "q": ("act", "q"), "a": ("act", "t"), "d": ("d", "t"), "x": ("d", "q"),
-               "B": ("back", "t"), "R": ("back", "q"), "A": ("act", "t"), "G": ("gram", "t")}
+        def banks_of(kind, side, i):
+            if kind == "act":
+                return [(kind, side, i, g) for g in range(3)]
+            if kind == "err_pair":
+                return [("err", side, 2 * i + j, b) for j in range(2) for b in range(2)]
+            return [(kind, side, i, b) for b in range(2)]
 
-        def key_of(z):
-            return KEY[z[0]] + (int(z[1]), int(z[2]) if len(z) > 2 else 0)
-
-        LOAD = {"b": load_bytes, "fb": load_first_bytes, "fa": load_first_act, "sc": load_scale, "vs": load_v_scales, "v": load_v, "w": load_w, "r": load_err_query,
-                "q": lambda p: load_act("q", p), "a": lambda p: load_act("t", p), "st": lambda p: load_slope("t", p), "sq": lambda p: load_slope("q", p)}
-        todo_use, todo_quant, todo_wq, laid, fresh = [], [], [], [], []
-
-        def flush(q, fn, leave=0):
-            while len(q) > leave:
-                key = q[0]
-                q.remove(key)
-                fn(key)
-
-        def extra(z):
-            if z[0] == "c":
-                widen(int(z[1]), int(z[2]))
-            elif z[0] == "w":
-                fresh.append(len(laid))
-                w_lay(len(laid), z[1])
-                laid.append(z)
-            elif z[0] == "L":
-                for y in LOADS.split():
-                    name = y.split(":")
-                    waiting.append(({"b": "bytes_pair", "q": "act_raw", "a": "act_raw", "w": "w_raw", "st": "slope_t"}.get(name[0]), LOAD[name[0]], [int(c) for c in (name[1] if len(name) > 1 else "")]))
+        def round_of(turns, ahead, products):
+            for key in turns:
+                turn(key)
+            for key in turns:
+                quantise(key)
+            for fn, *args in ahead:
+                fn(*args)
+            issue_loads()
+            for fn, *args in products:
+                fn(*args)
                 issue_loads()
-            else:
-                sort_words(key_of(z[2:]), z[1])
 
-        with tc.manual_schedule(engines={mybir.EngineType.PE, mybir.EngineType.SP, mybir.EngineType.DVE, mybir.EngineType.Pool}):
+        def sorts(keys):
+            return [(sort_words, key) for key in keys]
+
+        def backs(side, tiles, halves):
+            return [(back, side, i, h) for i in tiles for h in halves]
+
+        waiting.extend(
+            [
+                (None, load_first_bytes, [0]), (None, load_scale, []), (None, load_first_bytes, [1]), (None, load_v_scales, []), (None, load_v, [0]),
+                (None, load_first_act, [0]), (None, load_v, [1]), ("slope_train", load_slope, [TRAIN, 0]), ("err_bytes", load_bytes, [1]),
+                (None, load_first_act, [1]), (None, load_first_act, [2]), ("w_raw", load_w, [0]), ("act_raw", load_act, [QUERY, 1]),
+                ("slope_train", load_slope, [TRAIN, 1]), ("err_bytes", load_bytes, [2]), ("act_raw", load_act, [TRAIN, 0]), ("w_raw", load_w, [1]),
+                ("act_raw", load_act, [TRAIN, 1]), ("w_raw", load_w, [2]), ("slope_train", load_slope, [TRAIN, 2]), (None, load_err_query, [0]),
+                ("err_bytes", load_bytes, [3]), ("w_raw", load_w, [3]), (None, load_err_query, [1]), (None, load_slope, [QUERY, 0]),
+                ("w_raw", load_w, [4]), ("slope_train", load_slope, [TRAIN, 3]), ("w_raw", load_w, [5]), ("act_raw", load_act, [TRAIN, 2]),
+                ("w_raw", load_w, [6]), ("w_raw", load_w, [7]), (None, load_slope, [QUERY, 1]), ("act_raw", load_act, [TRAIN, 3]),
+            ]
+        )
+        first_act = banks_of("act", QUERY, 0)
+        sides = [
+            (first_act[1:], []),
+            (banks_of("act", QUERY, 1), []),
+            (banks_of("act", TRAIN, 0), [(gram_act, 0), (gram_act, 1)]),
+            (banks_of("act", TRAIN, 1), [(gram_act, 2), (gram_act, 3)]),
+            (banks_of("err_pair", QUERY, 0), backs(QUERY, [0, 1], [0])),
+            (banks_of("err_pair", QUERY, 1), backs(QUERY, [2, 3], [0])),
+            (banks_of("act", TRAIN, 2), []),
+        ]
+        with tc.manual_schedule():
             make_identity(nc, ident[:])
             nc.vector.memset(v_planes[:].rearrange("p g n -> p (g n)").bitcast(I32), 0)
-            for line in PLAN.split("\n")[1:-1]:
-                turns, extras, products = [part.split() for part in line.split("|")]
-                for z in turns:
-                    turn(key_of(z))
-                    empty(key_of(z))
-                if "wv" in extras:
-                    extra("wv")
-                for z in turns:
-                    quant(key_of(z))
-                if "wv" in extras:
-                    flush(fresh, w_quant)
-                flush(todo_wq, w_quant)
-                for z in extras:
-                    if z != "wv":
-                        extra(z)
-                todo_wq.extend(fresh)
-                fresh.clear()
-                issue_loads()
-                for z in products:
-                    if z == "!":
-                        flush(todo_wq, w_quant)
-                        continue
-                    product(key_of(z))
-                    use(key_of(z))
-                    issue_loads()
+            issue_loads()
+            widen(0)
+            widen(1)
+            round_of(banks_of("err", TRAIN, 0), [], [])
+            round_of(banks_of("err", TRAIN, 1), [], backs(TRAIN, [0], [0]))
+            round_of(first_act[:1], [(widen, 2), (widen, 3)], backs(TRAIN, [0], [1]) + backs(TRAIN, [1], [0]))
+            for i in range(2, 8):
+                side_banks, side_products = sides[i - 2]
+                ahead = [(quantise_w, i - 3)] if i > 2 else []
+                ahead += [(widen, i + 1)] if 2 < i < 7 else []
+                ahead += sorts(sides[i - 1][0]) + [(lay_w, i - 2, "gpsimd")]
+                ahead += [(lay_w, 6, "scalar")] if i == 7 else []
+                round_of(
+                    banks_of("err", TRAIN, i) + side_banks + [("d", TRAIN, i - 2, 0)],
+                    ahead,
+                    backs(TRAIN, [i - 1], [0, 1] if i > 2 else [1]) + side_products,
+                )
+            turns = [("d", QUERY, 0, 0)] + banks_of("act", TRAIN, 2) + [("d", TRAIN, 6, 0)]
+            for key in turns:
+                turn(key)
+            quantise_w(6)
+            lay_w(7, "vector")
+            for key in turns:
+                quantise(key)
+            round_of([], [(quantise_w, 5), (quantise_w, 7)] + sorts(banks_of("act", TRAIN, 3)), backs(TRAIN, [7], [0, 1]) + [(gram_act, 4)] + backs(QUERY, [0, 1], [1]))
+            round_of([("d", QUERY, 1, 0)] + banks_of("act", TRAIN, 3) + [("d", TRAIN, 7, 0), ("d", QUERY, 0, 1)], [], backs(QUERY, [2, 3], [1]) + [(gram_act, 5)])
+            round_of([("d", QUERY, 1, 1)], [], [(finish, i, slice(0, N // 2)) for i in range(6)] + [(gram_act, 6)] + [(finish, i, slice(N // 2, N)) for i in range(3)] + [(gram_act, 7)] + [(finish, i, slice(N // 2, N)) for i in range(3, 6)])
+            finish(6, slice(0, N))
+            finish(7, slice(0, N // 2))
+            finish(7, slice(N // 2, N))

@@ -39,10 +39,11 @@ def tile_gradient_inner_products_s11_kernel(
         def ring(name, shape, dtype, bufs):
             return work.tile(shape, dtype, tag=name, name=name, bufs=bufs, align_bytes=64)
 
-        def bank(shape):
-            return psum.tile(shape, F32, tag="bank", name="bank", bufs=8)
+        def bank(shape, dtype=F32):
+            return psum.tile(shape, dtype, tag="bank", name="bank", bufs=8)
 
         ident = kept("ident", [P, P], F32)
+        ident_bf = kept("ident_bf", [P, P], BF16)
         v_planes = kept("v_planes", [P, 4, F], U8)
         v_codes = [kept("v_codes%d" % h, [P, 4, F], U8) for h in range(2)]
         scale = kept("scale", [P, 4, 4], F32)
@@ -151,14 +152,29 @@ def tile_gradient_inner_products_s11_kernel(
             if key[0] == "act" and key[1:3] != (QUERY, 0):
                 was_read("act_raw")
 
-        def sort_words(key):
+        def sort_words(key, engine="scalar"):
             x = ring("sorted", [P, 2, 2, P], F32, 6)
-            nc.scalar.copy(out=x[:], in_=words_of(key).rearrange("p a (m u) -> p a u m", u=2))
+            copy = nc.scalar.copy if engine == "scalar" else nc.vector.tensor_copy
+            copy(out=x[:], in_=words_of(key).rearrange("p a (m u) -> p a u m", u=2))
             t["sorted", key] = x
             words_read(key)
 
         def turn(key):
             kind, side, i, g = key
+            x = ring("k_first", [P, 2 * P, 4], BF16, 8)
+            t["k_first", key] = x
+            if (kind, side) == ("err", TRAIN):
+                turned = bank([P, 2, 4, P], BF16)
+                for a in range(2):
+                    for j in range(4):
+                        nc.tensor.matmul(turned[:, a, j, :], lhsT=t[key][:, PASS * a + j : PASS * (a + 1) : 4], rhs=ident_bf[:], start=True, stop=True)
+                nc.vector.tensor_tensor(
+                    out=x[:].rearrange("p (a m) t -> p a m t", a=2),
+                    in0=turned[:].rearrange("p a t m -> p a m t"),
+                    in1=scale[:, 2 * g : 2 * g + 2, :].unsqueeze(2).to_broadcast([P, 2, P, 4]),
+                    op=MULT,
+                )
+                return
             turned = bank([P, 2, 2 * P])
             for a in range(2):
                 for u in range(2):
@@ -171,17 +187,7 @@ def tile_gradient_inner_products_s11_kernel(
                     nc.tensor.transpose(turned[:, u, P * a : P * (a + 1)], src, ident[:])
             if ("sorted", key) not in t:
                 words_read(key)
-            x = ring("k_first", [P, 2 * P, 4], BF16, 8)
-            if (kind, side) == ("err", TRAIN):
-                nc.vector.tensor_tensor(
-                    out=x[:].rearrange("p (a m) (u e) -> p a m u e", a=2, u=2),
-                    in0=turned[:].bitcast(BF16).rearrange("p u (a m e) -> p a m u e", a=2, e=2),
-                    in1=scale[:, 2 * g : 2 * g + 2, :].rearrange("p a (u e) -> p a u e", u=2).unsqueeze(2).to_broadcast([P, 2, P, 2, 2]),
-                    op=MULT,
-                )
-            else:
-                nc.scalar.copy(out=x[:].bitcast(F32), in_=turned[:].rearrange("p u r -> p r u"))
-            t["k_first", key] = x
+            nc.scalar.copy(out=x[:].bitcast(F32), in_=turned[:].rearrange("p u r -> p r u"))
 
         def quantise(key):
             kind, side, i, g = key
@@ -219,6 +225,10 @@ def tile_gradient_inner_products_s11_kernel(
             else:
                 moving = [(w_codes[:, h, g, :].bitcast(FP8X4), w_planes[:, h, g, :]) for g in range(4)]
             accumulate(acc[:], [(t["codes", side, i][:, g, :], t["planes", side, i][:, g, :]) + moving[g] for g in range(4)])
+            t["back", side, i, h] = acc
+
+        def times_slope(side, i, h):
+            acc = t["back", side, i, h]
             d = ring("d", [P, 2, P, 2], BF16, 8)
             nc.vector.tensor_tensor(
                 out=d[:],
@@ -281,7 +291,7 @@ def tile_gradient_inner_products_s11_kernel(
             return [(sort_words, key) for key in keys]
 
         def backs(side, tiles, halves):
-            return [(back, side, i, h) for i in tiles for h in halves]
+            return [(fn, side, i, h) for i in tiles for h in halves for fn in (back, times_slope)]
 
         waiting.extend(
             [
@@ -306,6 +316,7 @@ def tile_gradient_inner_products_s11_kernel(
             (banks_of("act", TRAIN, 2), []),
         ]
         with tc.manual_schedule():
+            make_identity(nc, ident_bf[:])
             make_identity(nc, ident[:])
             nc.vector.memset(v_planes[:].rearrange("p g n -> p (g n)").bitcast(I32), 0)
             issue_loads()
@@ -334,7 +345,4 @@ def tile_gradient_inner_products_s11_kernel(
                 quantise(key)
             round_of([], [(quantise_w, 5), (quantise_w, 7)] + sorts(banks_of("act", TRAIN, 3)), backs(TRAIN, [7], [0, 1]) + [(gram_act, 4)] + backs(QUERY, [0, 1], [1]))
             round_of([("d", QUERY, 1, 0)] + banks_of("act", TRAIN, 3) + [("d", TRAIN, 7, 0), ("d", QUERY, 0, 1)], [], backs(QUERY, [2, 3], [1]) + [(gram_act, 5)])
-            round_of([("d", QUERY, 1, 1)], [], [(finish, i, slice(0, N // 2)) for i in range(6)] + [(gram_act, 6)] + [(finish, i, slice(N // 2, N)) for i in range(3)] + [(gram_act, 7)] + [(finish, i, slice(N // 2, N)) for i in range(3, 6)])
-            finish(6, slice(0, N))
-            finish(7, slice(0, N // 2))
-            finish(7, slice(N // 2, N))
+            round_of([("d", QUERY, 1, 1)], [], [(gram_act, 6), (gram_act, 7)] + [(finish, i, slice(0, N)) for i in range(8)])

@@ -20,7 +20,7 @@ MULT = mybir.AluOpType.mult
 ADD = mybir.AluOpType.add
 
 TRAIN, QUERY = "train", "query"
-STREAMS = {"err_bytes": (2, 4), "act_raw": (3, 3), "w_raw": (4, 1), "slope_train": (3, 4)}
+STREAMS = {"err_bytes": (4, 2), "act_raw": (3, 3), "w_raw": (4, 1), "slope_train": (3, 4)}
 
 
 def tile_gradient_inner_products_s11_kernel(
@@ -81,16 +81,17 @@ def tile_gradient_inner_products_s11_kernel(
                 waiting.remove(waiting[0])
                 load(*args)
 
-        def load_first_bytes(j):
-            raw = kept("first_bytes%d" % j, [P, C], U8)
-            nc.sync.dma_start(out=raw[:], in_=rows(err_train_bytes, TRAIN, 0)[:, j, :])
-            t["bytes", j] = raw[:]
+        def load_first_bytes(j, k0, k1):
+            raw = kept("first_bytes%d_%d" % (j, k0), [P, k1 - k0], U8)
+            nc.sync.dma_start(out=raw[:], in_=rows(err_train_bytes, TRAIN, 0)[:, j, k0:k1])
+            for g in range(k0 // PASS, k1 // PASS):
+                t["bytes", j, g] = (raw, PASS * g - k0)
 
-        def load_bytes(pair):
-            raw = streamed("err_bytes", [P, 2, C], U8)
-            nc.sync.dma_start(out=raw[:], in_=rows(err_train_bytes, TRAIN, pair))
-            for j in range(2):
-                t["bytes", 2 * pair + j] = raw[:, j, :]
+        def load_bytes(i):
+            raw = streamed("err_bytes", [P, C], U8)
+            nc.sync.dma_start(out=raw[:], in_=rows(err_train_bytes, TRAIN, i // 2)[:, i % 2, :])
+            for g in range(4):
+                t["bytes", i, g] = (raw, PASS * g)
 
         def load_scale():
             nc.sync.dma_start(out=scale[:], in_=err_train_scale.rearrange("o (g p t) -> p (o g) t", p=P, t=4))
@@ -136,10 +137,12 @@ def tile_gradient_inner_products_s11_kernel(
                 t["slope", side, 2 * pair + j] = raw[:, j, :]
 
         def widen(i):
-            for b in range(2):
-                x = ring("wide", [P, 1024], BF16, 4)
-                nc.scalar.copy(out=x[:], in_=t["bytes", i][:, 1024 * b : 1024 * (b + 1)].bitcast(FP8))
-                t["err", TRAIN, i, b] = x[:]
+            for key in banks_of("err", TRAIN, i):
+                g, n = key[3]
+                raw, k0 = t["bytes", i, g]
+                x = ring("wide", [P, PASS * n], BF16, 4)
+                nc.scalar.copy(out=x[:], in_=raw[:, k0 : k0 + PASS * n].bitcast(FP8))
+                t[key] = x[:]
                 if i >= 2:
                     was_read("err_bytes")
 
@@ -161,20 +164,23 @@ def tile_gradient_inner_products_s11_kernel(
 
         def turn(key):
             kind, side, i, g = key
-            x = ring("k_first", [P, 2 * P, 4], BF16, 8)
-            t["k_first", key] = x
             if (kind, side) == ("err", TRAIN):
-                turned = bank([P, 2, 4, P], BF16)
-                for a in range(2):
+                g, n = g
+                x = ring("k_first", [P, n * P, 4], BF16, 8)
+                t["k_first", key] = x
+                turned = bank([P, n, 4, P], BF16)
+                for a in range(n):
                     for j in range(4):
                         nc.tensor.matmul(turned[:, a, j, :], lhsT=t[key][:, PASS * a + j : PASS * (a + 1) : 4], rhs=ident_bf[:], start=True, stop=True)
                 nc.vector.tensor_tensor(
-                    out=x[:].rearrange("p (a m) t -> p a m t", a=2),
+                    out=x[:].rearrange("p (a m) t -> p a m t", a=n),
                     in0=turned[:].rearrange("p a t m -> p a m t"),
-                    in1=scale[:, 2 * g : 2 * g + 2, :].unsqueeze(2).to_broadcast([P, 2, P, 4]),
+                    in1=scale[:, g : g + n, :].unsqueeze(2).to_broadcast([P, n, P, 4]),
                     op=MULT,
                 )
                 return
+            x = ring("k_first", [P, 2 * P, 4], BF16, 8)
+            t["k_first", key] = x
             turned = bank([P, 2, 2 * P])
             for a in range(2):
                 for u in range(2):
@@ -199,13 +205,14 @@ def tile_gradient_inner_products_s11_kernel(
                     t["at_planes", i] = ring("at_planes", [P, 3, 2 * P], U8, 2)
                 codes, planes = t["at_codes", i][:, g, :], t["at_planes", i][:, g, :]
             elif kind == "err":
+                g, n = (2 * g, 2) if side == QUERY else g
                 if side == QUERY:
                     t["codes", side, i], t["planes", side, i] = rq_codes[:, i], rq_planes[:, i]
                 elif g == 0:
                     t["codes", side, i] = ring("et_codes", [P, 4, P], U32, 3)
                     t["planes", side, i] = ring("et_planes", [P, 4, P], U8, 3)
-                codes = t["codes", side, i][:, 2 * g : 2 * g + 2, :].rearrange("p g r -> p (g r)")
-                planes = t["planes", side, i][:, 2 * g : 2 * g + 2, :].rearrange("p g r -> p (g r)")
+                codes = t["codes", side, i][:, g : g + n, :].rearrange("p g r -> p (g r)")
+                planes = t["planes", side, i][:, g : g + n, :].rearrange("p g r -> p (g r)")
             elif side == QUERY:
                 codes, planes = dq_codes[:, g, 256 * i : 256 * (i + 1)], dq_planes[:, g, 256 * i : 256 * (i + 1)]
             else:
@@ -240,18 +247,22 @@ def tile_gradient_inner_products_s11_kernel(
                 was_read("slope_train")
             t["d", side, i, h] = d[:].rearrange("p u m e -> p u (m e)").bitcast(F32)
 
-        def gram_act(i):
+        def gram_act(i, engine="scalar"):
             acc = bank([P, N])
             half = slice(P * (i % 2), P * (i % 2) + P)
             codes, planes = t["at_codes", i // 2], t["at_planes", i // 2]
             accumulate(acc[:], [(codes[:, g, half], planes[:, g, half], aq_codes[:, g, :].bitcast(FP8X4), aq_planes[:, g, :]) for g in range(3)])
-            nc.scalar.copy(out=gram[:, i, :], in_=acc[:])
+            copy = nc.scalar.copy if engine == "scalar" else nc.vector.tensor_copy
+            copy(out=gram[:, i, :], in_=acc[:])
 
         def finish(i, cols):
             acc = bank([P, cols.stop - cols.start])
             accumulate(acc[:], [(dt_codes[:, i, g, :], dt_planes[:, i, g, :], dq_codes[:, g, cols].bitcast(FP8X4), dq_planes[:, g, cols]) for g in range(2)])
             nc.vector.tensor_tensor(out=gram[:, i, cols], in0=acc[:], in1=gram[:, i, cols], op=MULT)
-            nc.sync.dma_start(out=rows(out, TRAIN, i // 2)[:, i % 2, cols], in_=gram[:, i, cols])
+
+        def store(tiles, cols):
+            first = tiles.start % 2
+            nc.sync.dma_start(out=rows(out, TRAIN, tiles.start // 2)[:, first : first + tiles.stop - tiles.start, cols], in_=gram[:, tiles, cols])
 
         def lay_w(piece, engine):
             x = ring("w_laid_gpsimd" if engine == "gpsimd" else "w_laid", [P, N, 4], BF16, 1)
@@ -273,7 +284,7 @@ def tile_gradient_inner_products_s11_kernel(
                 return [(kind, side, i, g) for g in range(3)]
             if kind == "err_pair":
                 return [("err", side, 2 * i + j, b) for j in range(2) for b in range(2)]
-            return [(kind, side, i, b) for b in range(2)]
+            return [(kind, side, i, unit) for unit in ([(0, 1), (1, 1), (2, 2)] if i == 0 else [(0, 2), (2, 2)])]
 
         def round_of(turns, ahead, products):
             for key in turns:
@@ -295,22 +306,27 @@ def tile_gradient_inner_products_s11_kernel(
 
         waiting.extend(
             [
-                (None, load_first_bytes, [0]), (None, load_scale, []), (None, load_first_bytes, [1]), (None, load_v_scales, []), (None, load_v, [0]),
-                (None, load_first_act, [0]), (None, load_v, [1]), ("slope_train", load_slope, [TRAIN, 0]), ("err_bytes", load_bytes, [1]),
-                (None, load_first_act, [1]), (None, load_first_act, [2]), ("w_raw", load_w, [0]), ("act_raw", load_act, [QUERY, 1]),
-                ("slope_train", load_slope, [TRAIN, 1]), ("err_bytes", load_bytes, [2]), ("act_raw", load_act, [TRAIN, 0]), ("w_raw", load_w, [1]),
-                ("act_raw", load_act, [TRAIN, 1]), ("w_raw", load_w, [2]), ("slope_train", load_slope, [TRAIN, 2]), (None, load_err_query, [0]),
-                ("err_bytes", load_bytes, [3]), ("w_raw", load_w, [3]), (None, load_err_query, [1]), (None, load_slope, [QUERY, 0]),
-                ("w_raw", load_w, [4]), ("slope_train", load_slope, [TRAIN, 3]), ("w_raw", load_w, [5]), ("act_raw", load_act, [TRAIN, 2]),
-                ("w_raw", load_w, [6]), ("w_raw", load_w, [7]), (None, load_slope, [QUERY, 1]), ("act_raw", load_act, [TRAIN, 3]),
+                (None, load_first_bytes, [0,0,1024]), (None, load_scale, []), (None, load_first_bytes, [0,1024,2048]),
+                (None, load_first_bytes, [1,0,2048]), (None, load_v_scales, []), (None, load_v, [0]),
+                (None, load_first_act, [0]), (None, load_v, [1]), ("slope_train", load_slope, [TRAIN, 0]),
+                ("err_bytes", load_bytes, [2]), ("w_raw", load_w, [0]), ("err_bytes", load_bytes, [3]),
+                (None, load_first_act, [1]), (None, load_first_act, [2]), ("act_raw", load_act, [QUERY, 1]),
+                ("slope_train", load_slope, [TRAIN, 1]), ("err_bytes", load_bytes, [4]), ("act_raw", load_act, [TRAIN, 0]),
+                ("w_raw", load_w, [1]), ("err_bytes", load_bytes, [5]), ("act_raw", load_act, [TRAIN, 1]),
+                ("w_raw", load_w, [2]), ("slope_train", load_slope, [TRAIN, 2]), (None, load_err_query, [0]),
+                ("err_bytes", load_bytes, [6]), ("w_raw", load_w, [3]), ("err_bytes", load_bytes, [7]),
+                (None, load_err_query, [1]), (None, load_slope, [QUERY, 0]), ("w_raw", load_w, [4]),
+                ("slope_train", load_slope, [TRAIN, 3]), ("w_raw", load_w, [5]), ("act_raw", load_act, [TRAIN, 2]),
+                ("w_raw", load_w, [6]), ("w_raw", load_w, [7]), (None, load_slope, [QUERY, 1]),
+                ("act_raw", load_act, [TRAIN, 3]),
             ]
         )
         first_act = banks_of("act", QUERY, 0)
         sides = [
             (first_act[1:], []),
             (banks_of("act", QUERY, 1), []),
-            (banks_of("act", TRAIN, 0), [(gram_act, 0), (gram_act, 1)]),
-            (banks_of("act", TRAIN, 1), [(gram_act, 2), (gram_act, 3)]),
+            (banks_of("act", TRAIN, 0), [(gram_act, 0, "vector"), (gram_act, 1)]),
+            (banks_of("act", TRAIN, 1), [(gram_act, 2, "vector"), (gram_act, 3)]),
             (banks_of("err_pair", QUERY, 0), backs(QUERY, [0, 1], [0])),
             (banks_of("err_pair", QUERY, 1), backs(QUERY, [2, 3], [0])),
             (banks_of("act", TRAIN, 2), []),
@@ -321,8 +337,7 @@ def tile_gradient_inner_products_s11_kernel(
             nc.vector.memset(v_planes[:].rearrange("p g n -> p (g n)").bitcast(I32), 0)
             issue_loads()
             widen(0)
-            widen(1)
-            round_of(banks_of("err", TRAIN, 0), [], [])
+            round_of(banks_of("err", TRAIN, 0), [(widen, 1)], [])
             round_of(banks_of("err", TRAIN, 1), [], backs(TRAIN, [0], [0]))
             round_of(first_act[:1], [(widen, 2), (widen, 3)], backs(TRAIN, [0], [1]) + backs(TRAIN, [1], [0]))
             for i in range(2, 8):
@@ -341,8 +356,9 @@ def tile_gradient_inner_products_s11_kernel(
                 turn(key)
             quantise_w(6)
             lay_w(7, "vector")
-            for key in turns:
-                quantise(key)
-            round_of([], [(quantise_w, 5), (quantise_w, 7)] + sorts(banks_of("act", TRAIN, 3)), backs(TRAIN, [7], [0, 1]) + [(gram_act, 4)] + backs(QUERY, [0, 1], [1]))
-            round_of([("d", QUERY, 1, 0)] + banks_of("act", TRAIN, 3) + [("d", TRAIN, 7, 0), ("d", QUERY, 0, 1)], [], backs(QUERY, [2, 3], [1]) + [(gram_act, 5)])
-            round_of([("d", QUERY, 1, 1)], [], [(gram_act, 6), (gram_act, 7)] + [(finish, i, slice(0, N)) for i in range(8)])
+            round_of([], [(quantise_w, 5), (quantise_w, 7)] + [(quantise, key) for key in turns] + sorts(banks_of("act", TRAIN, 3)), backs(TRAIN, [7], [0, 1]) + backs(QUERY, [0, 1], [1]) + [(gram_act, 4)])
+            round_of([("d", QUERY, 1, 0)] + banks_of("act", TRAIN, 3) + [("d", TRAIN, 7, 0), ("d", QUERY, 0, 1)], [], backs(QUERY, [2, 3], [1]) + [(gram_act, 5, "vector")])
+            round_of([("d", QUERY, 1, 1)], [], [(gram_act, 6), (gram_act, 7)])
+            for i in range(8):
+                finish(i, slice(0, N))
+                store(slice(i, i + 1), slice(0, N))

@@ -356,9 +356,11 @@ def tile_gradient_inner_products_s11_kernel(
                 turn(key)
             quantise_w(6)
             lay_w(7, "vector")
-            round_of([], [(quantise_w, 5), (quantise_w, 7)] + [(quantise, key) for key in turns] + sorts(banks_of("act", TRAIN, 3)), backs(TRAIN, [7], [0, 1]) + backs(QUERY, [0, 1], [1]) + [(gram_act, 4)])
-            round_of([("d", QUERY, 1, 0)] + banks_of("act", TRAIN, 3) + [("d", TRAIN, 7, 0), ("d", QUERY, 0, 1)], [], backs(QUERY, [2, 3], [1]) + [(gram_act, 5, "vector")])
-            round_of([("d", QUERY, 1, 1)], [], [(gram_act, 6), (gram_act, 7)])
+            round_of([], [(quantise_w, 5), (quantise_w, 7)] + [(quantise, key) for key in turns] + sorts(banks_of("act", TRAIN, 3)), backs(TRAIN, [7], [0, 1]) + backs(QUERY, range(4), [1]))
+            last_act = banks_of("act", TRAIN, 3)
+            round_of([("d", QUERY, 1, 0), ("d", TRAIN, 7, 0), ("d", QUERY, 0, 1), last_act[0], ("d", QUERY, 1, 1)] + last_act[1:], [], [(gram_act, 4), (gram_act, 5)])
             for i in range(8):
+                if i in (4, 6):
+                    gram_act(4 + i // 2)
                 finish(i, slice(0, N))
                 store(slice(i, i + 1), slice(0, N))

@@ -179,7 +179,7 @@ def tile_gradient_inner_products_s11_kernel(
                     op=MULT,
                 )
                 return
-            x = ring("k_first", [P, 2 * P, 4], BF16, 8)
+            x = ring("w_laid_gpsimd", [P, 2 * P, 4], BF16, 1) if key == ("act", QUERY, 0, 0) else ring("k_first", [P, 2 * P, 4], BF16, 8)
             t["k_first", key] = x
             turned = bank([P, 2, 2 * P])
             for a in range(2):

@@ -97,10 +97,10 @@ def tile_gradient_inner_products_s11_kernel(
             nc.sync.dma_start(out=scale[:], in_=err_train_scale.rearrange("o (g p t) -> p (o g) t", p=P, t=4))
 
         def load_v_scales():
-            for q in range(4):
+            for r in range(4):
                 nc.sync.dma_start(
-                    out=v_planes[32 * q : 32 * q + 4, :, :].bitcast(I32),
-                    in_=v_scales[:, 4 * q : 4 * q + 4, :].rearrange("g r n -> r g n").bitcast(I32),
+                    out=v_planes[r:P:32, :, :].bitcast(I32),
+                    in_=v_scales[:, r:16:4, :].rearrange("g q n -> q g n").bitcast(I32),
                 )
 
         def load_v(h):
@@ -338,8 +338,8 @@ def tile_gradient_inner_products_s11_kernel(
             issue_loads()
             widen(0)
             round_of(banks_of("err", TRAIN, 0), [(widen, 1)], [])
-            round_of(banks_of("err", TRAIN, 1), [], backs(TRAIN, [0], [0]))
-            round_of(first_act[:1], [(widen, 2), (widen, 3)], backs(TRAIN, [0], [1]) + backs(TRAIN, [1], [0]))
+            round_of(banks_of("err", TRAIN, 1), [], [(back, TRAIN, 0, 0)])
+            round_of(first_act[:1], [(widen, 2), (widen, 3), (times_slope, TRAIN, 0, 0)], backs(TRAIN, [0], [1]) + backs(TRAIN, [1], [0]))
             for i in range(2, 8):
                 side_banks, side_products = sides[i - 2]
                 ahead = [(quantise_w, i - 3)] if i > 2 else []

@@ -19,6 +19,7 @@ FP4X4 = mybir.dt.float4_e2m1fn_x4
 MULT = mybir.AluOpType.mult
 ADD = mybir.AluOpType.add
 
+FROM, BOTH = 5, False
 TRAIN, QUERY = "train", "query"
 STREAMS = {"err_bytes": (4, 2), "act_raw": (3, 3), "w_raw": (4, 1), "slope_train": (3, 4)}
 
@@ -136,8 +137,8 @@ def tile_gradient_inner_products_s11_kernel(
             for j in range(2):
                 t["slope", side, 2 * pair + j] = raw[:, j, :]
 
-        def widen(i):
-            for key in banks_of("err", TRAIN, i):
+        def widen(i, part=slice(0, 3)):
+            for key in banks_of("err", TRAIN, i)[part]:
                 g, n = key[3]
                 raw, k0 = t["bytes", i, g]
                 x = ring("wide", [P, PASS * n], BF16, 4)
@@ -168,6 +169,19 @@ def tile_gradient_inner_products_s11_kernel(
                 g, n = g
                 x = ring("k_first", [P, n * P, 4], BF16, 8)
                 t["k_first", key] = x
+                if i >= FROM and (g == 0 or BOTH):
+                    turned = bank([P, 2, 2 * P])
+                    for a in range(2):
+                        for u in range(2):
+                            src = t["sorted", key][:, a, u, :] if ("sorted", key) in t else words_of(key)[:, a, u : 256 : 2]
+                            nc.tensor.transpose(turned[:, u, P * a : P * (a + 1)], src, ident[:])
+                    nc.vector.tensor_tensor(
+                        out=x[:].rearrange("p (a m) (u e) -> p a m u e", a=2, u=2),
+                        in0=turned[:].bitcast(BF16).rearrange("p u (a m e) -> p a m u e", a=2, e=2),
+                        in1=scale[:, g : g + 2, :].rearrange("p a (u e) -> p a u e", u=2).unsqueeze(2).to_broadcast([P, 2, P, 2, 2]),
+                        op=MULT,
+                    )
+                    return
                 turned = bank([P, n, 4, P], BF16)
                 for a in range(n):
                     for j in range(4):
@@ -307,11 +321,11 @@ def tile_gradient_inner_products_s11_kernel(
         waiting.extend(
             [
                 (None, load_first_bytes, [0,0,1024]), (None, load_scale, []), (None, load_first_bytes, [0,1024,2048]),
-                (None, load_first_bytes, [1,0,2048]), (None, load_v_scales, []), (None, load_v, [0]),
-                (None, load_first_act, [0]), (None, load_v, [1]), ("slope_train", load_slope, [TRAIN, 0]),
+                (None, load_first_bytes, [1,0,2048]), (None, load_v_scales, []), (None, load_first_act, [0]),
+                (None, load_v, [0]), (None, load_v, [1]), ("slope_train", load_slope, [TRAIN, 0]),
                 ("err_bytes", load_bytes, [2]), ("w_raw", load_w, [0]), ("err_bytes", load_bytes, [3]),
                 (None, load_first_act, [1]), (None, load_first_act, [2]), ("act_raw", load_act, [QUERY, 1]),
-                ("slope_train", load_slope, [TRAIN, 1]), ("err_bytes", load_bytes, [4]), ("act_raw", load_act, [TRAIN, 0]),
+                ("err_bytes", load_bytes, [4]), ("act_raw", load_act, [TRAIN, 0]), ("slope_train", load_slope, [TRAIN, 1]),
                 ("w_raw", load_w, [1]), ("err_bytes", load_bytes, [5]), ("act_raw", load_act, [TRAIN, 1]),
                 ("w_raw", load_w, [2]), ("slope_train", load_slope, [TRAIN, 2]), (None, load_err_query, [0]),
                 ("err_bytes", load_bytes, [6]), ("w_raw", load_w, [3]), ("err_bytes", load_bytes, [7]),
@@ -338,12 +352,14 @@ def tile_gradient_inner_products_s11_kernel(
             issue_loads()
             widen(0)
             round_of(banks_of("err", TRAIN, 0), [(widen, 1)], [])
-            round_of(banks_of("err", TRAIN, 1), [], [(back, TRAIN, 0, 0)])
-            round_of(first_act[:1], [(widen, 2), (widen, 3), (times_slope, TRAIN, 0, 0)], backs(TRAIN, [0], [1]) + backs(TRAIN, [1], [0]))
+            round_of(banks_of("err", TRAIN, 1) + first_act[:1], [(widen, 2), (widen, 3)], backs(TRAIN, [0], [0, 1]) + backs(TRAIN, [1], [0]))
             for i in range(2, 8):
                 side_banks, side_products = sides[i - 2]
                 ahead = [(quantise_w, i - 3)] if i > 2 else []
-                ahead += [(widen, i + 1)] if 2 < i < 7 else []
+                if 2 < i < 7:
+                    widen(i + 1, slice(0, 1))
+                ahead = ([(sort_words, banks_of("err", TRAIN, i + 1)[0], "scalar")] if 5 <= i + 1 < 8 else []) + ahead
+                ahead += [(widen, i + 1, slice(1, 2))] if 2 < i < 7 else []
                 ahead += sorts(sides[i - 1][0]) + [(lay_w, i - 2, "gpsimd")]
                 ahead += [(lay_w, 6, "scalar")] if i == 7 else []
                 round_of(

@@ -19,9 +19,12 @@ FP4X4 = mybir.dt.float4_e2m1fn_x4
 MULT = mybir.AluOpType.mult
 ADD = mybir.AluOpType.add
 
-FROM, BOTH = 5, False
 TRAIN, QUERY = "train", "query"
-STREAMS = {"err_bytes": (4, 2), "act_raw": (3, 3), "w_raw": (4, 1), "slope_train": (3, 4)}
+RINGS = {
+    "err_bytes": (3, 2), "act_raw": (3, 3), "w_raw": (3, 1), "slope_train": (2, 4), "err_query": (2, 4),
+    "wide": (3, 1), "sorted": (9, 1), "k_first": (10, 1), "d": (8, 1), "w_laid": (1, 1), "w_laid_gpsimd": (1, 1),
+    "et_codes": (3, 2), "at_codes": (2, 2),
+}
 
 
 def tile_gradient_inner_products_s11_kernel(
@@ -31,22 +34,46 @@ def tile_gradient_inner_products_s11_kernel(
     with ExitStack() as ctx:
         keep = ctx.enter_context(tc.tile_pool(name="keep", bufs=1))
         work = ctx.enter_context(tc.tile_pool(name="work", bufs=2))
-        psum = ctx.enter_context(tc.psum_pool(name="psum", bufs=8))
+        psum = ctx.enter_context(tc.psum_pool(name="psum", bufs=1))
         t = {}
+        readers = {}
+        taken = {name: 0 for name in RINGS}
+        free_banks = list(range(8))
 
         def kept(name, shape, dtype):
             return keep.tile(shape, dtype, name=name, align_bytes=64)
 
-        def ring(name, shape, dtype, bufs):
-            return work.tile(shape, dtype, tag=name, name=name, bufs=bufs, align_bytes=64)
+        def room(name):
+            return taken[name] < RINGS[name][0]
 
-        def bank(shape, dtype=F32):
-            return psum.tile(shape, dtype, tag="bank", name="bank", bufs=8)
+        def ring(name, owner, shape, dtype):
+            taken[name] += 1
+            readers[owner] = [name, RINGS[name][1]]
+            return work.tile(shape, dtype, tag=name, name=name, bufs=RINGS[name][0], align_bytes=64)
+
+        def was_read(owner):
+            if owner in readers:
+                readers[owner][1] -= 1
+                if readers[owner][1] == 0:
+                    taken[readers[owner][0]] -= 1
+
+        def there(*names):
+            return all(name in t for name in names)
+
+        def take_bank(key, shape, dtype=F32):
+            b = free_banks[0]
+            free_banks.remove(b)
+            t["bank", key] = psum.tile(shape, dtype, tag="bank%d" % b, name="bank%d" % b, bufs=1)
+            t["bank_number", key] = b
+            return t["bank", key]
+
+        def give_bank(key):
+            free_banks.append(t["bank_number", key])
+            return t["bank", key]
 
         ident = kept("ident", [P, P], F32)
-        ident_bf = kept("ident_bf", [P, P], BF16)
         v_planes = kept("v_planes", [P, 4, F], U8)
-        v_codes = [kept("v_codes%d" % h, [P, 4, F], U8) for h in range(2)]
+        v_codes = [kept("v_codes%d" % b, [P, 2, 2 * F], U8) for b in range(2)]
         scale = kept("scale", [P, 4, 4], F32)
         w_codes = kept("w_codes", [P, 2, 4, N], U32)
         w_planes = kept("w_planes", [P, 2, 4, N], U8)
@@ -64,38 +91,25 @@ def tile_gradient_inner_products_s11_kernel(
             pattern = "(p j) k -> p j k" if side == TRAIN else "(j p) k -> p j k"
             return src[256 * pair : 256 * (pair + 1), :].rearrange(pattern, j=2)
 
-        unread = {name: 0 for name in STREAMS}
-        waiting = []
-
-        def streamed(name, shape, dtype):
-            unread[name] += STREAMS[name][1]
-            return ring(name, shape, dtype, STREAMS[name][0])
-
-        def was_read(name):
-            unread[name] -= 1
-
-        def issue_loads():
-            while waiting:
-                name, load, args = waiting[0]
-                if name in STREAMS and unread[name] > (STREAMS[name][0] - 1) * STREAMS[name][1]:
-                    return
-                waiting.remove(waiting[0])
-                load(*args)
-
-        def load_first_bytes(j, k0, k1):
-            raw = kept("first_bytes%d_%d" % (j, k0), [P, k1 - k0], U8)
-            nc.sync.dma_start(out=raw[:], in_=rows(err_train_bytes, TRAIN, 0)[:, j, k0:k1])
-            for g in range(k0 // PASS, k1 // PASS):
-                t["bytes", j, g] = (raw, PASS * g - k0)
+        def load_first_bytes(b):
+            raw = kept("first_bytes%d" % b, [P, 1024], U8)
+            nc.sync.dma_start(out=raw[:], in_=rows(err_train_bytes, TRAIN, 0)[:, 0, 1024 * b : 1024 * (b + 1)])
+            t["bytes", 0, b] = raw[:]
+            return True
 
         def load_bytes(i):
-            raw = streamed("err_bytes", [P, C], U8)
+            if not room("err_bytes"):
+                return False
+            raw = ring("err_bytes", ("bytes", i), [P, C], U8)
             nc.sync.dma_start(out=raw[:], in_=rows(err_train_bytes, TRAIN, i // 2)[:, i % 2, :])
-            for g in range(4):
-                t["bytes", i, g] = (raw, PASS * g)
+            for b in range(2):
+                t["bytes", i, b] = raw[:, 1024 * b : 1024 * (b + 1)]
+            return True
 
         def load_scale():
             nc.sync.dma_start(out=scale[:], in_=err_train_scale.rearrange("o (g p t) -> p (o g) t", p=P, t=4))
+            t["scale"] = True
+            return True
 
         def load_v_scales():
             for r in range(4):
@@ -103,183 +117,237 @@ def tile_gradient_inner_products_s11_kernel(
                     out=v_planes[r:P:32, :, :].bitcast(I32),
                     in_=v_scales[:, r:16:4, :].rearrange("g q n -> q g n").bitcast(I32),
                 )
+            return True
 
-        def load_v(h):
-            nc.sync.dma_start(out=v_codes[h][:], in_=v_words[:, :, F * h : F * (h + 1)].rearrange("g p b -> p g b"))
-
-        def load_first_act(g):
-            raw = kept("first_act%d" % g, [P, 2, PASS], BF16)
-            nc.sync.dma_start(out=raw[:], in_=rows(act_query, QUERY, 0)[:, :, PASS * g : PASS * (g + 1)])
-            t["act", QUERY, 0, g] = raw[:]
+        def load_v(b):
+            nc.sync.dma_start(out=v_codes[b][:], in_=v_words[2 * b : 2 * b + 2].rearrange("g p b -> p g b"))
+            t["v", b] = True
+            return True
 
         def load_act(side, pair):
-            raw = streamed("act_raw", [P, 2, K], BF16)
+            if not room("act_raw"):
+                return False
+            raw = ring("act_raw", ("raw", "act", side, pair), [P, 2, K], BF16)
             nc.sync.dma_start(out=raw[:], in_=rows(act_train if side == TRAIN else act_query, side, pair))
             for g in range(3):
-                t["act", side, pair, g] = raw[:, :, PASS * g : PASS * (g + 1)]
+                t["rows", ("act", side, pair, g)] = raw[:, :, PASS * g : PASS * (g + 1)].bitcast(F32)
+            return True
 
         def load_w(piece):
+            if not room("w_raw"):
+                return False
             h, g = divmod(piece, 4)
-            raw = streamed("w_raw", [P, 4, N], BF16)
+            raw = ring("w_raw", ("w_raw", piece), [P, 4, N], BF16)
             nc.sync.dma_start(out=raw[:], in_=w[PASS * g : PASS * (g + 1), N * h : N * (h + 1)].rearrange("(p t) n -> p t n", t=4))
             t["w_raw", piece] = raw
+            return True
 
         def load_err_query(pair):
-            raw = kept("err_query%d" % pair, [P, 2, C], BF16)
+            if not room("err_query"):
+                return False
+            raw = ring("err_query", ("raw", "err", QUERY, pair), [P, 2, C], BF16)
             nc.sync.dma_start(out=raw[:], in_=rows(err_query, QUERY, pair))
             for j in range(2):
                 for b in range(2):
-                    t["err", QUERY, 2 * pair + j, b] = raw[:, j, 1024 * b : 1024 * (b + 1)]
+                    t["rows", ("err", QUERY, 2 * pair + j, b)] = raw[:, j, 1024 * b : 1024 * (b + 1)].bitcast(F32).rearrange("p (a m) -> p a m", a=2)
+            return True
 
         def load_slope(side, pair):
-            raw = streamed("slope_train", [P, 2, F], BF16) if side == TRAIN else kept("slope_query%d" % pair, [P, 2, F], BF16)
+            if side == TRAIN and not room("slope_train"):
+                return False
+            raw = ring("slope_train", ("slope", side, pair), [P, 2, F], BF16) if side == TRAIN else kept("slope_query%d" % pair, [P, 2, F], BF16)
             nc.sync.dma_start(out=raw[:], in_=rows(slope_train if side == TRAIN else slope_query, side, pair))
             for j in range(2):
                 t["slope", side, 2 * pair + j] = raw[:, j, :]
+            return True
 
-        def widen(i, part=slice(0, 3)):
-            for key in banks_of("err", TRAIN, i)[part]:
-                g, n = key[3]
-                raw, k0 = t["bytes", i, g]
-                x = ring("wide", [P, PASS * n], BF16, 4)
-                nc.scalar.copy(out=x[:], in_=raw[:, k0 : k0 + PASS * n].bitcast(FP8))
-                t[key] = x[:]
-                if i >= 2:
-                    was_read("err_bytes")
+        def widen(key):
+            kind, side, i, b = key
+            if not (there(("bytes", i, b)) and room("wide")):
+                return False
+            x = ring("wide", ("wide", key), [P, 1024], BF16)
+            nc.scalar.copy(out=x[:], in_=t["bytes", i, b].bitcast(FP8))
+            t["rows", key] = x[:].bitcast(F32).rearrange("p (a m) -> p a m", a=2)
+            was_read(("bytes", i))
+            return True
 
-        def words_of(key):
-            if key[0] == "act":
-                return t[key].bitcast(F32)
-            return t[key].bitcast(F32).rearrange("p (a m) -> p a m", a=2)
-
-        def words_read(key):
-            if key[0] == "act" and key[1:3] != (QUERY, 0):
-                was_read("act_raw")
+        def rows_read(key):
+            kind, side, i, g = key
+            was_read(("wide", key))
+            was_read(("raw", kind, side, i if kind == "act" else i // 2))
 
         def sort_words(key, engine="scalar"):
-            x = ring("sorted", [P, 2, 2, P], F32, 6)
+            if not (there(("rows", key)) and room("sorted")):
+                return False
+            x = ring("sorted", ("sorted", key), [P, 2, 2, P], F32)
             copy = nc.scalar.copy if engine == "scalar" else nc.vector.tensor_copy
-            copy(out=x[:], in_=words_of(key).rearrange("p a (m u) -> p a u m", u=2))
+            copy(out=x[:], in_=t["rows", key].rearrange("p a (m u) -> p a u m", u=2))
             t["sorted", key] = x
-            words_read(key)
+            rows_read(key)
+            return True
 
-        def turn(key):
+        def turn(key, stepped=False):
             kind, side, i, g = key
-            if (kind, side) == ("err", TRAIN):
-                g, n = g
-                x = ring("k_first", [P, n * P, 4], BF16, 8)
-                t["k_first", key] = x
-                if i >= FROM and (g == 0 or BOTH):
-                    turned = bank([P, 2, 2 * P])
-                    for a in range(2):
-                        for u in range(2):
-                            src = t["sorted", key][:, a, u, :] if ("sorted", key) in t else words_of(key)[:, a, u : 256 : 2]
-                            nc.tensor.transpose(turned[:, u, P * a : P * (a + 1)], src, ident[:])
-                    nc.vector.tensor_tensor(
-                        out=x[:].rearrange("p (a m) (u e) -> p a m u e", a=2, u=2),
-                        in0=turned[:].bitcast(BF16).rearrange("p u (a m e) -> p a m u e", a=2, e=2),
-                        in1=scale[:, g : g + 2, :].rearrange("p a (u e) -> p a u e", u=2).unsqueeze(2).to_broadcast([P, 2, P, 2, 2]),
-                        op=MULT,
-                    )
-                    return
-                turned = bank([P, n, 4, P], BF16)
-                for a in range(n):
-                    for j in range(4):
-                        nc.tensor.matmul(turned[:, a, j, :], lhsT=t[key][:, PASS * a + j : PASS * (a + 1) : 4], rhs=ident_bf[:], start=True, stop=True)
-                nc.vector.tensor_tensor(
-                    out=x[:].rearrange("p (a m) t -> p a m t", a=n),
-                    in0=turned[:].rearrange("p a t m -> p a m t"),
-                    in1=scale[:, g : g + n, :].unsqueeze(2).to_broadcast([P, n, P, 4]),
-                    op=MULT,
-                )
-                return
-            x = ring("w_laid_gpsimd", [P, 2 * P, 4], BF16, 1) if key == ("act", QUERY, 0, 0) else ring("k_first", [P, 2 * P, 4], BF16, 8)
-            t["k_first", key] = x
-            turned = bank([P, 2, 2 * P])
+            if kind == "d":
+                sources = [("d", side, i, a) if side == TRAIN else ("d", side, 2 * i + a, g) for a in range(2)]
+            else:
+                sources = [("rows" if stepped else "sorted", key)]
+            if not (there(*sources) and free_banks):
+                return False
+            turned = take_bank(key, [P, 2, 2 * P])
             for a in range(2):
                 for u in range(2):
                     if kind == "d":
-                        src = t["d", side, i, a][:, u, :] if side == TRAIN else t["d", side, 2 * i + a, g][:, u, :]
-                    elif ("sorted", key) in t:
-                        src = t["sorted", key][:, a, u, :]
+                        src = t[sources[a]][:, u, :]
+                    elif stepped:
+                        src = t["rows", key][:, a, u : 256 : 2]
                     else:
-                        src = words_of(key)[:, a, u : 256 : 2]
+                        src = t["sorted", key][:, a, u, :]
                     nc.tensor.transpose(turned[:, u, P * a : P * (a + 1)], src, ident[:])
-            if ("sorted", key) not in t:
-                words_read(key)
-            nc.scalar.copy(out=x[:].bitcast(F32), in_=turned[:].rearrange("p u r -> p r u"))
+            for source in sources:
+                was_read(source)
+            if stepped:
+                rows_read(key)
+            t["full", key] = True
+            return True
+
+        def empty(key, engine="scalar"):
+            kind, side, i, g = key
+            if not (there(("full", key)) and room("k_first")):
+                return False
+            turned = give_bank(key)
+            x = ring("k_first", ("k_first", key), [P, 2 * P, 4], BF16)
+            t["k_first", key] = x
+            if (kind, side) != ("err", TRAIN):
+                copy = nc.scalar.copy if engine == "scalar" else nc.vector.tensor_copy
+                copy(out=x[:].bitcast(F32), in_=turned[:].rearrange("p u r -> p r u"))
+            else:
+                nc.vector.tensor_tensor(
+                    out=x[:].rearrange("p (a m) (u e) -> p a m u e", a=2, u=2),
+                    in0=turned[:].bitcast(BF16).rearrange("p u (a m e) -> p a m u e", a=2, e=2),
+                    in1=scale[:, 2 * g : 2 * g + 2, :].rearrange("p a (u e) -> p a u e", u=2).unsqueeze(2).to_broadcast([P, 2, P, 2, 2]),
+                    op=MULT,
+                )
+            return True
 
         def quantise(key):
             kind, side, i, g = key
+            opens = side == TRAIN and g == 0 and kind != "d"
+            name = "at_codes" if kind == "act" else "et_codes"
+            if not there(("k_first", key)) or (opens and not room(name)):
+                return False
             if (kind, side) == ("act", QUERY):
                 codes, planes = aq_codes[:, g, 256 * i : 256 * (i + 1)], aq_planes[:, g, 256 * i : 256 * (i + 1)]
             elif kind == "act":
-                if g == 0:
-                    t["at_codes", i] = ring("at_codes", [P, 3, 2 * P], U32, 2)
-                    t["at_planes", i] = ring("at_planes", [P, 3, 2 * P], U8, 2)
+                if opens:
+                    t["at_codes", i] = ring("at_codes", ("at_codes", i), [P, 3, 2 * P], U32)
+                    t["at_planes", i] = work.tile([P, 3, 2 * P], U8, tag="at_planes", name="at_planes", bufs=RINGS[name][0], align_bytes=64)
                 codes, planes = t["at_codes", i][:, g, :], t["at_planes", i][:, g, :]
             elif kind == "err":
-                g, n = (2 * g, 2) if side == QUERY else g
                 if side == QUERY:
                     t["codes", side, i], t["planes", side, i] = rq_codes[:, i], rq_planes[:, i]
-                elif g == 0:
-                    t["codes", side, i] = ring("et_codes", [P, 4, P], U32, 3)
-                    t["planes", side, i] = ring("et_planes", [P, 4, P], U8, 3)
-                codes = t["codes", side, i][:, g : g + n, :].rearrange("p g r -> p (g r)")
-                planes = t["planes", side, i][:, g : g + n, :].rearrange("p g r -> p (g r)")
+                elif opens:
+                    t["codes", side, i] = ring("et_codes", ("codes", side, i), [P, 4, P], U32)
+                    t["planes", side, i] = work.tile([P, 4, P], U8, tag="et_planes", name="et_planes", bufs=RINGS[name][0], align_bytes=64)
+                codes = t["codes", side, i][:, 2 * g : 2 * g + 2, :].rearrange("p g r -> p (g r)")
+                planes = t["planes", side, i][:, 2 * g : 2 * g + 2, :].rearrange("p g r -> p (g r)")
             elif side == QUERY:
                 codes, planes = dq_codes[:, g, 256 * i : 256 * (i + 1)], dq_planes[:, g, 256 * i : 256 * (i + 1)]
             else:
                 codes, planes = dt_codes[:, i].rearrange("p g r -> p (g r)"), dt_planes[:, i].rearrange("p g r -> p (g r)")
             nc.vector.quantize_mx(out=codes.bitcast(FP8X4), scales=planes, in_=t["k_first", key][:].rearrange("p r t -> p (r t)"))
+            was_read(("k_first", key))
+            t["mx", key] = True
+            return True
 
-        def accumulate(acc, operands):
-            for g, (lhs, lhs_scale, rhs, rhs_scale) in enumerate(operands):
+        def accumulate(acc, operands, part=slice(0, 4)):
+            for g, (lhs, lhs_scale, rhs, rhs_scale) in list(enumerate(operands))[part]:
                 nc.tensor.matmul_mx(
                     out=acc, lhsT=lhs.bitcast(FP8X4), lhsT_scale=lhs_scale, rhs=rhs, rhs_scale=rhs_scale, start=g == 0, stop=g == len(operands) - 1
                 )
 
-        def back(side, i, h):
-            acc = bank([P, N])
+        def back(side, i, h, part=slice(0, 4)):
+            key = ("back", side, i, h)
+            needs = [("mx", ("err", side, i, g // 2)) for g in range(4)[part]]
+            needs += [("v", g // 2) if side == TRAIN else ("mx", ("w", 4 * h + g)) for g in range(4)[part]]
+            if not there(*needs) or (part.start == 0 and not free_banks):
+                return False
+            acc = take_bank(key, [P, N]) if part.start == 0 else t["bank", key]
             if side == TRAIN:
-                moving = [(v_codes[h][:, g, :].bitcast(FP4X4), v_planes[:, g, N * h : N * (h + 1)]) for g in range(4)]
+                moving = [(v_codes[g // 2][:, g % 2, F * h : F * (h + 1)].bitcast(FP4X4), v_planes[:, g, N * h : N * (h + 1)]) for g in range(4)]
             else:
                 moving = [(w_codes[:, h, g, :].bitcast(FP8X4), w_planes[:, h, g, :]) for g in range(4)]
-            accumulate(acc[:], [(t["codes", side, i][:, g, :], t["planes", side, i][:, g, :]) + moving[g] for g in range(4)])
-            t["back", side, i, h] = acc
+            accumulate(acc[:], [(t["codes", side, i][:, g, :], t["planes", side, i][:, g, :]) + moving[g] for g in range(4)], part)
+            if part.stop == 4:
+                was_read(("codes", side, i))
+                t["full", key] = True
+            return True
 
         def times_slope(side, i, h):
-            acc = t["back", side, i, h]
-            d = ring("d", [P, 2, P, 2], BF16, 8)
+            key = ("back", side, i, h)
+            if not (there(("full", key), ("slope", side, i)) and room("d")):
+                return False
+            d = ring("d", ("d", side, i, h), [P, 2, P, 2], BF16)
             nc.vector.tensor_tensor(
                 out=d[:],
-                in0=acc[:].rearrange("p (m u e) -> p u m e", u=2, e=2),
+                in0=give_bank(key)[:].rearrange("p (m u e) -> p u m e", u=2, e=2),
                 in1=t["slope", side, i][:, N * h : N * (h + 1)].rearrange("p (m u e) -> p u m e", u=2, e=2),
                 op=MULT,
             )
-            if side == TRAIN:
-                was_read("slope_train")
+            was_read(("slope", side, i // 2))
             t["d", side, i, h] = d[:].rearrange("p u m e -> p u (m e)").bitcast(F32)
+            return True
 
-        def gram_act(i, engine="scalar"):
-            acc = bank([P, N])
+        def gram_act(i):
+            key = ("gram_act", i)
+            if not (there(*[("mx", k) for k in aq(0) + aq(1) + at(i // 2)]) and free_banks):
+                return False
             half = slice(P * (i % 2), P * (i % 2) + P)
             codes, planes = t["at_codes", i // 2], t["at_planes", i // 2]
-            accumulate(acc[:], [(codes[:, g, half], planes[:, g, half], aq_codes[:, g, :].bitcast(FP8X4), aq_planes[:, g, :]) for g in range(3)])
+            accumulate(take_bank(key, [P, N])[:], [(codes[:, g, half], planes[:, g, half], aq_codes[:, g, :].bitcast(FP8X4), aq_planes[:, g, :]) for g in range(3)])
+            was_read(("at_codes", i // 2))
+            t["full", key] = True
+            return True
+
+        def keep_gram(i, engine="scalar"):
+            key = ("gram_act", i)
+            if not there(("full", key)):
+                return False
             copy = nc.scalar.copy if engine == "scalar" else nc.vector.tensor_copy
-            copy(out=gram[:, i, :], in_=acc[:])
+            copy(out=gram[:, i, :], in_=give_bank(key)[:])
+            t["gram", i] = True
+            return True
 
-        def finish(i, cols):
-            acc = bank([P, cols.stop - cols.start])
-            accumulate(acc[:], [(dt_codes[:, i, g, :], dt_planes[:, i, g, :], dq_codes[:, g, cols].bitcast(FP8X4), dq_planes[:, g, cols]) for g in range(2)])
-            nc.vector.tensor_tensor(out=gram[:, i, cols], in0=acc[:], in1=gram[:, i, cols], op=MULT)
+        def gram_err(i, part=slice(0, 2)):
+            key = ("gram_err", i)
+            needs = dt(i) + [k for g in range(2)[part] for k in dq(0, g) + dq(1, g)]
+            if not there(*[("mx", k) for k in needs]) or (part.start == 0 and not free_banks):
+                return False
+            acc = take_bank(key, [P, N]) if part.start == 0 else t["bank", key]
+            accumulate(acc[:], [(dt_codes[:, i, g, :], dt_planes[:, i, g, :], dq_codes[:, g, :].bitcast(FP8X4), dq_planes[:, g, :]) for g in range(2)], part)
+            if part.stop == 2:
+                t["full", key] = True
+            return True
 
-        def store(tiles, cols):
-            first = tiles.start % 2
-            nc.sync.dma_start(out=rows(out, TRAIN, tiles.start // 2)[:, first : first + tiles.stop - tiles.start, cols], in_=gram[:, tiles, cols])
+        def finish(i):
+            key = ("gram_err", i)
+            if not there(("full", key), ("gram", i)):
+                return False
+            nc.vector.tensor_tensor(out=gram[:, i, :], in0=give_bank(key)[:], in1=gram[:, i, :], op=MULT)
+            t["done", i] = True
+            return True
 
-        def lay_w(piece, engine):
-            x = ring("w_laid_gpsimd" if engine == "gpsimd" else "w_laid", [P, N, 4], BF16, 1)
+        def store(i):
+            if not there(("done", i)):
+                return False
+            nc.sync.dma_start(out=rows(out, TRAIN, i // 2)[:, i % 2, :], in_=gram[:, i, :])
+            return True
+
+        def lay_w(piece, engine="gpsimd"):
+            name = "w_laid_gpsimd" if engine == "gpsimd" else "w_laid"
+            if not (there(("w_raw", piece)) and room(name)):
+                return False
+            x = ring(name, ("w_laid", piece), [P, N, 4], BF16)
             raw = t["w_raw", piece]
             if engine == "gpsimd":
                 nc.gpsimd.tensor_scalar(out=x[:], in0=raw[:].rearrange("p t n -> p n t"), scalar1=1.0, scalar2=0.0, op0=MULT, op1=ADD)
@@ -287,96 +355,94 @@ def tile_gradient_inner_products_s11_kernel(
                 copy = nc.scalar.copy if engine == "scalar" else nc.vector.tensor_copy
                 copy(out=x[:].rearrange("p (c i) t -> p c t i", i=4), in_=raw[:].rearrange("p t (c i) -> p c t i", i=4))
             t["w_laid", piece] = x
-            was_read("w_raw")
+            was_read(("w_raw", piece))
+            return True
 
         def quantise_w(piece):
+            if not there(("w_laid", piece)):
+                return False
             h, g = divmod(piece, 4)
             nc.vector.quantize_mx(out=w_codes[:, h, g, :].bitcast(FP8X4), scales=w_planes[:, h, g, :], in_=t["w_laid", piece][:].rearrange("p n t -> p (n t)"))
+            was_read(("w_laid", piece))
+            t["mx", ("w", piece)] = True
+            return True
 
-        def banks_of(kind, side, i):
-            if kind == "act":
-                return [(kind, side, i, g) for g in range(3)]
-            if kind == "err_pair":
-                return [("err", side, 2 * i + j, b) for j in range(2) for b in range(2)]
-            return [(kind, side, i, unit) for unit in ([(0, 1), (1, 1), (2, 2)] if i == 0 else [(0, 2), (2, 2)])]
+        def et(i):
+            return [("err", TRAIN, i, b) for b in range(2)]
 
-        def round_of(turns, ahead, products):
-            for key in turns:
-                turn(key)
-            for key in turns:
-                quantise(key)
-            for fn, *args in ahead:
-                fn(*args)
-            issue_loads()
-            for fn, *args in products:
-                fn(*args)
-                issue_loads()
+        def eq(*tiles):
+            return [("err", QUERY, i, b) for i in tiles for b in range(2)]
+
+        def aq(pair):
+            return [("act", QUERY, pair, g) for g in range(3)]
+
+        def at(pair):
+            return [("act", TRAIN, pair, g) for g in range(3)]
+
+        def dt(*tiles):
+            return [("d", TRAIN, i, 0) for i in tiles]
+
+        def dq(pair, g):
+            return [("d", QUERY, pair, g)]
+
+        def each(fn, keys, *more):
+            return [(fn, key) + more for key in keys]
+
+        def both(fn, side, tiles, halves=(0, 1)):
+            return [(fn, side, i, h) for i in tiles for h in halves]
+
+        def write_out(queues):
+            while any(queues):
+                moved = False
+                for queue in queues[:-1]:
+                    while queue and queue[0][0](*queue[0][1:]):
+                        queue.remove(queue[0])
+                        moved = True
+                queue = queues[-1]
+                if not moved:
+                    assert queue and queue[0][0](*queue[0][1:]), [q[:1] for q in queues]
+                    queue.remove(queue[0])
+
+        lo, hi = slice(0, 2), slice(2, 4)
+
+        def prep(i):
+            return each(widen, et(i)) + each(sort_words, et(i))
 
         def sorts(keys):
-            return [(sort_words, key) for key in keys]
+            return each(sort_words, keys)
 
-        def backs(side, tiles, halves):
-            return [(fn, side, i, h) for i in tiles for h in halves for fn in (back, times_slope)]
+        def quants(i, keys):
+            return each(quantise, et(i)[:1] + keys[:1] + et(i)[1:] + keys[1:])
 
-        waiting.extend(
-            [
-                (None, load_first_bytes, [0,0,1024]), (None, load_scale, []), (None, load_first_bytes, [0,1024,2048]),
-                (None, load_first_bytes, [1,0,2048]), (None, load_v_scales, []), (None, load_first_act, [0]),
-                (None, load_v, [0]), (None, load_v, [1]), ("slope_train", load_slope, [TRAIN, 0]),
-                ("err_bytes", load_bytes, [2]), ("w_raw", load_w, [0]), ("err_bytes", load_bytes, [3]),
-                (None, load_first_act, [1]), (None, load_first_act, [2]), ("act_raw", load_act, [QUERY, 1]),
-                ("err_bytes", load_bytes, [4]), ("act_raw", load_act, [TRAIN, 0]), ("slope_train", load_slope, [TRAIN, 1]),
-                ("w_raw", load_w, [1]), ("err_bytes", load_bytes, [5]), ("act_raw", load_act, [TRAIN, 1]),
-                ("w_raw", load_w, [2]), ("slope_train", load_slope, [TRAIN, 2]), (None, load_err_query, [0]),
-                ("err_bytes", load_bytes, [6]), ("w_raw", load_w, [3]), ("err_bytes", load_bytes, [7]),
-                (None, load_err_query, [1]), (None, load_slope, [QUERY, 0]), ("w_raw", load_w, [4]),
-                ("slope_train", load_slope, [TRAIN, 3]), ("w_raw", load_w, [5]), ("act_raw", load_act, [TRAIN, 2]),
-                ("w_raw", load_w, [6]), ("w_raw", load_w, [7]), (None, load_slope, [QUERY, 1]),
-                ("act_raw", load_act, [TRAIN, 3]),
-            ]
-        )
-        first_act = banks_of("act", QUERY, 0)
-        sides = [
-            (first_act[1:], []),
-            (banks_of("act", QUERY, 1), []),
-            (banks_of("act", TRAIN, 0), [(gram_act, 0, "vector"), (gram_act, 1)]),
-            (banks_of("act", TRAIN, 1), [(gram_act, 2, "vector"), (gram_act, 3)]),
-            (banks_of("err_pair", QUERY, 0), backs(QUERY, [0, 1], [0])),
-            (banks_of("err_pair", QUERY, 1), backs(QUERY, [2, 3], [0])),
-            (banks_of("act", TRAIN, 2), []),
-        ]
+        sync = [(load_first_bytes, 0), (load_scale,), (load_first_bytes, 1), (load_bytes, 1), (load_v_scales,), (load_bytes, 2), (load_v, 0), (load_v, 1), (load_bytes, 3), (load_slope, TRAIN, 0),
+            (load_bytes, 4), (load_w, 0), (load_act, QUERY, 0), (load_act, QUERY, 1), (load_act, TRAIN, 0), (load_slope, TRAIN, 1), (load_w, 1), (load_bytes, 5), (load_act, TRAIN, 1),
+            (load_w, 2), (load_slope, TRAIN, 2), (load_bytes, 6), (load_act, TRAIN, 2), (load_w, 3), (load_bytes, 7), (load_err_query, 0), (load_slope, QUERY, 0), (load_w, 4), (load_err_query, 1), (load_slope, TRAIN, 3),
+            (load_w, 5), (load_slope, QUERY, 1), (load_w, 6), (load_act, TRAIN, 3), (load_w, 7)] + each(store, range(8))
+        tensor = each(turn, et(0) + et(1), True) + [(back, TRAIN, 0, 0, lo), (back, TRAIN, 0, 1, lo)] + each(turn, et(2)) + [(back, TRAIN, 0, 0, hi), (back, TRAIN, 0, 1, hi)] + both(back, TRAIN, [1])
+        vector = each(empty, et(0)) + each(quantise, et(0)[:1]) + each(empty, et(1)[:1]) + each(quantise, et(0)[1:]) + each(empty, et(1)[1:]) + each(quantise, et(1))
+        vector += each(empty, et(2)) + both(times_slope, TRAIN, [0, 1])
+        scalar = each(widen, et(0) + et(1)) + prep(2) + prep(3) + prep(4)
+        gpsimd = each(lay_w, range(6))
+        tensor += each(turn, et(3) + dt(0)) + each(turn, aq(0), True) + both(back, TRAIN, [2], [0]) + each(turn, aq(1), True) + both(back, TRAIN, [2], [1])
+        vector += each(empty, et(3)[:1]) + each(quantise, et(2)) + each(empty, et(3)[1:]) + each(quantise, et(3)[:1] + dt(0) + aq(0) + et(3)[1:] + aq(1)) + [(quantise_w, 0)] + both(times_slope, TRAIN, [2])
+        scalar += each(empty, dt(0) + aq(0) + aq(1)) + sorts(at(0))
+        for i in (4, 5, 6):
+            pair = i - 4
+            tensor += each(turn, et(i) + at(pair) + dt(i - 3)) + both(back, TRAIN, [i - 1]) + each(gram_act, [2 * pair, 2 * pair + 1])
+            vector += each(empty, et(i)) + each(quantise, et(i)[:1] + at(pair) + et(i)[1:] + dt(i - 3)) + each(sort_words, et(i + 1), "vector") + [(quantise_w, i - 3)] + both(times_slope, TRAIN, [i - 1])
+            scalar += each(empty, at(pair) + dt(i - 3)) + each(widen, et(i + 1)) + sorts(at(pair + 1) if i < 6 else eq(0, 1)) + each(keep_gram, [2 * pair, 2 * pair + 1])
+        tensor += each(turn, et(7) + eq(0, 1) + dt(4)) + both(back, TRAIN, [6]) + both(back, QUERY, [0, 1], [0])
+        vector += each(empty, et(7)) + each(quantise, et(7)[:1] + eq(0, 1) + dt(4) + et(7)[1:]) + [(quantise_w, 4)] + both(times_slope, TRAIN, [6]) + both(times_slope, QUERY, [0, 1], [0])
+        scalar += each(empty, eq(0, 1) + dt(4)) + sorts(eq(2, 3)) + [(lay_w, 6, "scalar")]
+        tensor += each(turn, eq(2, 3) + dt(5, 6) + dq(0, 0)) + both(back, TRAIN, [7]) + both(back, QUERY, [2, 3], [0])
+        vector += each(empty, eq(2), "vector") + [(quantise_w, 6)] + each(quantise, eq(2, 3)) + [(quantise_w, 5)] + each(quantise, dt(5, 6) + dq(0, 0)) + both(times_slope, TRAIN, [7]) + [(quantise_w, 7)] + both(times_slope, QUERY, [2, 3], [0])
+        scalar += each(empty, eq(3) + dt(5, 6) + dq(0, 0)) + [(lay_w, 7, "scalar")] + sorts(at(3))
+        tensor += both(back, QUERY, range(4), [1]) + each(turn, dq(0, 1) + dt(7) + dq(1, 0) + at(3)[:1] + dq(1, 1) + at(3)[1:])
+        vector += both(times_slope, QUERY, range(4), [1]) + each(quantise, dq(0, 1) + dq(1, 0) + dq(1, 1) + dt(7) + at(3)) + each(finish, range(8))
+        scalar += each(empty, dq(0, 1) + dq(1, 0) + dq(1, 1) + dt(7) + at(3)) + each(keep_gram, [6, 7])
+        first, second = slice(0, 1), slice(1, 2)
+        tensor += each(gram_err, range(4)) + [(gram_act, 6), (gram_err, 4), (gram_err, 5), (gram_act, 7), (gram_err, 6), (gram_err, 7)]
         with tc.manual_schedule():
-            make_identity(nc, ident_bf[:])
             make_identity(nc, ident[:])
             nc.vector.memset(v_planes[:].rearrange("p g n -> p (g n)").bitcast(I32), 0)
-            issue_loads()
-            widen(0)
-            round_of(banks_of("err", TRAIN, 0), [(widen, 1)], [])
-            round_of(banks_of("err", TRAIN, 1) + first_act[:1], [(widen, 2), (widen, 3)], backs(TRAIN, [0], [0, 1]) + backs(TRAIN, [1], [0]))
-            for i in range(2, 8):
-                side_banks, side_products = sides[i - 2]
-                ahead = [(quantise_w, i - 3)] if i > 2 else []
-                if 2 < i < 7:
-                    widen(i + 1, slice(0, 1))
-                ahead = ([(sort_words, banks_of("err", TRAIN, i + 1)[0], "scalar")] if 5 <= i + 1 < 8 else []) + ahead
-                ahead += [(widen, i + 1, slice(1, 2))] if 2 < i < 7 else []
-                ahead += sorts(sides[i - 1][0]) + [(lay_w, i - 2, "gpsimd")]
-                ahead += [(lay_w, 6, "scalar")] if i == 7 else []
-                round_of(
-                    banks_of("err", TRAIN, i) + side_banks + [("d", TRAIN, i - 2, 0)],
-                    ahead,
-                    backs(TRAIN, [i - 1], [0, 1] if i > 2 else [1]) + side_products,
-                )
-            turns = [("d", QUERY, 0, 0)] + banks_of("act", TRAIN, 2) + [("d", TRAIN, 6, 0)]
-            for key in turns:
-                turn(key)
-            quantise_w(6)
-            lay_w(7, "vector")
-            round_of([], [(quantise_w, 5), (quantise_w, 7)] + [(quantise, key) for key in turns] + sorts(banks_of("act", TRAIN, 3)), backs(TRAIN, [7], [0, 1]) + backs(QUERY, range(4), [1]))
-            last_act = banks_of("act", TRAIN, 3)
-            round_of([("d", QUERY, 1, 0), ("d", TRAIN, 7, 0), ("d", QUERY, 0, 1), last_act[0], ("d", QUERY, 1, 1)] + last_act[1:], [], [(gram_act, 4), (gram_act, 5)])
-            for i in range(8):
-                if i in (4, 6):
-                    gram_act(4 + i // 2)
-                finish(i, slice(0, N))
-                store(slice(i, i + 1), slice(0, N))
+            write_out([sync, vector, scalar, gpsimd, tensor])

@@ -21,8 +21,8 @@ ADD = mybir.AluOpType.add
 
 TRAIN, QUERY = "train", "query"
 RINGS = {
-    "err_bytes": (3, 2), "act_raw": (3, 3), "w_raw": (3, 1), "slope_train": (2, 4), "err_query": (2, 4),
-    "wide": (3, 1), "sorted": (9, 1), "k_first": (10, 1), "d": (8, 1), "w_laid": (1, 1), "w_laid_gpsimd": (1, 1),
+    "err_bytes": (3, 2), "act_raw": (3, 3), "w_raw": (3, 1), "slope_train": (3, 4), "err_query": (2, 4),
+    "wide": (3, 1), "sorted": (9, 1), "k_first": (10, 1), "d": (11, 1), "w_laid": (1, 1), "w_laid0": (1, 1), "w_laid1": (1, 1),
     "et_codes": (3, 2), "at_codes": (2, 2),
 }
 
@@ -73,7 +73,7 @@ def tile_gradient_inner_products_s11_kernel(
 
         ident = kept("ident", [P, P], F32)
         v_planes = kept("v_planes", [P, 4, F], U8)
-        v_codes = [kept("v_codes%d" % b, [P, 2, 2 * F], U8) for b in range(2)]
+        v_codes = [kept("v_codes%d" % g, [P, 2 * F], U8) for g in range(4)]
         scale = kept("scale", [P, 4, 4], F32)
         w_codes = kept("w_codes", [P, 2, 4, N], U32)
         w_planes = kept("w_planes", [P, 2, 4, N], U8)
@@ -91,10 +91,11 @@ def tile_gradient_inner_products_s11_kernel(
             pattern = "(p j) k -> p j k" if side == TRAIN else "(j p) k -> p j k"
             return src[256 * pair : 256 * (pair + 1), :].rearrange(pattern, j=2)
 
-        def load_first_bytes(b):
-            raw = kept("first_bytes%d" % b, [P, 1024], U8)
-            nc.sync.dma_start(out=raw[:], in_=rows(err_train_bytes, TRAIN, 0)[:, 0, 1024 * b : 1024 * (b + 1)])
-            t["bytes", 0, b] = raw[:]
+        def load_first_bytes(g0, g1):
+            raw = kept("first_bytes%d" % g0, [P, PASS * (g1 - g0)], U8)
+            nc.sync.dma_start(out=raw[:], in_=rows(err_train_bytes, TRAIN, 0)[:, 0, PASS * g0 : PASS * g1])
+            for g in range(g0, g1):
+                t["bytes", 0, g] = (raw, PASS * (g - g0))
             return True
 
         def load_bytes(i):
@@ -102,8 +103,8 @@ def tile_gradient_inner_products_s11_kernel(
                 return False
             raw = ring("err_bytes", ("bytes", i), [P, C], U8)
             nc.sync.dma_start(out=raw[:], in_=rows(err_train_bytes, TRAIN, i // 2)[:, i % 2, :])
-            for b in range(2):
-                t["bytes", i, b] = raw[:, 1024 * b : 1024 * (b + 1)]
+            for g in range(4):
+                t["bytes", i, g] = (raw, PASS * g)
             return True
 
         def load_scale():
@@ -119,9 +120,9 @@ def tile_gradient_inner_products_s11_kernel(
                 )
             return True
 
-        def load_v(b):
-            nc.sync.dma_start(out=v_codes[b][:], in_=v_words[2 * b : 2 * b + 2].rearrange("g p b -> p g b"))
-            t["v", b] = True
+        def load_v(g):
+            nc.sync.dma_start(out=v_codes[g][:], in_=v_words[g])
+            t["v", g] = True
             return True
 
         def load_act(side, pair):
@@ -152,22 +153,28 @@ def tile_gradient_inner_products_s11_kernel(
                     t["rows", ("err", QUERY, 2 * pair + j, b)] = raw[:, j, 1024 * b : 1024 * (b + 1)].bitcast(F32).rearrange("p (a m) -> p a m", a=2)
             return True
 
-        def load_slope(side, pair):
+        def load_slope(side, tiles):
             if side == TRAIN and not room("slope_train"):
                 return False
-            raw = ring("slope_train", ("slope", side, pair), [P, 2, F], BF16) if side == TRAIN else kept("slope_query%d" % pair, [P, 2, F], BF16)
-            nc.sync.dma_start(out=raw[:], in_=rows(slope_train if side == TRAIN else slope_query, side, pair))
-            for j in range(2):
-                t["slope", side, 2 * pair + j] = raw[:, j, :]
+            pair, first = divmod(tiles[0], 2)
+            shape = [P, len(tiles), F]
+            raw = ring("slope_train", ("slope", side, tiles[0]), shape, BF16) if side == TRAIN else kept("slope_query%d" % pair, shape, BF16)
+            if side == TRAIN:
+                readers["slope", side, tiles[0]][1] = 2 * len(tiles)
+            nc.sync.dma_start(out=raw[:], in_=rows(slope_train if side == TRAIN else slope_query, side, pair)[:, first : first + len(tiles), :])
+            for j, i in enumerate(tiles):
+                t["slope", side, i] = raw[:, j, :]
+                t["slope_owner", side, i] = ("slope", side, tiles[0])
             return True
 
         def widen(key):
-            kind, side, i, b = key
-            if not (there(("bytes", i, b)) and room("wide")):
+            kind, side, i, (g, n) = key
+            if not (there(("bytes", i, g)) and room("wide")):
                 return False
-            x = ring("wide", ("wide", key), [P, 1024], BF16)
-            nc.scalar.copy(out=x[:], in_=t["bytes", i, b].bitcast(FP8))
-            t["rows", key] = x[:].bitcast(F32).rearrange("p (a m) -> p a m", a=2)
+            x = ring("wide", ("wide", key), [P, PASS * n], BF16)
+            raw, k0 = t["bytes", i, g]
+            nc.scalar.copy(out=x[:], in_=raw[:, k0 : k0 + PASS * n].bitcast(FP8))
+            t["rows", key] = x[:].bitcast(F32).rearrange("p (a m) -> p a m", a=n)
             was_read(("bytes", i))
             return True
 
@@ -194,8 +201,9 @@ def tile_gradient_inner_products_s11_kernel(
                 sources = [("rows" if stepped else "sorted", key)]
             if not (there(*sources) and free_banks):
                 return False
-            turned = take_bank(key, [P, 2, 2 * P])
-            for a in range(2):
+            n = g[1] if key[:2] == ("err", TRAIN) else 2
+            turned = take_bank(key, [P, 2, n * P])
+            for a in range(n):
                 for u in range(2):
                     if kind == "d":
                         src = t[sources[a]][:, u, :]
@@ -211,27 +219,29 @@ def tile_gradient_inner_products_s11_kernel(
             t["full", key] = True
             return True
 
-        def empty(key, engine="scalar"):
+        def empty(key, engine="scalar", name="k_first"):
             kind, side, i, g = key
-            if not (there(("full", key)) and room("k_first")):
+            if not (there(("full", key)) and room(name)):
                 return False
             turned = give_bank(key)
-            x = ring("k_first", ("k_first", key), [P, 2 * P, 4], BF16)
+            g, n = g if key[:2] == ("err", TRAIN) else (g, 2)
+            x = ring(name, ("k_first", key), [P, n * P, 4], BF16)
             t["k_first", key] = x
             if (kind, side) != ("err", TRAIN):
                 copy = nc.scalar.copy if engine == "scalar" else nc.vector.tensor_copy
                 copy(out=x[:].bitcast(F32), in_=turned[:].rearrange("p u r -> p r u"))
             else:
                 nc.vector.tensor_tensor(
-                    out=x[:].rearrange("p (a m) (u e) -> p a m u e", a=2, u=2),
-                    in0=turned[:].bitcast(BF16).rearrange("p u (a m e) -> p a m u e", a=2, e=2),
-                    in1=scale[:, 2 * g : 2 * g + 2, :].rearrange("p a (u e) -> p a u e", u=2).unsqueeze(2).to_broadcast([P, 2, P, 2, 2]),
+                    out=x[:].rearrange("p (a m) (u e) -> p a m u e", a=n, u=2),
+                    in0=turned[:].bitcast(BF16).rearrange("p u (a m e) -> p a m u e", a=n, e=2),
+                    in1=scale[:, g : g + n, :].rearrange("p a (u e) -> p a u e", u=2).unsqueeze(2).to_broadcast([P, n, P, 2, 2]),
                     op=MULT,
                 )
             return True
 
         def quantise(key):
             kind, side, i, g = key
+            g, n = g if key[:2] == ("err", TRAIN) else (2 * g, 2) if kind == "err" else (g, 1)
             opens = side == TRAIN and g == 0 and kind != "d"
             name = "at_codes" if kind == "act" else "et_codes"
             if not there(("k_first", key)) or (opens and not room(name)):
@@ -249,8 +259,8 @@ def tile_gradient_inner_products_s11_kernel(
                 elif opens:
                     t["codes", side, i] = ring("et_codes", ("codes", side, i), [P, 4, P], U32)
                     t["planes", side, i] = work.tile([P, 4, P], U8, tag="et_planes", name="et_planes", bufs=RINGS[name][0], align_bytes=64)
-                codes = t["codes", side, i][:, 2 * g : 2 * g + 2, :].rearrange("p g r -> p (g r)")
-                planes = t["planes", side, i][:, 2 * g : 2 * g + 2, :].rearrange("p g r -> p (g r)")
+                codes = t["codes", side, i][:, g : g + n, :].rearrange("p g r -> p (g r)")
+                planes = t["planes", side, i][:, g : g + n, :].rearrange("p g r -> p (g r)")
             elif side == QUERY:
                 codes, planes = dq_codes[:, g, 256 * i : 256 * (i + 1)], dq_planes[:, g, 256 * i : 256 * (i + 1)]
             else:
@@ -268,13 +278,13 @@ def tile_gradient_inner_products_s11_kernel(
 
         def back(side, i, h, part=slice(0, 4)):
             key = ("back", side, i, h)
-            needs = [("mx", ("err", side, i, g // 2)) for g in range(4)[part]]
-            needs += [("v", g // 2) if side == TRAIN else ("mx", ("w", 4 * h + g)) for g in range(4)[part]]
+            needs = [("mx", key) for key in (et(i) if side == TRAIN else eq(i)) if side == QUERY or key[3][0] < part.stop]
+            needs += [("v", g) if side == TRAIN else ("mx", ("w", 4 * h + g)) for g in range(4)[part]]
             if not there(*needs) or (part.start == 0 and not free_banks):
                 return False
             acc = take_bank(key, [P, N]) if part.start == 0 else t["bank", key]
             if side == TRAIN:
-                moving = [(v_codes[g // 2][:, g % 2, F * h : F * (h + 1)].bitcast(FP4X4), v_planes[:, g, N * h : N * (h + 1)]) for g in range(4)]
+                moving = [(v_codes[g][:, F * h : F * (h + 1)].bitcast(FP4X4), v_planes[:, g, N * h : N * (h + 1)]) for g in range(4)]
             else:
                 moving = [(w_codes[:, h, g, :].bitcast(FP8X4), w_planes[:, h, g, :]) for g in range(4)]
             accumulate(acc[:], [(t["codes", side, i][:, g, :], t["planes", side, i][:, g, :]) + moving[g] for g in range(4)], part)
@@ -294,7 +304,7 @@ def tile_gradient_inner_products_s11_kernel(
                 in1=t["slope", side, i][:, N * h : N * (h + 1)].rearrange("p (m u e) -> p u m e", u=2, e=2),
                 op=MULT,
             )
-            was_read(("slope", side, i // 2))
+            was_read(t["slope_owner", side, i])
             t["d", side, i, h] = d[:].rearrange("p u m e -> p u (m e)").bitcast(F32)
             return True
 
@@ -318,34 +328,33 @@ def tile_gradient_inner_products_s11_kernel(
             t["gram", i] = True
             return True
 
-        def gram_err(i, part=slice(0, 2)):
-            key = ("gram_err", i)
+        def gram_err(i, part=slice(0, 2), cols=slice(0, N)):
+            key = ("gram_err", i, cols.start)
             needs = dt(i) + [k for g in range(2)[part] for k in dq(0, g) + dq(1, g)]
             if not there(*[("mx", k) for k in needs]) or (part.start == 0 and not free_banks):
                 return False
-            acc = take_bank(key, [P, N]) if part.start == 0 else t["bank", key]
-            accumulate(acc[:], [(dt_codes[:, i, g, :], dt_planes[:, i, g, :], dq_codes[:, g, :].bitcast(FP8X4), dq_planes[:, g, :]) for g in range(2)], part)
+            acc = take_bank(key, [P, cols.stop - cols.start]) if part.start == 0 else t["bank", key]
+            accumulate(acc[:], [(dt_codes[:, i, g, :], dt_planes[:, i, g, :], dq_codes[:, g, cols].bitcast(FP8X4), dq_planes[:, g, cols]) for g in range(2)], part)
             if part.stop == 2:
                 t["full", key] = True
             return True
 
-        def finish(i):
-            key = ("gram_err", i)
+        def finish(i, cols=slice(0, N)):
+            key = ("gram_err", i, cols.start)
             if not there(("full", key), ("gram", i)):
                 return False
-            nc.vector.tensor_tensor(out=gram[:, i, :], in0=give_bank(key)[:], in1=gram[:, i, :], op=MULT)
-            t["done", i] = True
+            nc.vector.tensor_tensor(out=gram[:, i, cols], in0=give_bank(key)[:], in1=gram[:, i, cols], op=MULT)
+            t["done", i, cols.start] = True
             return True
 
-        def store(i):
-            if not there(("done", i)):
+        def store(i, cols=slice(0, N)):
+            if not there(("done", i, cols.start)):
                 return False
-            nc.sync.dma_start(out=rows(out, TRAIN, i // 2)[:, i % 2, :], in_=gram[:, i, :])
+            nc.sync.dma_start(out=rows(out, TRAIN, i // 2)[:, i % 2, cols], in_=gram[:, i, cols])
             return True
 
-        def lay_w(piece, engine="gpsimd"):
-            name = "w_laid_gpsimd" if engine == "gpsimd" else "w_laid"
-            if not (there(("w_raw", piece)) and room(name)):
+        def lay_w(piece, engine="gpsimd", name="w_laid", behind=()):
+            if not (there(("w_raw", piece), *[("mx", key) for key in behind]) and room(name)):
                 return False
             x = ring(name, ("w_laid", piece), [P, N, 4], BF16)
             raw = t["w_raw", piece]
@@ -368,7 +377,7 @@ def tile_gradient_inner_products_s11_kernel(
             return True
 
         def et(i):
-            return [("err", TRAIN, i, b) for b in range(2)]
+            return [("err", TRAIN, i, unit) for unit in ([(0, 1), (1, 1), (2, 2)] if i == 0 else [(0, 2), (2, 2)])]
 
         def eq(*tiles):
             return [("err", QUERY, i, b) for i in tiles for b in range(2)]
@@ -414,34 +423,39 @@ def tile_gradient_inner_products_s11_kernel(
         def quants(i, keys):
             return each(quantise, et(i)[:1] + keys[:1] + et(i)[1:] + keys[1:])
 
-        sync = [(load_first_bytes, 0), (load_scale,), (load_first_bytes, 1), (load_bytes, 1), (load_v_scales,), (load_bytes, 2), (load_v, 0), (load_v, 1), (load_bytes, 3), (load_slope, TRAIN, 0),
-            (load_bytes, 4), (load_w, 0), (load_act, QUERY, 0), (load_act, QUERY, 1), (load_act, TRAIN, 0), (load_slope, TRAIN, 1), (load_w, 1), (load_bytes, 5), (load_act, TRAIN, 1),
-            (load_w, 2), (load_slope, TRAIN, 2), (load_bytes, 6), (load_act, TRAIN, 2), (load_w, 3), (load_bytes, 7), (load_err_query, 0), (load_slope, QUERY, 0), (load_w, 4), (load_err_query, 1), (load_slope, TRAIN, 3),
-            (load_w, 5), (load_slope, QUERY, 1), (load_w, 6), (load_act, TRAIN, 3), (load_w, 7)] + each(store, range(8))
-        tensor = each(turn, et(0) + et(1), True) + [(back, TRAIN, 0, 0, lo), (back, TRAIN, 0, 1, lo)] + each(turn, et(2)) + [(back, TRAIN, 0, 0, hi), (back, TRAIN, 0, 1, hi)] + both(back, TRAIN, [1])
-        vector = each(empty, et(0)) + each(quantise, et(0)[:1]) + each(empty, et(1)[:1]) + each(quantise, et(0)[1:]) + each(empty, et(1)[1:]) + each(quantise, et(1))
+        sync = [(load_first_bytes, 0, 1), (load_scale,), (load_first_bytes, 1, 4), (load_bytes, 1), (load_v_scales,), (load_v, 0), (load_bytes, 2), (load_v, 1), (load_v, 2), (load_v, 3), (load_bytes, 3), (load_slope, TRAIN, [0, 1]),
+            (load_w, 0), (load_bytes, 4), (load_act, QUERY, 0), (load_act, QUERY, 1), (load_act, TRAIN, 0), (load_slope, TRAIN, [2]), (load_w, 1), (load_bytes, 5), (load_act, TRAIN, 1), (load_slope, TRAIN, [3]),
+            (load_w, 2), (load_slope, TRAIN, [4, 5]), (load_bytes, 6), (load_err_query, 0), (load_w, 3), (load_bytes, 7), (load_slope, QUERY, [0, 1]), (load_err_query, 1), (load_w, 4), (load_w, 6), (load_slope, QUERY, [2, 3]), (load_act, TRAIN, 2), (load_slope, TRAIN, [6, 7]),
+            (load_w, 5), (load_w, 7), (load_act, TRAIN, 3)]
+        left, right = slice(0, 256), slice(256, N)
+        sync += each(store, range(7)) + [(store, 7, left), (store, 7, right)]
+        tensor = each(turn, et(0) + et(1), True) + [(back, TRAIN, 0, h, slice(g, g + 1)) for g in range(2) for h in range(2)] + each(turn, et(2)) + [(back, TRAIN, 0, 0, hi), (back, TRAIN, 0, 1, hi)] + both(back, TRAIN, [1])
+        vector = each(empty, et(0)[:2]) + each(quantise, et(0)[:1]) + each(empty, et(0)[2:]) + each(quantise, et(0)[1:2]) + each(empty, et(1)[:1]) + each(quantise, et(0)[2:]) + each(empty, et(1)[1:]) + each(quantise, et(1))
         vector += each(empty, et(2)) + both(times_slope, TRAIN, [0, 1])
         scalar = each(widen, et(0) + et(1)) + prep(2) + prep(3) + prep(4)
-        gpsimd = each(lay_w, range(6))
-        tensor += each(turn, et(3) + dt(0)) + each(turn, aq(0), True) + both(back, TRAIN, [2], [0]) + each(turn, aq(1), True) + both(back, TRAIN, [2], [1])
-        vector += each(empty, et(3)[:1]) + each(quantise, et(2)) + each(empty, et(3)[1:]) + each(quantise, et(3)[:1] + dt(0) + aq(0) + et(3)[1:] + aq(1)) + [(quantise_w, 0)] + both(times_slope, TRAIN, [2])
-        scalar += each(empty, dt(0) + aq(0) + aq(1)) + sorts(at(0))
-        for i in (4, 5, 6):
+        held = ["w_laid0", "w_laid0", "w_laid0", "w_laid0", "w_laid1", "w_laid1"]
+        gpsimd = [(lay_w, piece, "gpsimd", held[piece], dt(1) if piece == 4 else []) for piece in range(6)]
+        tensor += each(turn, et(3)) + each(turn, aq(0)[:2], True) + each(turn, aq(0)[2:]) + both(back, TRAIN, [2], [0]) + each(turn, aq(1)[:1], True) + each(turn, aq(1)[1:]) + both(back, TRAIN, [2], [1])
+        vector += each(empty, et(3)[:1]) + each(quantise, et(2)) + each(empty, et(3)[1:]) + each(quantise, et(3)[:1] + aq(0) + et(3)[1:]) + [(quantise_w, 0)] + both(times_slope, TRAIN, [2])
+        scalar += sorts(aq(0)[2:]) + each(empty, aq(0)) + sorts(aq(1)[1:]) + each(empty, aq(1)) + sorts(at(0))
+        for i in (4, 5):
             pair = i - 4
-            tensor += each(turn, et(i) + at(pair) + dt(i - 3)) + both(back, TRAIN, [i - 1]) + each(gram_act, [2 * pair, 2 * pair + 1])
-            vector += each(empty, et(i)) + each(quantise, et(i)[:1] + at(pair) + et(i)[1:] + dt(i - 3)) + each(sort_words, et(i + 1), "vector") + [(quantise_w, i - 3)] + both(times_slope, TRAIN, [i - 1])
-            scalar += each(empty, at(pair) + dt(i - 3)) + each(widen, et(i + 1)) + sorts(at(pair + 1) if i < 6 else eq(0, 1)) + each(keep_gram, [2 * pair, 2 * pair + 1])
-        tensor += each(turn, et(7) + eq(0, 1) + dt(4)) + both(back, TRAIN, [6]) + both(back, QUERY, [0, 1], [0])
-        vector += each(empty, et(7)) + each(quantise, et(7)[:1] + eq(0, 1) + dt(4) + et(7)[1:]) + [(quantise_w, 4)] + both(times_slope, TRAIN, [6]) + both(times_slope, QUERY, [0, 1], [0])
-        scalar += each(empty, eq(0, 1) + dt(4)) + sorts(eq(2, 3)) + [(lay_w, 6, "scalar")]
-        tensor += each(turn, eq(2, 3) + dt(5, 6) + dq(0, 0)) + both(back, TRAIN, [7]) + both(back, QUERY, [2, 3], [0])
-        vector += each(empty, eq(2), "vector") + [(quantise_w, 6)] + each(quantise, eq(2, 3)) + [(quantise_w, 5)] + each(quantise, dt(5, 6) + dq(0, 0)) + both(times_slope, TRAIN, [7]) + [(quantise_w, 7)] + both(times_slope, QUERY, [2, 3], [0])
-        scalar += each(empty, eq(3) + dt(5, 6) + dq(0, 0)) + [(lay_w, 7, "scalar")] + sorts(at(3))
-        tensor += both(back, QUERY, range(4), [1]) + each(turn, dq(0, 1) + dt(7) + dq(1, 0) + at(3)[:1] + dq(1, 1) + at(3)[1:])
-        vector += both(times_slope, QUERY, range(4), [1]) + each(quantise, dq(0, 1) + dq(1, 0) + dq(1, 1) + dt(7) + at(3)) + each(finish, range(8))
-        scalar += each(empty, dq(0, 1) + dq(1, 0) + dq(1, 1) + dt(7) + at(3)) + each(keep_gram, [6, 7])
-        first, second = slice(0, 1), slice(1, 2)
-        tensor += each(gram_err, range(4)) + [(gram_act, 6), (gram_err, 4), (gram_err, 5), (gram_act, 7), (gram_err, 6), (gram_err, 7)]
+            tensor += each(turn, et(i) + at(pair) + (dt(0) if i == 4 else [])) + both(back, TRAIN, [i - 1]) + each(gram_act, [2 * pair, 2 * pair + 1])
+            vector += each(empty, et(i)) + each(quantise, (aq(1) if i == 4 else []) + at(pair) + et(i) + (dt(0) if i == 4 else [])) + [(quantise_w, i - 3)] + both(times_slope, TRAIN, [i - 1]) + [(keep_gram, 2 * pair, "vector")]
+            scalar += each(empty, at(pair) + (dt(0) if i == 4 else [])) + each(widen, et(i + 1)) + sorts(et(i + 1) + (at(pair + 1) if i < 5 else eq(0, 1))) + each(keep_gram, [2 * pair + 1])
+        tensor += each(turn, et(6) + eq(0, 1) + dt(1)) + both(back, TRAIN, [5]) + both(back, QUERY, [0, 1], [0])
+        vector += each(empty, et(6)) + [(quantise_w, 3)] + each(quantise, eq(0, 1) + et(6)) + each(sort_words, et(7)[:1], "vector") + each(quantise, dt(1)) + both(times_slope, TRAIN, [5]) + both(times_slope, QUERY, [0, 1], [0])
+        scalar += each(empty, eq(0, 1)) + each(empty, dt(1), "scalar", "w_laid1") + each(widen, et(7)) + sorts(et(7)[1:] + eq(2, 3))
+        tensor += each(turn, et(7) + eq(2, 3) + dt(2) + dq(0, 0)) + both(back, TRAIN, [6]) + both(back, QUERY, [2, 3], [0])
+        vector += each(empty, et(7)) + each(quantise, eq(2, 3) + et(7) + dt(2) + dq(0, 0)) + [(quantise_w, 4)] + both(times_slope, TRAIN, [6]) + both(times_slope, QUERY, [2, 3], [0])
+        scalar += each(empty, eq(2, 3) + dt(2) + dq(0, 0)) + sorts(at(2)) + [(lay_w, 6, "scalar")]
+        three, last = slice(0, 3), slice(3, 4)
+        tensor += each(turn, at(2) + dt(3, 4) + dq(1, 0)) + both(back, TRAIN, [7], [0]) + each(gram_act, [4, 5]) + [(back, QUERY, i, 1, three) for i in range(3)] + [(back, QUERY, i, 1, last) for i in range(3)] + [(back, QUERY, 3, 1)]
+        vector += each(empty, at(2), "vector") + each(quantise, at(2)) + [(quantise_w, 6), (quantise_w, 5)] + each(quantise, dt(3, 4) + dq(1, 0)) + both(times_slope, TRAIN, [7], [0]) + [(quantise_w, 7)] + both(times_slope, QUERY, range(4), [1])
+        scalar += each(empty, dt(3, 4) + dq(1, 0)) + [(lay_w, 7, "scalar")] + each(keep_gram, [4, 5]) + sorts(at(3))
+        tensor += each(turn, dq(0, 1) + dt(5) + at(3)[:2] + dq(1, 1) + at(3)[2:]) + both(back, TRAIN, [7], [1]) + each(gram_err, [0, 1]) + each(turn, dt(6, 7)) + [(gram_err, 2), (gram_act, 6), (gram_err, 3), (gram_err, 4), (gram_err, 5), (gram_act, 7), (gram_err, 6), (gram_err, 7, slice(0, 2), left), (gram_err, 7, slice(0, 2), right)]
+        vector += each(quantise, dq(0, 1) + dq(1, 1)) + both(times_slope, TRAIN, [7], [1]) + each(quantise, at(3) + dt(5)) + each(finish, [0, 1, 2]) + each(quantise, dt(6, 7)) + each(finish, range(3, 7)) + [(finish, 7, left), (finish, 7, right)]
+        scalar += each(empty, dq(0, 1) + dq(1, 1) + at(3) + dt(5, 6, 7)) + each(keep_gram, [6, 7])
         with tc.manual_schedule():
             make_identity(nc, ident[:])
             nc.vector.memset(v_planes[:].rearrange("p g n -> p (g n)").bitcast(I32), 0)

@@ -21,8 +21,8 @@ ADD = mybir.AluOpType.add
 
 TRAIN, QUERY = "train", "query"
 RINGS = {
-    "err_bytes": (3, 2), "act_raw": (3, 3), "w_raw": (3, 1), "slope_train": (3, 4), "err_query": (2, 4),
-    "wide": (3, 1), "sorted": (9, 1), "k_first": (10, 1), "d": (11, 1), "w_laid": (1, 1), "w_laid0": (1, 1), "w_laid1": (1, 1),
+    "err_bytes": (3, 2), "act_raw": (3, 3), "w_raw": (3, 1), "slope_train": (3, 4), "err_query": (3, 2),
+    "wide": (2, 1), "sorted1": (9, 1), "k_first1": (3, 1), "k_first2": (4, 1), "d": (11, 1), "w_laid": (1, 1), "w_laid0": (1, 1), "w_laid1": (1, 1),
     "et_codes": (3, 2), "at_codes": (2, 2),
 }
 
@@ -39,6 +39,7 @@ def tile_gradient_inner_products_s11_kernel(
         readers = {}
         taken = {name: 0 for name in RINGS}
         free_banks = list(range(8))
+        groups = {}
 
         def kept(name, shape, dtype):
             return keep.tile(shape, dtype, name=name, align_bytes=64)
@@ -46,9 +47,9 @@ def tile_gradient_inner_products_s11_kernel(
         def room(name):
             return taken[name] < RINGS[name][0]
 
-        def ring(name, owner, shape, dtype):
+        def ring(name, owner, shape, dtype, count=None):
             taken[name] += 1
-            readers[owner] = [name, RINGS[name][1]]
+            readers[owner] = [name, count or RINGS[name][1]]
             return work.tile(shape, dtype, tag=name, name=name, bufs=RINGS[name][0], align_bytes=64)
 
         def was_read(owner):
@@ -131,7 +132,8 @@ def tile_gradient_inner_products_s11_kernel(
             raw = ring("act_raw", ("raw", "act", side, pair), [P, 2, K], BF16)
             nc.sync.dma_start(out=raw[:], in_=rows(act_train if side == TRAIN else act_query, side, pair))
             for g in range(3):
-                t["rows", ("act", side, pair, g)] = raw[:, :, PASS * g : PASS * (g + 1)].bitcast(F32)
+                t["rows", (("act", side, pair, g),)] = raw[:, :, PASS * g : PASS * (g + 1)].bitcast(F32)
+                t["owner", ("act", side, pair, g)] = ("raw", "act", side, pair)
             return True
 
         def load_w(piece):
@@ -143,14 +145,16 @@ def tile_gradient_inner_products_s11_kernel(
             t["w_raw", piece] = raw
             return True
 
-        def load_err_query(pair):
+        def load_err_query(i):
             if not room("err_query"):
                 return False
-            raw = ring("err_query", ("raw", "err", QUERY, pair), [P, 2, C], BF16)
-            nc.sync.dma_start(out=raw[:], in_=rows(err_query, QUERY, pair))
-            for j in range(2):
-                for b in range(2):
-                    t["rows", ("err", QUERY, 2 * pair + j, b)] = raw[:, j, 1024 * b : 1024 * (b + 1)].bitcast(F32).rearrange("p (a m) -> p a m", a=2)
+            raw = ring("err_query", ("raw", "err", QUERY, i), [P, C], BF16)
+            nc.sync.dma_start(out=raw[:], in_=err_query[P * i : P * (i + 1), :])
+            words = raw[:].bitcast(F32).rearrange("p (a m) -> p a m", a=4)
+            t["rows", tuple(eq(i))] = words
+            for b, key in enumerate(eq(i)):
+                t["rows", (key,)] = words[:, 2 * b : 2 * b + 2, :]
+                t["owner", key] = ("raw", "err", QUERY, i)
             return True
 
         def load_slope(side, tiles):
@@ -167,30 +171,34 @@ def tile_gradient_inner_products_s11_kernel(
                 t["slope_owner", side, i] = ("slope", side, tiles[0])
             return True
 
-        def widen(key):
-            kind, side, i, (g, n) = key
-            if not (there(("bytes", i, g)) and room("wide")):
+        def widen(*keys):
+            kind, side, i, (g, n) = keys[0]
+            n = sum(key[3][1] for key in keys)
+            if not (there(("bytes", i, g)) and (g > 0 or room("wide"))):
                 return False
-            x = ring("wide", ("wide", key), [P, PASS * n], BF16)
+            if g == 0:
+                t["wide", i] = ring("wide", ("wide", i), [P, C], BF16, len(et(i)))
+            x = t["wide", i][:, PASS * g : PASS * (g + n)]
             raw, k0 = t["bytes", i, g]
-            nc.scalar.copy(out=x[:], in_=raw[:, k0 : k0 + PASS * n].bitcast(FP8))
-            t["rows", key] = x[:].bitcast(F32).rearrange("p (a m) -> p a m", a=n)
-            was_read(("bytes", i))
+            nc.scalar.copy(out=x, in_=raw[:, k0 : k0 + PASS * n].bitcast(FP8))
+            words = x.bitcast(F32).rearrange("p (a m) -> p a m", a=n)
+            t["rows", keys] = words
+            for key in keys:
+                t["rows", (key,)] = words[:, key[3][0] - g : key[3][0] - g + key[3][1], :]
+                t["owner", key] = ("wide", i)
+                was_read(("bytes", i))
             return True
 
-        def rows_read(key):
-            kind, side, i, g = key
-            was_read(("wide", key))
-            was_read(("raw", kind, side, i if kind == "act" else i // 2))
-
-        def sort_words(key, engine="scalar"):
-            if not (there(("rows", key)) and room("sorted")):
+        def sort_words(keys, engine="scalar"):
+            if not (there(("rows", keys)) and room("sorted%d" % len(keys))):
                 return False
-            x = ring("sorted", ("sorted", key), [P, 2, 2, P], F32)
+            x = ring("sorted%d" % len(keys), ("sorted", keys[0]), [P, 2 * len(keys), 2, P], F32, len(keys))
             copy = nc.scalar.copy if engine == "scalar" else nc.vector.tensor_copy
-            copy(out=x[:], in_=t["rows", key].rearrange("p a (m u) -> p a u m", u=2))
-            t["sorted", key] = x
-            rows_read(key)
+            copy(out=x[:], in_=t["rows", keys].rearrange("p a (m u) -> p a u m", u=2))
+            for n, key in enumerate(keys):
+                t["sorted", key] = x[:, 2 * n : 2 * n + 2]
+                was_read(t["owner", key])
+                t["owner", key] = ("sorted", keys[0])
             return True
 
         def turn(key, stepped=False):
@@ -198,7 +206,7 @@ def tile_gradient_inner_products_s11_kernel(
             if kind == "d":
                 sources = [("d", side, i, a) if side == TRAIN else ("d", side, 2 * i + a, g) for a in range(2)]
             else:
-                sources = [("rows" if stepped else "sorted", key)]
+                sources = [("rows", (key,)) if stepped else ("sorted", key)]
             if not (there(*sources) and free_banks):
                 return False
             n = g[1] if key[:2] == ("err", TRAIN) else 2
@@ -208,31 +216,33 @@ def tile_gradient_inner_products_s11_kernel(
                     if kind == "d":
                         src = t[sources[a]][:, u, :]
                     elif stepped:
-                        src = t["rows", key][:, a, u : 256 : 2]
+                        src = t["rows", (key,)][:, a, u : 256 : 2]
                     else:
                         src = t["sorted", key][:, a, u, :]
                     nc.tensor.transpose(turned[:, u, P * a : P * (a + 1)], src, ident[:])
-            for source in sources:
+            for source in sources if kind == "d" else [t["owner", key]]:
                 was_read(source)
-            if stepped:
-                rows_read(key)
             t["full", key] = True
             return True
 
         def empty(key, engine="scalar", name="k_first"):
             kind, side, i, g = key
-            if not (there(("full", key)) and room(name)):
+            group = groups[key]
+            name = name if name != "k_first" else "k_first%d" % len(group)
+            if not (there(("full", key)) and (("k_first", group) in t or room(name))):
                 return False
             turned = give_bank(key)
             g, n = g if key[:2] == ("err", TRAIN) else (g, 2)
-            x = ring(name, ("k_first", key), [P, n * P, 4], BF16)
-            t["k_first", key] = x
+            if ("k_first", group) not in t:
+                t["k_first", group] = ring(name, ("k_first", group), [P, len(group), n * P, 4], BF16, 1)
+            x = t["k_first", group][:, group.index(key)]
+            t["laid", key] = True
             if (kind, side) != ("err", TRAIN):
                 copy = nc.scalar.copy if engine == "scalar" else nc.vector.tensor_copy
-                copy(out=x[:].bitcast(F32), in_=turned[:].rearrange("p u r -> p r u"))
+                copy(out=x.bitcast(F32), in_=turned[:].rearrange("p u r -> p r u"))
             else:
                 nc.vector.tensor_tensor(
-                    out=x[:].rearrange("p (a m) (u e) -> p a m u e", a=n, u=2),
+                    out=x.rearrange("p (a m) (u e) -> p a m u e", a=n, u=2),
                     in0=turned[:].bitcast(BF16).rearrange("p u (a m e) -> p a m u e", a=n, e=2),
                     in1=scale[:, g : g + n, :].rearrange("p a (u e) -> p a u e", u=2).unsqueeze(2).to_broadcast([P, n, P, 2, 2]),
                     op=MULT,
@@ -241,33 +251,29 @@ def tile_gradient_inner_products_s11_kernel(
 
         def quantise(key):
             kind, side, i, g = key
-            g, n = g if key[:2] == ("err", TRAIN) else (2 * g, 2) if kind == "err" else (g, 1)
+            group = groups[key]
+            n = len(group)
+            g, n = (g[0], n * g[1]) if key[:2] == ("err", TRAIN) else (2 * g, 2 * n) if kind == "err" else (g, n)
             opens = side == TRAIN and g == 0 and kind != "d"
             name = "at_codes" if kind == "act" else "et_codes"
-            if not there(("k_first", key)) or (opens and not room(name)):
+            if not there(*[("laid", k) for k in group]) or (opens and not room(name)):
                 return False
-            if (kind, side) == ("act", QUERY):
-                codes, planes = aq_codes[:, g, 256 * i : 256 * (i + 1)], aq_planes[:, g, 256 * i : 256 * (i + 1)]
-            elif kind == "act":
-                if opens:
-                    t["at_codes", i] = ring("at_codes", ("at_codes", i), [P, 3, 2 * P], U32)
-                    t["at_planes", i] = work.tile([P, 3, 2 * P], U8, tag="at_planes", name="at_planes", bufs=RINGS[name][0], align_bytes=64)
-                codes, planes = t["at_codes", i][:, g, :], t["at_planes", i][:, g, :]
-            elif kind == "err":
-                if side == QUERY:
-                    t["codes", side, i], t["planes", side, i] = rq_codes[:, i], rq_planes[:, i]
-                elif opens:
-                    t["codes", side, i] = ring("et_codes", ("codes", side, i), [P, 4, P], U32)
-                    t["planes", side, i] = work.tile([P, 4, P], U8, tag="et_planes", name="et_planes", bufs=RINGS[name][0], align_bytes=64)
-                codes = t["codes", side, i][:, g : g + n, :].rearrange("p g r -> p (g r)")
-                planes = t["planes", side, i][:, g : g + n, :].rearrange("p g r -> p (g r)")
+            if opens:
+                shape = [P, 3, 2 * P] if kind == "act" else [P, 4, P]
+                t["codes", kind, side, i] = ring(name, ("codes", kind, side, i), shape, U32)
+                t["planes", kind, side, i] = work.tile(shape, U8, tag=name + "_planes", name=name + "_planes", bufs=RINGS[name][0], align_bytes=64)
+            if kind == "err" and side == QUERY:
+                t["codes", kind, side, i], t["planes", kind, side, i] = rq_codes[:, i], rq_planes[:, i]
+            if kind == "err" or key[:2] == ("act", TRAIN):
+                both_parts = [t[part, kind, side, i][:, g : g + n, :].rearrange("p g r -> p (g r)") for part in ("codes", "planes")]
             elif side == QUERY:
-                codes, planes = dq_codes[:, g, 256 * i : 256 * (i + 1)], dq_planes[:, g, 256 * i : 256 * (i + 1)]
+                both_parts = [x[:, g, 256 * i : 256 * (i + n)] for x in ((aq_codes, aq_planes) if kind == "act" else (dq_codes, dq_planes))]
             else:
-                codes, planes = dt_codes[:, i].rearrange("p g r -> p (g r)"), dt_planes[:, i].rearrange("p g r -> p (g r)")
-            nc.vector.quantize_mx(out=codes.bitcast(FP8X4), scales=planes, in_=t["k_first", key][:].rearrange("p r t -> p (r t)"))
-            was_read(("k_first", key))
-            t["mx", key] = True
+                both_parts = [x[:, i : i + n].rearrange("p i g r -> p (i g r)") for x in (dt_codes, dt_planes)]
+            nc.vector.quantize_mx(out=both_parts[0].bitcast(FP8X4), scales=both_parts[1], in_=t["k_first", group][:].rearrange("p b r t -> p (b r t)"))
+            was_read(("k_first", group))
+            for k in group:
+                t["mx", k] = True
             return True
 
         def accumulate(acc, operands, part=slice(0, 4)):
@@ -287,9 +293,9 @@ def tile_gradient_inner_products_s11_kernel(
                 moving = [(v_codes[g][:, F * h : F * (h + 1)].bitcast(FP4X4), v_planes[:, g, N * h : N * (h + 1)]) for g in range(4)]
             else:
                 moving = [(w_codes[:, h, g, :].bitcast(FP8X4), w_planes[:, h, g, :]) for g in range(4)]
-            accumulate(acc[:], [(t["codes", side, i][:, g, :], t["planes", side, i][:, g, :]) + moving[g] for g in range(4)], part)
+            accumulate(acc[:], [(t["codes", "err", side, i][:, g, :], t["planes", "err", side, i][:, g, :]) + moving[g] for g in range(4)], part)
             if part.stop == 4:
-                was_read(("codes", side, i))
+                was_read(("codes", "err", side, i))
                 t["full", key] = True
             return True
 
@@ -297,11 +303,11 @@ def tile_gradient_inner_products_s11_kernel(
             key = ("back", side, i, h)
             if not (there(("full", key), ("slope", side, i)) and room("d")):
                 return False
-            d = ring("d", ("d", side, i, h), [P, 2, P, 2], BF16)
+            d = ring("d", ("d", side, i, h), [P, 2, 256 // 16, 16], BF16)
             nc.vector.tensor_tensor(
                 out=d[:],
-                in0=give_bank(key)[:].rearrange("p (m u e) -> p u m e", u=2, e=2),
-                in1=t["slope", side, i][:, N * h : N * (h + 1)].rearrange("p (m u e) -> p u m e", u=2, e=2),
+                in0=give_bank(key)[:].rearrange("p (q u r) -> p u q r", u=2, r=16),
+                in1=t["slope", side, i][:, N * h : N * (h + 1)].rearrange("p (q u r) -> p u q r", u=2, r=16),
                 op=MULT,
             )
             was_read(t["slope_owner", side, i])
@@ -313,9 +319,9 @@ def tile_gradient_inner_products_s11_kernel(
             if not (there(*[("mx", k) for k in aq(0) + aq(1) + at(i // 2)]) and free_banks):
                 return False
             half = slice(P * (i % 2), P * (i % 2) + P)
-            codes, planes = t["at_codes", i // 2], t["at_planes", i // 2]
+            codes, planes = t["codes", "act", TRAIN, i // 2], t["planes", "act", TRAIN, i // 2]
             accumulate(take_bank(key, [P, N])[:], [(codes[:, g, half], planes[:, g, half], aq_codes[:, g, :].bitcast(FP8X4), aq_planes[:, g, :]) for g in range(3)])
-            was_read(("at_codes", i // 2))
+            was_read(("codes", "act", TRAIN, i // 2))
             t["full", key] = True
             return True
 
@@ -394,6 +400,17 @@ def tile_gradient_inner_products_s11_kernel(
         def dq(pair, g):
             return [("d", QUERY, pair, g)]
 
+        def joined(*lists):
+            heads = []
+            for keys in lists:
+                for key in keys:
+                    groups[key] = tuple(keys)
+                heads.append(keys[0])
+            return each(quantise, heads)
+
+        def apart(keys):
+            return joined(*[[key] for key in keys])
+
         def each(fn, keys, *more):
             return [(fn, key) + more for key in keys]
 
@@ -415,46 +432,49 @@ def tile_gradient_inner_products_s11_kernel(
         lo, hi = slice(0, 2), slice(2, 4)
 
         def prep(i):
-            return each(widen, et(i)) + each(sort_words, et(i))
+            return each(widen, et(i)) + sorts(et(i)[: 2 if i < 5 else 1])
+
+        def turn_err(i):
+            return [(turn, key, i >= 5 and b == 1) for b, key in enumerate(et(i))]
 
         def sorts(keys):
-            return each(sort_words, keys)
+            return [(sort_words, (key,)) for key in keys]
 
-        def quants(i, keys):
-            return each(quantise, et(i)[:1] + keys[:1] + et(i)[1:] + keys[1:])
+        def sorts_eq(*tiles):
+            return sorts(eq(*tiles))
 
         sync = [(load_first_bytes, 0, 1), (load_scale,), (load_first_bytes, 1, 4), (load_bytes, 1), (load_v_scales,), (load_v, 0), (load_bytes, 2), (load_v, 1), (load_v, 2), (load_v, 3), (load_bytes, 3), (load_slope, TRAIN, [0, 1]),
             (load_w, 0), (load_bytes, 4), (load_act, QUERY, 0), (load_act, QUERY, 1), (load_act, TRAIN, 0), (load_slope, TRAIN, [2]), (load_w, 1), (load_bytes, 5), (load_act, TRAIN, 1), (load_slope, TRAIN, [3]),
-            (load_w, 2), (load_slope, TRAIN, [4, 5]), (load_bytes, 6), (load_err_query, 0), (load_w, 3), (load_bytes, 7), (load_slope, QUERY, [0, 1]), (load_err_query, 1), (load_w, 4), (load_w, 6), (load_slope, QUERY, [2, 3]), (load_act, TRAIN, 2), (load_slope, TRAIN, [6, 7]),
+            (load_w, 2), (load_slope, TRAIN, [4, 5]), (load_bytes, 6), (load_err_query, 0), (load_err_query, 1), (load_w, 3), (load_bytes, 7), (load_slope, QUERY, [0, 1]), (load_err_query, 2), (load_err_query, 3), (load_w, 4), (load_w, 6), (load_slope, QUERY, [2, 3]), (load_act, TRAIN, 2), (load_slope, TRAIN, [6, 7]),
             (load_w, 5), (load_w, 7), (load_act, TRAIN, 3)]
         left, right = slice(0, 256), slice(256, N)
         sync += each(store, range(7)) + [(store, 7, left), (store, 7, right)]
         tensor = each(turn, et(0) + et(1), True) + [(back, TRAIN, 0, h, slice(g, g + 1)) for g in range(2) for h in range(2)] + each(turn, et(2)) + [(back, TRAIN, 0, 0, hi), (back, TRAIN, 0, 1, hi)] + both(back, TRAIN, [1])
-        vector = each(empty, et(0)[:2]) + each(quantise, et(0)[:1]) + each(empty, et(0)[2:]) + each(quantise, et(0)[1:2]) + each(empty, et(1)[:1]) + each(quantise, et(0)[2:]) + each(empty, et(1)[1:]) + each(quantise, et(1))
+        vector = each(empty, et(0)[:2]) + apart(et(0)[:1]) + each(empty, et(0)[2:]) + apart(et(0)[1:2]) + each(empty, et(1)[:1]) + apart(et(0)[2:]) + each(empty, et(1)[1:]) + apart(et(1))
         vector += each(empty, et(2)) + both(times_slope, TRAIN, [0, 1])
         scalar = each(widen, et(0) + et(1)) + prep(2) + prep(3) + prep(4)
         held = ["w_laid0", "w_laid0", "w_laid0", "w_laid0", "w_laid1", "w_laid1"]
         gpsimd = [(lay_w, piece, "gpsimd", held[piece], dt(1) if piece == 4 else []) for piece in range(6)]
-        tensor += each(turn, et(3)) + each(turn, aq(0)[:2], True) + each(turn, aq(0)[2:]) + both(back, TRAIN, [2], [0]) + each(turn, aq(1)[:1], True) + each(turn, aq(1)[1:]) + both(back, TRAIN, [2], [1])
-        vector += each(empty, et(3)[:1]) + each(quantise, et(2)) + each(empty, et(3)[1:]) + each(quantise, et(3)[:1] + aq(0) + et(3)[1:]) + [(quantise_w, 0)] + both(times_slope, TRAIN, [2])
-        scalar += sorts(aq(0)[2:]) + each(empty, aq(0)) + sorts(aq(1)[1:]) + each(empty, aq(1)) + sorts(at(0))
+        tensor += each(turn, et(3)) + each(turn, aq(0), True) + both(back, TRAIN, [2], [0]) + each(turn, aq(1), True) + both(back, TRAIN, [2], [1])
+        vector += joined(et(2)) + each(empty, et(3)) + apart(aq(0)) + joined(et(3)) + [(quantise_w, 0)] + both(times_slope, TRAIN, [2])
+        scalar += each(empty, aq(0)) + sorts(at(0)[:1]) + each(empty, aq(1)) + sorts(at(0)[1:])
         for i in (4, 5):
             pair = i - 4
-            tensor += each(turn, et(i) + at(pair) + (dt(0) if i == 4 else [])) + both(back, TRAIN, [i - 1]) + each(gram_act, [2 * pair, 2 * pair + 1])
-            vector += each(empty, et(i)) + each(quantise, (aq(1) if i == 4 else []) + at(pair) + et(i) + (dt(0) if i == 4 else [])) + [(quantise_w, i - 3)] + both(times_slope, TRAIN, [i - 1]) + [(keep_gram, 2 * pair, "vector")]
-            scalar += each(empty, at(pair) + (dt(0) if i == 4 else [])) + each(widen, et(i + 1)) + sorts(et(i + 1) + (at(pair + 1) if i < 5 else eq(0, 1))) + each(keep_gram, [2 * pair + 1])
-        tensor += each(turn, et(6) + eq(0, 1) + dt(1)) + both(back, TRAIN, [5]) + both(back, QUERY, [0, 1], [0])
-        vector += each(empty, et(6)) + [(quantise_w, 3)] + each(quantise, eq(0, 1) + et(6)) + each(sort_words, et(7)[:1], "vector") + each(quantise, dt(1)) + both(times_slope, TRAIN, [5]) + both(times_slope, QUERY, [0, 1], [0])
-        scalar += each(empty, eq(0, 1)) + each(empty, dt(1), "scalar", "w_laid1") + each(widen, et(7)) + sorts(et(7)[1:] + eq(2, 3))
-        tensor += each(turn, et(7) + eq(2, 3) + dt(2) + dq(0, 0)) + both(back, TRAIN, [6]) + both(back, QUERY, [2, 3], [0])
-        vector += each(empty, et(7)) + each(quantise, eq(2, 3) + et(7) + dt(2) + dq(0, 0)) + [(quantise_w, 4)] + both(times_slope, TRAIN, [6]) + both(times_slope, QUERY, [2, 3], [0])
+            tensor += turn_err(i) + each(turn, at(pair) + (dt(0) if i == 4 else [])) + both(back, TRAIN, [i - 1]) + each(gram_act, [2 * pair, 2 * pair + 1])
+            vector += each(empty, et(i)) + apart(aq(1) if i == 4 else []) + joined(at(pair)[:2], at(pair)[2:], et(i)) + apart(dt(0) if i == 4 else []) + [(quantise_w, i - 3)] + both(times_slope, TRAIN, [i - 1]) + [(keep_gram, 2 * pair, "vector")]
+            scalar += each(empty, at(pair) + (dt(0) if i == 4 else [])) + prep(i + 1) + (sorts(at(1)) if i < 5 else sorts_eq(0, 1)) + each(keep_gram, [2 * pair + 1])
+        tensor += turn_err(6) + each(turn, eq(0, 1) + dt(1)) + both(back, TRAIN, [5]) + both(back, QUERY, [0, 1], [0])
+        vector += each(empty, et(6)) + [(quantise_w, 3)] + joined(eq(0), eq(1), et(6), dt(1)) + both(times_slope, TRAIN, [5]) + both(times_slope, QUERY, [0, 1], [0])
+        scalar += each(empty, eq(0, 1)) + each(empty, dt(1), "scalar", "w_laid1") + prep(7) + sorts_eq(2, 3)
+        tensor += turn_err(7) + each(turn, eq(2, 3) + dt(2) + dq(0, 0)) + both(back, TRAIN, [6]) + both(back, QUERY, [2, 3], [0])
+        vector += each(empty, et(7)) + joined(eq(2), eq(3), et(7)) + [(quantise_w, 4)] + both(times_slope, TRAIN, [6]) + both(times_slope, QUERY, [2, 3], [0])
         scalar += each(empty, eq(2, 3) + dt(2) + dq(0, 0)) + sorts(at(2)) + [(lay_w, 6, "scalar")]
         three, last = slice(0, 3), slice(3, 4)
         tensor += each(turn, at(2) + dt(3, 4) + dq(1, 0)) + both(back, TRAIN, [7], [0]) + each(gram_act, [4, 5]) + [(back, QUERY, i, 1, three) for i in range(3)] + [(back, QUERY, i, 1, last) for i in range(3)] + [(back, QUERY, 3, 1)]
-        vector += each(empty, at(2), "vector") + each(quantise, at(2)) + [(quantise_w, 6), (quantise_w, 5)] + each(quantise, dt(3, 4) + dq(1, 0)) + both(times_slope, TRAIN, [7], [0]) + [(quantise_w, 7)] + both(times_slope, QUERY, range(4), [1])
+        vector += each(empty, at(2), "vector") + joined(at(2)[:2], at(2)[2:]) + [(quantise_w, 6), (quantise_w, 5)] + joined(dt(2, 3), dq(0, 0) + dq(1, 0)) + both(times_slope, TRAIN, [7], [0]) + [(quantise_w, 7)] + both(times_slope, QUERY, range(4), [1])
         scalar += each(empty, dt(3, 4) + dq(1, 0)) + [(lay_w, 7, "scalar")] + each(keep_gram, [4, 5]) + sorts(at(3))
         tensor += each(turn, dq(0, 1) + dt(5) + at(3)[:2] + dq(1, 1) + at(3)[2:]) + both(back, TRAIN, [7], [1]) + each(gram_err, [0, 1]) + each(turn, dt(6, 7)) + [(gram_err, 2), (gram_act, 6), (gram_err, 3), (gram_err, 4), (gram_err, 5), (gram_act, 7), (gram_err, 6), (gram_err, 7, slice(0, 2), left), (gram_err, 7, slice(0, 2), right)]
-        vector += each(quantise, dq(0, 1) + dq(1, 1)) + both(times_slope, TRAIN, [7], [1]) + each(quantise, at(3) + dt(5)) + each(finish, [0, 1, 2]) + each(quantise, dt(6, 7)) + each(finish, range(3, 7)) + [(finish, 7, left), (finish, 7, right)]
+        vector += apart(dq(0, 1) + dq(1, 1)) + both(times_slope, TRAIN, [7], [1]) + joined(at(3)[:2], at(3)[2:], dt(4, 5)) + each(finish, [0, 1, 2]) + joined(dt(6, 7)) + each(finish, range(3, 7)) + [(finish, 7, left), (finish, 7, right)]
         scalar += each(empty, dq(0, 1) + dq(1, 1) + at(3) + dt(5, 6, 7)) + each(keep_gram, [6, 7])
         with tc.manual_schedule():
             make_identity(nc, ident[:])

@@ -21,8 +21,8 @@ ADD = mybir.AluOpType.add
 
 TRAIN, QUERY = "train", "query"
 RINGS = {
-    "err_bytes": (3, 2), "act_raw": (3, 3), "w_raw": (3, 1), "slope_train": (3, 4), "err_query": (3, 2),
-    "wide": (2, 1), "sorted1": (9, 1), "k_first1": (3, 1), "k_first2": (4, 1), "d": (11, 1), "w_laid": (1, 1), "w_laid0": (1, 1), "w_laid1": (1, 1),
+    "err_bytes": (3, 2), "act_raw": (3, 3), "w_raw": (3, 1), "slope": (4, 4), "err_query": (3, 2),
+    "wide": (2, 1), "sorted1": (8, 1), "k_first": (7, 1), "d": (11, 1), "w_laid": (1, 1), "w_laid0": (1, 1), "w_laid1": (1, 1),
     "et_codes": (3, 2), "at_codes": (2, 2),
 }
 
@@ -40,6 +40,7 @@ def tile_gradient_inner_products_s11_kernel(
         taken = {name: 0 for name in RINGS}
         free_banks = list(range(8))
         groups = {}
+        mates = {}
 
         def kept(name, shape, dtype):
             return keep.tile(shape, dtype, name=name, align_bytes=64)
@@ -158,13 +159,10 @@ def tile_gradient_inner_products_s11_kernel(
             return True
 
         def load_slope(side, tiles):
-            if side == TRAIN and not room("slope_train"):
+            if not room("slope"):
                 return False
             pair, first = divmod(tiles[0], 2)
-            shape = [P, len(tiles), F]
-            raw = ring("slope_train", ("slope", side, tiles[0]), shape, BF16) if side == TRAIN else kept("slope_query%d" % pair, shape, BF16)
-            if side == TRAIN:
-                readers["slope", side, tiles[0]][1] = 2 * len(tiles)
+            raw = ring("slope", ("slope", side, tiles[0]), [P, len(tiles), F], BF16, 2 * len(tiles))
             nc.sync.dma_start(out=raw[:], in_=rows(slope_train if side == TRAIN else slope_query, side, pair)[:, first : first + len(tiles), :])
             for j, i in enumerate(tiles):
                 t["slope", side, i] = raw[:, j, :]
@@ -227,14 +225,13 @@ def tile_gradient_inner_products_s11_kernel(
 
         def empty(key, engine="scalar", name="k_first"):
             kind, side, i, g = key
-            group = groups[key]
-            name = name if name != "k_first" else "k_first%d" % len(group)
+            group = mates[key]
             if not (there(("full", key)) and (("k_first", group) in t or room(name))):
                 return False
             turned = give_bank(key)
             g, n = g if key[:2] == ("err", TRAIN) else (g, 2)
             if ("k_first", group) not in t:
-                t["k_first", group] = ring(name, ("k_first", group), [P, len(group), n * P, 4], BF16, 1)
+                t["k_first", group] = ring(name, ("k_first", group), [P, len(group), n * P, 4], BF16, len(group))
             x = t["k_first", group][:, group.index(key)]
             t["laid", key] = True
             if (kind, side) != ("err", TRAIN):
@@ -252,6 +249,7 @@ def tile_gradient_inner_products_s11_kernel(
         def quantise(key):
             kind, side, i, g = key
             group = groups[key]
+            first = mates[key].index(key)
             n = len(group)
             g, n = (g[0], n * g[1]) if key[:2] == ("err", TRAIN) else (2 * g, 2 * n) if kind == "err" else (g, n)
             opens = side == TRAIN and g == 0 and kind != "d"
@@ -270,9 +268,9 @@ def tile_gradient_inner_products_s11_kernel(
                 both_parts = [x[:, g, 256 * i : 256 * (i + n)] for x in ((aq_codes, aq_planes) if kind == "act" else (dq_codes, dq_planes))]
             else:
                 both_parts = [x[:, i : i + n].rearrange("p i g r -> p (i g r)") for x in (dt_codes, dt_planes)]
-            nc.vector.quantize_mx(out=both_parts[0].bitcast(FP8X4), scales=both_parts[1], in_=t["k_first", group][:].rearrange("p b r t -> p (b r t)"))
-            was_read(("k_first", group))
+            nc.vector.quantize_mx(out=both_parts[0].bitcast(FP8X4), scales=both_parts[1], in_=t["k_first", mates[key]][:, first : first + len(group)].rearrange("p b r t -> p (b r t)"))
             for k in group:
+                was_read(("k_first", mates[key]))
                 t["mx", k] = True
             return True
 
@@ -405,8 +403,13 @@ def tile_gradient_inner_products_s11_kernel(
             for keys in lists:
                 for key in keys:
                     groups[key] = tuple(keys)
+                    mates.setdefault(key, tuple(keys))
                 heads.append(keys[0])
             return each(quantise, heads)
+
+        def share(*keys):
+            for key in keys:
+                mates[key] = keys
 
         def apart(keys):
             return joined(*[[key] for key in keys])
@@ -435,7 +438,7 @@ def tile_gradient_inner_products_s11_kernel(
             return each(widen, et(i)) + sorts(et(i)[: 2 if i < 5 else 1])
 
         def turn_err(i):
-            return [(turn, key, i >= 5 and b == 1) for b, key in enumerate(et(i))]
+            return [(turn, key, i in (5, 6) and b == 1) for b, key in enumerate(et(i))]
 
         def sorts(keys):
             return [(sort_words, (key,)) for key in keys]
@@ -443,13 +446,19 @@ def tile_gradient_inner_products_s11_kernel(
         def sorts_eq(*tiles):
             return sorts(eq(*tiles))
 
-        sync = [(load_first_bytes, 0, 1), (load_scale,), (load_first_bytes, 1, 4), (load_bytes, 1), (load_v_scales,), (load_v, 0), (load_bytes, 2), (load_v, 1), (load_v, 2), (load_v, 3), (load_bytes, 3), (load_slope, TRAIN, [0, 1]),
-            (load_w, 0), (load_bytes, 4), (load_act, QUERY, 0), (load_act, QUERY, 1), (load_act, TRAIN, 0), (load_slope, TRAIN, [2]), (load_w, 1), (load_bytes, 5), (load_act, TRAIN, 1), (load_slope, TRAIN, [3]),
+        share(*et(0)[:2])
+        share(*et(1))
+        share(*aq(0)[1:])
+        share(*aq(1)[:2])
+        share(aq(1)[2], at(0)[2])
+        share(*(dq(0, 1) + dq(1, 1)))
+        sync = [(load_first_bytes, 0, 1), (load_scale,), (load_first_bytes, 1, 4), (load_bytes, 1), (load_v_scales,), (load_v, 0), (load_bytes, 2), (load_v, 1), (load_v, 2), (load_v, 3), (load_bytes, 3), (load_w, 0), (load_slope, TRAIN, [0, 1]),
+            (load_bytes, 4), (load_act, QUERY, 0), (load_act, QUERY, 1), (load_act, TRAIN, 0), (load_slope, TRAIN, [2]), (load_w, 1), (load_bytes, 5), (load_act, TRAIN, 1), (load_slope, TRAIN, [3]),
             (load_w, 2), (load_slope, TRAIN, [4, 5]), (load_bytes, 6), (load_err_query, 0), (load_err_query, 1), (load_w, 3), (load_bytes, 7), (load_slope, QUERY, [0, 1]), (load_err_query, 2), (load_err_query, 3), (load_w, 4), (load_w, 6), (load_slope, QUERY, [2, 3]), (load_act, TRAIN, 2), (load_slope, TRAIN, [6, 7]),
             (load_w, 5), (load_w, 7), (load_act, TRAIN, 3)]
         left, right = slice(0, 256), slice(256, N)
         sync += each(store, range(7)) + [(store, 7, left), (store, 7, right)]
-        tensor = each(turn, et(0) + et(1), True) + [(back, TRAIN, 0, h, slice(g, g + 1)) for g in range(2) for h in range(2)] + each(turn, et(2)) + [(back, TRAIN, 0, 0, hi), (back, TRAIN, 0, 1, hi)] + both(back, TRAIN, [1])
+        tensor = each(turn, et(0)[:1], True) + each(turn, et(0)[1:] + et(1)[:1], True) + [(back, TRAIN, 0, h, slice(0, 1)) for h in range(2)] + each(turn, et(1)[1:], True) + [(back, TRAIN, 0, h, slice(1, 2)) for h in range(2)] + each(turn, et(2)) + [(back, TRAIN, 0, 0, hi), (back, TRAIN, 0, 1, hi)] + both(back, TRAIN, [1])
         vector = each(empty, et(0)[:2]) + apart(et(0)[:1]) + each(empty, et(0)[2:]) + apart(et(0)[1:2]) + each(empty, et(1)[:1]) + apart(et(0)[2:]) + each(empty, et(1)[1:]) + apart(et(1))
         vector += each(empty, et(2)) + both(times_slope, TRAIN, [0, 1])
         scalar = each(widen, et(0) + et(1)) + prep(2) + prep(3) + prep(4)
@@ -461,21 +470,21 @@ def tile_gradient_inner_products_s11_kernel(
         for i in (4, 5):
             pair = i - 4
             tensor += turn_err(i) + each(turn, at(pair) + (dt(0) if i == 4 else [])) + both(back, TRAIN, [i - 1]) + each(gram_act, [2 * pair, 2 * pair + 1])
-            vector += each(empty, et(i)) + apart(aq(1) if i == 4 else []) + joined(at(pair)[:2], at(pair)[2:], et(i)) + apart(dt(0) if i == 4 else []) + [(quantise_w, i - 3)] + both(times_slope, TRAIN, [i - 1]) + [(keep_gram, 2 * pair, "vector")]
-            scalar += each(empty, at(pair) + (dt(0) if i == 4 else [])) + prep(i + 1) + (sorts(at(1)) if i < 5 else sorts_eq(0, 1)) + each(keep_gram, [2 * pair + 1])
+            vector += each(empty, et(i)) + apart(aq(1) if i == 4 else []) + joined(at(pair)[:2], at(pair)[2:], et(i)) + apart(dt(0) if i == 4 else []) + [(quantise_w, i - 3)] + both(times_slope, TRAIN, [i - 1]) + each(keep_gram, [2] if i == 5 else [], "vector")
+            scalar += each(empty, at(pair) + (dt(0) if i == 4 else [])) + prep(i + 1) + (sorts(at(1)) if i < 5 else sorts_eq(0, 1)) + each(keep_gram, [0, 1] if i == 4 else [3])
         tensor += turn_err(6) + each(turn, eq(0, 1) + dt(1)) + both(back, TRAIN, [5]) + both(back, QUERY, [0, 1], [0])
         vector += each(empty, et(6)) + [(quantise_w, 3)] + joined(eq(0), eq(1), et(6), dt(1)) + both(times_slope, TRAIN, [5]) + both(times_slope, QUERY, [0, 1], [0])
-        scalar += each(empty, eq(0, 1)) + each(empty, dt(1), "scalar", "w_laid1") + prep(7) + sorts_eq(2, 3)
-        tensor += turn_err(7) + each(turn, eq(2, 3) + dt(2) + dq(0, 0)) + both(back, TRAIN, [6]) + both(back, QUERY, [2, 3], [0])
-        vector += each(empty, et(7)) + joined(eq(2), eq(3), et(7)) + [(quantise_w, 4)] + both(times_slope, TRAIN, [6]) + both(times_slope, QUERY, [2, 3], [0])
-        scalar += each(empty, eq(2, 3) + dt(2) + dq(0, 0)) + sorts(at(2)) + [(lay_w, 6, "scalar")]
+        scalar += each(empty, eq(0, 1)) + each(empty, dt(1), "scalar", "w_laid1") + sorts_eq(2, 3) + each(widen, et(7))
+        tensor += each(turn, eq(2, 3) + dt(2) + dq(0, 0)) + both(back, TRAIN, [6]) + both(back, QUERY, [2], [0])
+        vector += each(empty, eq(2), "vector") + joined(eq(2), eq(3)) + [(quantise_w, 4)] + both(times_slope, TRAIN, [6]) + both(times_slope, QUERY, [2], [0])
+        scalar += each(empty, eq(3) + dt(2) + dq(0, 0)) + sorts(et(7) + at(2))
         three, last = slice(0, 3), slice(3, 4)
-        tensor += each(turn, at(2) + dt(3, 4) + dq(1, 0)) + both(back, TRAIN, [7], [0]) + each(gram_act, [4, 5]) + [(back, QUERY, i, 1, three) for i in range(3)] + [(back, QUERY, i, 1, last) for i in range(3)] + [(back, QUERY, 3, 1)]
-        vector += each(empty, at(2), "vector") + joined(at(2)[:2], at(2)[2:]) + [(quantise_w, 6), (quantise_w, 5)] + joined(dt(2, 3), dq(0, 0) + dq(1, 0)) + both(times_slope, TRAIN, [7], [0]) + [(quantise_w, 7)] + both(times_slope, QUERY, range(4), [1])
-        scalar += each(empty, dt(3, 4) + dq(1, 0)) + [(lay_w, 7, "scalar")] + each(keep_gram, [4, 5]) + sorts(at(3))
-        tensor += each(turn, dq(0, 1) + dt(5) + at(3)[:2] + dq(1, 1) + at(3)[2:]) + both(back, TRAIN, [7], [1]) + each(gram_err, [0, 1]) + each(turn, dt(6, 7)) + [(gram_err, 2), (gram_act, 6), (gram_err, 3), (gram_err, 4), (gram_err, 5), (gram_act, 7), (gram_err, 6), (gram_err, 7, slice(0, 2), left), (gram_err, 7, slice(0, 2), right)]
-        vector += apart(dq(0, 1) + dq(1, 1)) + both(times_slope, TRAIN, [7], [1]) + joined(at(3)[:2], at(3)[2:], dt(4, 5)) + each(finish, [0, 1, 2]) + joined(dt(6, 7)) + each(finish, range(3, 7)) + [(finish, 7, left), (finish, 7, right)]
-        scalar += each(empty, dq(0, 1) + dq(1, 1) + at(3) + dt(5, 6, 7)) + each(keep_gram, [6, 7])
+        tensor += turn_err(7) + each(turn, at(2) + dt(3, 4)) + both(back, QUERY, [3], [0]) + each(gram_act, [4, 5]) + [(back, QUERY, i, 1, three) for i in range(3)] + [(back, QUERY, i, 1, last) for i in range(3)] + [(back, QUERY, 3, 1)]
+        vector += each(empty, et(7)) + joined(at(2)[:2], at(2)[2:]) + [(quantise_w, 5)] + both(times_slope, QUERY, [3], [0]) + [(quantise_w, 6)] + joined(et(7)) + [(quantise_w, 7)] + joined(dt(2, 3)) + both(times_slope, QUERY, range(4), [1])
+        scalar += each(empty, at(2)) + [(lay_w, 6, "scalar", "w_laid0"), (lay_w, 7, "scalar")] + each(empty, dt(3, 4)) + each(keep_gram, [4, 5]) + sorts(at(3))
+        tensor += each(turn, dq(1, 0) + dq(0, 1) + dt(5) + at(3)[:1] + dq(1, 1) + at(3)[1:]) + both(back, TRAIN, [7]) + each(gram_err, [0, 1, 2]) + each(turn, dt(6, 7)) + [(gram_act, 6), (gram_err, 3), (gram_err, 4), (gram_err, 5), (gram_act, 7), (gram_err, 6), (gram_err, 7, slice(0, 2), left), (gram_err, 7, slice(0, 2), right)]
+        vector += joined(dq(0, 0) + dq(1, 0), dq(0, 1) + dq(1, 1)) + both(times_slope, TRAIN, [7]) + joined(at(3)[:2], at(3)[2:], dt(4, 5)) + each(finish, [0, 1, 2]) + joined(dt(6, 7)) + each(finish, range(3, 7)) + [(finish, 7, left), (finish, 7, right)]
+        scalar += each(empty, dq(1, 0) + dq(0, 1) + dq(1, 1) + at(3) + dt(5, 6, 7)) + each(keep_gram, [6, 7])
         with tc.manual_schedule():
             make_identity(nc, ident[:])
             nc.vector.memset(v_planes[:].rearrange("p g n -> p (g n)").bitcast(I32), 0)

@@ -22,7 +22,7 @@ ADD = mybir.AluOpType.add
 TRAIN, QUERY = "train", "query"
 RINGS = {
     "err_bytes": (3, 2), "act_raw": (3, 3), "w_raw": (3, 1), "slope": (4, 4), "err_query": (3, 2),
-    "wide": (2, 1), "sorted1": (8, 1), "k_first": (7, 1), "d": (11, 1), "w_laid": (1, 1), "w_laid0": (1, 1), "w_laid1": (1, 1),
+    "wide": (2, 1), "sorted1": (6, 1), "k_first": (7, 1), "d": (10, 1), "w_laid": (1, 1), "w_laid0": (1, 1), "w_laid1": (1, 1),
     "et_codes": (3, 2), "at_codes": (2, 2),
 }
 
@@ -252,7 +252,7 @@ def tile_gradient_inner_products_s11_kernel(
             first = mates[key].index(key)
             n = len(group)
             g, n = (g[0], n * g[1]) if key[:2] == ("err", TRAIN) else (2 * g, 2 * n) if kind == "err" else (g, n)
-            opens = side == TRAIN and g == 0 and kind != "d"
+            opens = side == TRAIN and kind != "d" and ("codes", kind, side, i) not in t
             name = "at_codes" if kind == "act" else "et_codes"
             if not there(*[("laid", k) for k in group]) or (opens and not room(name)):
                 return False
@@ -457,33 +457,33 @@ def tile_gradient_inner_products_s11_kernel(
             (load_w, 2), (load_slope, TRAIN, [4, 5]), (load_bytes, 6), (load_err_query, 0), (load_err_query, 1), (load_w, 3), (load_bytes, 7), (load_slope, QUERY, [0, 1]), (load_err_query, 2), (load_err_query, 3), (load_w, 4), (load_w, 6), (load_slope, QUERY, [2, 3]), (load_act, TRAIN, 2), (load_slope, TRAIN, [6, 7]),
             (load_w, 5), (load_w, 7), (load_act, TRAIN, 3)]
         left, right = slice(0, 256), slice(256, N)
-        sync += each(store, range(7)) + [(store, 7, left), (store, 7, right)]
+        sync += each(store, [1, 0, 2, 4, 3, 5, 6]) + [(store, 7, left), (store, 7, right)]
         tensor = each(turn, et(0)[:1], True) + each(turn, et(0)[1:] + et(1)[:1], True) + [(back, TRAIN, 0, h, slice(0, 1)) for h in range(2)] + each(turn, et(1)[1:], True) + [(back, TRAIN, 0, h, slice(1, 2)) for h in range(2)] + each(turn, et(2)) + [(back, TRAIN, 0, 0, hi), (back, TRAIN, 0, 1, hi)] + both(back, TRAIN, [1])
         vector = each(empty, et(0)[:2]) + apart(et(0)[:1]) + each(empty, et(0)[2:]) + apart(et(0)[1:2]) + each(empty, et(1)[:1]) + apart(et(0)[2:]) + each(empty, et(1)[1:]) + apart(et(1))
-        vector += each(empty, et(2)) + both(times_slope, TRAIN, [0, 1])
-        scalar = each(widen, et(0) + et(1)) + prep(2) + prep(3) + prep(4)
+        vector += each(empty, et(2)[::-1]) + both(times_slope, TRAIN, [0, 1], (1, 0))
+        scalar = each(widen, et(0) + et(1)) + prep(2) + [step for i in (3, 4) for step in each(widen, et(i)) + sorts(et(i)[::-1])]
         held = ["w_laid0", "w_laid0", "w_laid0", "w_laid0", "w_laid1", "w_laid1"]
         gpsimd = [(lay_w, piece, "gpsimd", held[piece], dt(1) if piece == 4 else []) for piece in range(6)]
         tensor += each(turn, et(3)) + each(turn, aq(0), True) + both(back, TRAIN, [2], [0]) + each(turn, aq(1), True) + both(back, TRAIN, [2], [1])
-        vector += joined(et(2)) + each(empty, et(3)) + apart(aq(0)) + joined(et(3)) + [(quantise_w, 0)] + both(times_slope, TRAIN, [2])
+        vector += joined(et(2)) + each(empty, et(3)[::-1]) + apart(aq(0)[::-1]) + joined(et(3)) + [(quantise_w, 0)] + both(times_slope, TRAIN, [2])
         scalar += each(empty, aq(0)) + sorts(at(0)[:1]) + each(empty, aq(1)) + sorts(at(0)[1:])
         for i in (4, 5):
             pair = i - 4
             tensor += turn_err(i) + each(turn, at(pair) + (dt(0) if i == 4 else [])) + both(back, TRAIN, [i - 1]) + each(gram_act, [2 * pair, 2 * pair + 1])
-            vector += each(empty, et(i)) + apart(aq(1) if i == 4 else []) + joined(at(pair)[:2], at(pair)[2:], et(i)) + apart(dt(0) if i == 4 else []) + [(quantise_w, i - 3)] + both(times_slope, TRAIN, [i - 1]) + each(keep_gram, [2] if i == 5 else [], "vector")
+            vector += each(empty, et(i)) + apart(aq(1)[::-1] if i == 4 else []) + joined(at(pair)[:2], at(pair)[2:], et(i)) + apart(dt(0) if i == 4 else []) + [(quantise_w, i - 3)] + both(times_slope, TRAIN, [i - 1], (1, 0)) + each(keep_gram, [2] if i == 5 else [], "vector")
             scalar += each(empty, at(pair) + (dt(0) if i == 4 else [])) + prep(i + 1) + (sorts(at(1)) if i < 5 else sorts_eq(0, 1)) + each(keep_gram, [0, 1] if i == 4 else [3])
         tensor += turn_err(6) + each(turn, eq(0, 1) + dt(1)) + both(back, TRAIN, [5]) + both(back, QUERY, [0, 1], [0])
-        vector += each(empty, et(6)) + [(quantise_w, 3)] + joined(eq(0), eq(1), et(6), dt(1)) + both(times_slope, TRAIN, [5]) + both(times_slope, QUERY, [0, 1], [0])
+        vector += each(empty, et(6)) + [(quantise_w, 3)] + joined(eq(0), eq(1), et(6), dt(1)) + both(times_slope, TRAIN, [5], (1, 0)) + both(times_slope, QUERY, [0, 1], [0])
         scalar += each(empty, eq(0, 1)) + each(empty, dt(1), "scalar", "w_laid1") + sorts_eq(2, 3) + each(widen, et(7))
         tensor += each(turn, eq(2, 3) + dt(2) + dq(0, 0)) + both(back, TRAIN, [6]) + both(back, QUERY, [2], [0])
-        vector += each(empty, eq(2), "vector") + joined(eq(2), eq(3)) + [(quantise_w, 4)] + both(times_slope, TRAIN, [6]) + both(times_slope, QUERY, [2], [0])
+        vector += each(empty, eq(2), "vector") + joined(eq(2), eq(3)) + [(quantise_w, 4)] + both(times_slope, TRAIN, [6], (1, 0)) + both(times_slope, QUERY, [2], [0])
         scalar += each(empty, eq(3) + dt(2) + dq(0, 0)) + sorts(et(7) + at(2))
         three, last = slice(0, 3), slice(3, 4)
         tensor += turn_err(7) + each(turn, at(2) + dt(3, 4)) + both(back, QUERY, [3], [0]) + each(gram_act, [4, 5]) + [(back, QUERY, i, 1, three) for i in range(3)] + [(back, QUERY, i, 1, last) for i in range(3)] + [(back, QUERY, 3, 1)]
         vector += each(empty, et(7)) + joined(at(2)[:2], at(2)[2:]) + [(quantise_w, 5)] + both(times_slope, QUERY, [3], [0]) + [(quantise_w, 6)] + joined(et(7)) + [(quantise_w, 7)] + joined(dt(2, 3)) + both(times_slope, QUERY, range(4), [1])
-        scalar += each(empty, at(2)) + [(lay_w, 6, "scalar", "w_laid0"), (lay_w, 7, "scalar")] + each(empty, dt(3, 4)) + each(keep_gram, [4, 5]) + sorts(at(3))
+        scalar += each(empty, at(2)) + [(lay_w, 6, "scalar", "w_laid0"), (lay_w, 7, "scalar")] + each(empty, dt(3, 4)) + each(keep_gram, [4, 5]) + sorts(at(3)[::-1])
         tensor += each(turn, dq(1, 0) + dq(0, 1) + dt(5) + at(3)[:1] + dq(1, 1) + at(3)[1:]) + both(back, TRAIN, [7]) + each(gram_err, [0, 1, 2]) + each(turn, dt(6, 7)) + [(gram_act, 6), (gram_err, 3), (gram_err, 4), (gram_err, 5), (gram_act, 7), (gram_err, 6), (gram_err, 7, slice(0, 2), left), (gram_err, 7, slice(0, 2), right)]
-        vector += joined(dq(0, 0) + dq(1, 0), dq(0, 1) + dq(1, 1)) + both(times_slope, TRAIN, [7]) + joined(at(3)[:2], at(3)[2:], dt(4, 5)) + each(finish, [0, 1, 2]) + joined(dt(6, 7)) + each(finish, range(3, 7)) + [(finish, 7, left), (finish, 7, right)]
+        vector += joined(dq(0, 0) + dq(1, 0), dq(0, 1) + dq(1, 1)) + both(times_slope, TRAIN, [7]) + joined(at(3)[:2], at(3)[2:], dt(4, 5)) + each(finish, [1, 0, 2]) + joined(dt(6, 7)) + each(finish, [4, 3, 5, 6]) + [(finish, 7, left), (finish, 7, right)]
         scalar += each(empty, dq(1, 0) + dq(0, 1) + dq(1, 1) + at(3) + dt(5, 6, 7)) + each(keep_gram, [6, 7])
         with tc.manual_schedule():
             make_identity(nc, ident[:])

from contextlib import ExitStack

import concourse.mybir as mybir
from concourse.masks import make_identity

M, N, K, C, F = 1024, 512, 1536, 2048, 1024
P = 128
PASS = 512
FLOPS = 2 * (M * F * C + N * F * C + M * N * F + M * N * K)

F32 = mybir.dt.float32
BF16 = mybir.dt.bfloat16
I32 = mybir.dt.int32
U32 = mybir.dt.uint32
U8 = mybir.dt.uint8
FP8 = mybir.dt.float8_e4m3fn
FP8X4 = mybir.dt.float8_e4m3fn_x4
FP4X4 = mybir.dt.float4_e2m1fn_x4
MULT = mybir.AluOpType.mult
ADD = mybir.AluOpType.add

TRAIN, QUERY = "train", "query"
RINGS = {
    "err_bytes": (3, 2), "act_raw": (3, 3), "w_raw": (3, 1), "slope": (4, 4), "err_query": (3, 2),
    "wide": (2, 1), "sorted1": (6, 1), "k_first": (7, 1), "d": (10, 1), "w_laid": (1, 1), "w_laid0": (1, 1), "w_laid1": (1, 1),
    "et_codes": (3, 2), "at_codes": (2, 2),
}


def tile_gradient_inner_products_s11_kernel(
    tc, act_train, act_query, err_train_bytes, err_train_scale, err_query, slope_train, slope_query, v_words, v_scales, w, out
):
    nc = tc.nc
    with ExitStack() as ctx:
        keep = ctx.enter_context(tc.tile_pool(name="keep", bufs=1))
        work = ctx.enter_context(tc.tile_pool(name="work", bufs=2))
        psum = ctx.enter_context(tc.psum_pool(name="psum", bufs=1))
        t = {}
        readers = {}
        taken = {name: 0 for name in RINGS}
        free_banks = list(range(8))
        groups = {}
        mates = {}

        def kept(name, shape, dtype):
            return keep.tile(shape, dtype, name=name, align_bytes=64)

        def room(name):
            return taken[name] < RINGS[name][0]

        def ring(name, owner, shape, dtype, count=None):
            taken[name] += 1
            readers[owner] = [name, count or RINGS[name][1]]
            return work.tile(shape, dtype, tag=name, name=name, bufs=RINGS[name][0], align_bytes=64)

        def was_read(owner):
            if owner in readers:
                readers[owner][1] -= 1
                if readers[owner][1] == 0:
                    taken[readers[owner][0]] -= 1

        def there(*names):
            return all(name in t for name in names)

        def take_bank(key, shape, dtype=F32):
            b = free_banks[0]
            free_banks.remove(b)
            t["bank", key] = psum.tile(shape, dtype, tag="bank%d" % b, name="bank%d" % b, bufs=1)
            t["bank_number", key] = b
            return t["bank", key]

        def give_bank(key):
            free_banks.append(t["bank_number", key])
            return t["bank", key]

        ident = kept("ident", [P, P], F32)
        v_planes = kept("v_planes", [P, 4, F], U8)
        v_codes = [kept("v_codes%d" % g, [P, 2 * F], U8) for g in range(4)]
        scale = kept("scale", [P, 4, 4], F32)
        w_codes = kept("w_codes", [P, 2, 4, N], U32)
        w_planes = kept("w_planes", [P, 2, 4, N], U8)
        aq_codes = kept("aq_codes", [P, 3, N], U32)
        aq_planes = kept("aq_planes", [P, 3, N], U8)
        rq_codes = kept("rq_codes", [P, 4, 4, P], U32)
        rq_planes = kept("rq_planes", [P, 4, 4, P], U8)
        dq_codes = kept("dq_codes", [P, 2, N], U32)
        dq_planes = kept("dq_planes", [P, 2, N], U8)
        dt_codes = kept("dt_codes", [P, 8, 2, P], U32)
        dt_planes = kept("dt_planes", [P, 8, 2, P], U8)
        gram = kept("gram", [P, 8, N], F32)

        def rows(src, side, pair):
            pattern = "(p j) k -> p j k" if side == TRAIN else "(j p) k -> p j k"
            return src[256 * pair : 256 * (pair + 1), :].rearrange(pattern, j=2)

        def load_first_bytes(g0, g1):
            raw = kept("first_bytes%d" % g0, [P, PASS * (g1 - g0)], U8)
            nc.sync.dma_start(out=raw[:], in_=rows(err_train_bytes, TRAIN, 0)[:, 0, PASS * g0 : PASS * g1])
            for g in range(g0, g1):
                t["bytes", 0, g] = (raw, PASS * (g - g0))
            return True

        def load_bytes(i):
            if not room("err_bytes"):
                return False
            raw = ring("err_bytes", ("bytes", i), [P, C], U8)
            nc.sync.dma_start(out=raw[:], in_=rows(err_train_bytes, TRAIN, i // 2)[:, i % 2, :])
            for g in range(4):
                t["bytes", i, g] = (raw, PASS * g)
            return True

        def load_scale():
            nc.sync.dma_start(out=scale[:], in_=err_train_scale.rearrange("o (g p t) -> p (o g) t", p=P, t=4))
            t["scale"] = True
            return True

        def load_v_scales():
            for r in range(4):
                nc.sync.dma_start(
                    out=v_planes[r:P:32, :, :].bitcast(I32),
                    in_=v_scales[:, r:16:4, :].rearrange("g q n -> q g n").bitcast(I32),
                )
            return True

        def load_v(g):
            nc.sync.dma_start(out=v_codes[g][:], in_=v_words[g])
            t["v", g] = True
            return True

        def load_act(side, pair):
            if not room("act_raw"):
                return False
            raw = ring("act_raw", ("raw", "act", side, pair), [P, 2, K], BF16)
            nc.sync.dma_start(out=raw[:], in_=rows(act_train if side == TRAIN else act_query, side, pair))
            for g in range(3):
                t["rows", (("act", side, pair, g),)] = raw[:, :, PASS * g : PASS * (g + 1)].bitcast(F32)
                t["owner", ("act", side, pair, g)] = ("raw", "act", side, pair)
            return True

        def load_w(piece):
            if not room("w_raw"):
                return False
            h, g = divmod(piece, 4)
            raw = ring("w_raw", ("w_raw", piece), [P, 4, N], BF16)
            nc.sync.dma_start(out=raw[:], in_=w[PASS * g : PASS * (g + 1), N * h : N * (h + 1)].rearrange("(p t) n -> p t n", t=4))
            t["w_raw", piece] = raw
            return True

        def load_err_query(i):
            if not room("err_query"):
                return False
            raw = ring("err_query", ("raw", "err", QUERY, i), [P, C], BF16)
            nc.sync.dma_start(out=raw[:], in_=err_query[P * i : P * (i + 1), :])
            words = raw[:].bitcast(F32).rearrange("p (a m) -> p a m", a=4)
            t["rows", tuple(eq(i))] = words
            for b, key in enumerate(eq(i)):
                t["rows", (key,)] = words[:, 2 * b : 2 * b + 2, :]
                t["owner", key] = ("raw", "err", QUERY, i)
            return True

        def load_slope(side, tiles):
            if not room("slope"):
                return False
            pair, first = divmod(tiles[0], 2)
            raw = ring("slope", ("slope", side, tiles[0]), [P, len(tiles), F], BF16, 2 * len(tiles))
            nc.sync.dma_start(out=raw[:], in_=rows(slope_train if side == TRAIN else slope_query, side, pair)[:, first : first + len(tiles), :])
            for j, i in enumerate(tiles):
                t["slope", side, i] = raw[:, j, :]
                t["slope_owner", side, i] = ("slope", side, tiles[0])
            return True

        def widen(*keys):
            kind, side, i, (g, n) = keys[0]
            n = sum(key[3][1] for key in keys)
            if not (there(("bytes", i, g)) and (g > 0 or room("wide"))):
                return False
            if g == 0:
                t["wide", i] = ring("wide", ("wide", i), [P, C], BF16, len(et(i)))
            x = t["wide", i][:, PASS * g : PASS * (g + n)]
            raw, k0 = t["bytes", i, g]
            nc.scalar.copy(out=x, in_=raw[:, k0 : k0 + PASS * n].bitcast(FP8))
            words = x.bitcast(F32).rearrange("p (a m) -> p a m", a=n)
            t["rows", keys] = words
            for key in keys:
                t["rows", (key,)] = words[:, key[3][0] - g : key[3][0] - g + key[3][1], :]
                t["owner", key] = ("wide", i)
                was_read(("bytes", i))
            return True

        def sort_words(keys, engine="scalar"):
            if not (there(("rows", keys)) and room("sorted%d" % len(keys))):
                return False
            x = ring("sorted%d" % len(keys), ("sorted", keys[0]), [P, 2 * len(keys), 2, P], F32, len(keys))
            copy = nc.scalar.copy if engine == "scalar" else nc.vector.tensor_copy
            copy(out=x[:], in_=t["rows", keys].rearrange("p a (m u) -> p a u m", u=2))
            for n, key in enumerate(keys):
                t["sorted", key] = x[:, 2 * n : 2 * n + 2]
                was_read(t["owner", key])
                t["owner", key] = ("sorted", keys[0])
            return True

        def turn(key, stepped=False):
            kind, side, i, g = key
            if kind == "d":
                sources = [("d", side, i, a) if side == TRAIN else ("d", side, 2 * i + a, g) for a in range(2)]
            else:
                sources = [("rows", (key,)) if stepped else ("sorted", key)]
            if not (there(*sources) and free_banks):
                return False
            n = g[1] if key[:2] == ("err", TRAIN) else 2
            turned = take_bank(key, [P, 2, n * P])
            for a in range(n):
                for u in range(2):
                    if kind == "d":
                        src = t[sources[a]][:, u, :]
                    elif stepped:
                        src = t["rows", (key,)][:, a, u : 256 : 2]
                    else:
                        src = t["sorted", key][:, a, u, :]
                    nc.tensor.transpose(turned[:, u, P * a : P * (a + 1)], src, ident[:])
            for source in sources if kind == "d" else [t["owner", key]]:
                was_read(source)
            t["full", key] = True
            return True

        def empty(key, engine="scalar", name="k_first"):
            kind, side, i, g = key
            group = mates[key]
            if not (there(("full", key)) and (("k_first", group) in t or room(name))):
                return False
            turned = give_bank(key)
            g, n = g if key[:2] == ("err", TRAIN) else (g, 2)
            if ("k_first", group) not in t:
                t["k_first", group] = ring(name, ("k_first", group), [P, len(group), n * P, 4], BF16, len(group))
            x = t["k_first", group][:, group.index(key)]
            t["laid", key] = True
            if (kind, side) != ("err", TRAIN):
                copy = nc.scalar.copy if engine == "scalar" else nc.vector.tensor_copy
                copy(out=x.bitcast(F32), in_=turned[:].rearrange("p u r -> p r u"))
            else:
                nc.vector.tensor_tensor(
                    out=x.rearrange("p (a m) (u e) -> p a m u e", a=n, u=2),
                    in0=turned[:].bitcast(BF16).rearrange("p u (a m e) -> p a m u e", a=n, e=2),
                    in1=scale[:, g : g + n, :].rearrange("p a (u e) -> p a u e", u=2).unsqueeze(2).to_broadcast([P, n, P, 2, 2]),
                    op=MULT,
                )
            return True

        def quantise(key):
            kind, side, i, g = key
            group = groups[key]
            first = mates[key].index(key)
            n = len(group)
            g, n = (g[0], n * g[1]) if key[:2] == ("err", TRAIN) else (2 * g, 2 * n) if kind == "err" else (g, n)
            opens = side == TRAIN and kind != "d" and ("codes", kind, side, i) not in t
            name = "at_codes" if kind == "act" else "et_codes"
            if not there(*[("laid", k) for k in group]) or (opens and not room(name)):
                return False
            if opens:
                shape = [P, 3, 2 * P] if kind == "act" else [P, 4, P]
                t["codes", kind, side, i] = ring(name, ("codes", kind, side, i), shape, U32)
                t["planes", kind, side, i] = work.tile(shape, U8, tag=name + "_planes", name=name + "_planes", bufs=RINGS[name][0], align_bytes=64)
            if kind == "err" and side == QUERY:
                t["codes", kind, side, i], t["planes", kind, side, i] = rq_codes[:, i], rq_planes[:, i]
            if kind == "err" or key[:2] == ("act", TRAIN):
                both_parts = [t[part, kind, side, i][:, g : g + n, :].rearrange("p g r -> p (g r)") for part in ("codes", "planes")]
            elif side == QUERY:
                both_parts = [x[:, g, 256 * i : 256 * (i + n)] for x in ((aq_codes, aq_planes) if kind == "act" else (dq_codes, dq_planes))]
            else:
                both_parts = [x[:, i : i + n].rearrange("p i g r -> p (i g r)") for x in (dt_codes, dt_planes)]
            nc.vector.quantize_mx(out=both_parts[0].bitcast(FP8X4), scales=both_parts[1], in_=t["k_first", mates[key]][:, first : first + len(group)].rearrange("p b r t -> p (b r t)"))
            for k in group:
                was_read(("k_first", mates[key]))
                t["mx", k] = True
            return True

        def accumulate(acc, operands, part=slice(0, 4)):
            for g, (lhs, lhs_scale, rhs, rhs_scale) in list(enumerate(operands))[part]:
                nc.tensor.matmul_mx(
                    out=acc, lhsT=lhs.bitcast(FP8X4), lhsT_scale=lhs_scale, rhs=rhs, rhs_scale=rhs_scale, start=g == 0, stop=g == len(operands) - 1
                )

        def back(side, i, h, part=slice(0, 4)):
            key = ("back", side, i, h)
            needs = [("mx", key) for key in (et(i) if side == TRAIN else eq(i)) if side == QUERY or key[3][0] < part.stop]
            needs += [("v", g) if side == TRAIN else ("mx", ("w", 4 * h + g)) for g in range(4)[part]]
            if not there(*needs) or (part.start == 0 and not free_banks):
                return False
            acc = take_bank(key, [P, N]) if part.start == 0 else t["bank", key]
            if side == TRAIN:
                moving = [(v_codes[g][:, F * h : F * (h + 1)].bitcast(FP4X4), v_planes[:, g, N * h : N * (h + 1)]) for g in range(4)]
            else:
                moving = [(w_codes[:, h, g, :].bitcast(FP8X4), w_planes[:, h, g, :]) for g in range(4)]
            accumulate(acc[:], [(t["codes", "err", side, i][:, g, :], t["planes", "err", side, i][:, g, :]) + moving[g] for g in range(4)], part)
            if part.stop == 4:
                was_read(("codes", "err", side, i))
                t["full", key] = True
            return True

        def times_slope(side, i, h):
            key = ("back", side, i, h)
            if not (there(("full", key), ("slope", side, i)) and room("d")):
                return False
            d = ring("d", ("d", side, i, h), [P, 2, 256 // 16, 16], BF16)
            nc.vector.tensor_tensor(
                out=d[:],
                in0=give_bank(key)[:].rearrange("p (q u r) -> p u q r", u=2, r=16),
                in1=t["slope", side, i][:, N * h : N * (h + 1)].rearrange("p (q u r) -> p u q r", u=2, r=16),
                op=MULT,
            )
            was_read(t["slope_owner", side, i])
            t["d", side, i, h] = d[:].rearrange("p u m e -> p u (m e)").bitcast(F32)
            return True

        def gram_act(i):
            key = ("gram_act", i)
            if not (there(*[("mx", k) for k in aq(0) + aq(1) + at(i // 2)]) and free_banks):
                return False
            half = slice(P * (i % 2), P * (i % 2) + P)
            codes, planes = t["codes", "act", TRAIN, i // 2], t["planes", "act", TRAIN, i // 2]
            accumulate(take_bank(key, [P, N])[:], [(codes[:, g, half], planes[:, g, half], aq_codes[:, g, :].bitcast(FP8X4), aq_planes[:, g, :]) for g in range(3)])
            was_read(("codes", "act", TRAIN, i // 2))
            t["full", key] = True
            return True

        def keep_gram(i, engine="scalar"):
            key = ("gram_act", i)
            if not there(("full", key)):
                return False
            copy = nc.scalar.copy if engine == "scalar" else nc.vector.tensor_copy
            copy(out=gram[:, i, :], in_=give_bank(key)[:])
            t["gram", i] = True
            return True

        def gram_err(i, part=slice(0, 2), cols=slice(0, N)):
            key = ("gram_err", i, cols.start)
            needs = dt(i) + [k for g in range(2)[part] for k in dq(0, g) + dq(1, g)]
            if not there(*[("mx", k) for k in needs]) or (part.start == 0 and not free_banks):
                return False
            acc = take_bank(key, [P, cols.stop - cols.start]) if part.start == 0 else t["bank", key]
            accumulate(acc[:], [(dt_codes[:, i, g, :], dt_planes[:, i, g, :], dq_codes[:, g, cols].bitcast(FP8X4), dq_planes[:, g, cols]) for g in range(2)], part)
            if part.stop == 2:
                t["full", key] = True
            return True

        def finish(i, cols=slice(0, N)):
            key = ("gram_err", i, cols.start)
            if not there(("full", key), ("gram", i)):
                return False
            nc.vector.tensor_tensor(out=gram[:, i, cols], in0=give_bank(key)[:], in1=gram[:, i, cols], op=MULT)
            t["done", i, cols.start] = True
            return True

        def store(i, cols=slice(0, N)):
            if not there(("done", i, cols.start)):
                return False
            nc.sync.dma_start(out=rows(out, TRAIN, i // 2)[:, i % 2, cols], in_=gram[:, i, cols])
            return True

        def lay_w(piece, engine="gpsimd", name="w_laid", behind=()):
            if not (there(("w_raw", piece), *[("mx", key) for key in behind]) and room(name)):
                return False
            x = ring(name, ("w_laid", piece), [P, N, 4], BF16)
            raw = t["w_raw", piece]
            if engine == "gpsimd":
                nc.gpsimd.tensor_scalar(out=x[:], in0=raw[:].rearrange("p t n -> p n t"), scalar1=1.0, scalar2=0.0, op0=MULT, op1=ADD)
            else:
                copy = nc.scalar.copy if engine == "scalar" else nc.vector.tensor_copy
                copy(out=x[:].rearrange("p (c i) t -> p c t i", i=4), in_=raw[:].rearrange("p t (c i) -> p c t i", i=4))
            t["w_laid", piece] = x
            was_read(("w_raw", piece))
            return True

        def quantise_w(piece):
            if not there(("w_laid", piece)):
                return False
            h, g = divmod(piece, 4)
            nc.vector.quantize_mx(out=w_codes[:, h, g, :].bitcast(FP8X4), scales=w_planes[:, h, g, :], in_=t["w_laid", piece][:].rearrange("p n t -> p (n t)"))
            was_read(("w_laid", piece))
            t["mx", ("w", piece)] = True
            return True

        def et(i):
            return [("err", TRAIN, i, unit) for unit in ([(0, 1), (1, 1), (2, 2)] if i == 0 else [(0, 2), (2, 2)])]

        def eq(*tiles):
            return [("err", QUERY, i, b) for i in tiles for b in range(2)]

        def aq(pair):
            return [("act", QUERY, pair, g) for g in range(3)]

        def at(pair):
            return [("act", TRAIN, pair, g) for g in range(3)]

        def dt(*tiles):
            return [("d", TRAIN, i, 0) for i in tiles]

        def dq(pair, g):
            return [("d", QUERY, pair, g)]

        def joined(*lists):
            heads = []
            for keys in lists:
                for key in keys:
                    groups[key] = tuple(keys)
                    mates.setdefault(key, tuple(keys))
                heads.append(keys[0])
            return each(quantise, heads)

        def share(*keys):
            for key in keys:
                mates[key] = keys

        def apart(keys):
            return joined(*[[key] for key in keys])

        def each(fn, keys, *more):
            return [(fn, key) + more for key in keys]

        def both(fn, side, tiles, halves=(0, 1)):
            return [(fn, side, i, h) for i in tiles for h in halves]

        def write_out(queues):
            while any(queues):
                moved = False
                for queue in queues[:-1]:
                    while queue and queue[0][0](*queue[0][1:]):
                        queue.remove(queue[0])
                        moved = True
                queue = queues[-1]
                if not moved:
                    assert queue and queue[0][0](*queue[0][1:]), [q[:1] for q in queues]
                    queue.remove(queue[0])

        lo, hi = slice(0, 2), slice(2, 4)

        def prep(i):
            return each(widen, et(i)) + sorts(et(i)[: 2 if i < 5 else 1])

        def turn_err(i):
            return [(turn, key, i in (5, 6) and b == 1) for b, key in enumerate(et(i))]

        def sorts(keys):
            return [(sort_words, (key,)) for key in keys]

        def sorts_eq(*tiles):
            return sorts(eq(*tiles))

        share(*et(0)[:2])
        share(*et(1))
        share(*aq(0)[1:])
        share(*aq(1)[:2])
        share(aq(1)[2], at(0)[2])
        share(*(dq(0, 1) + dq(1, 1)))
        sync = [(load_first_bytes, 0, 1), (load_scale,), (load_first_bytes, 1, 4), (load_bytes, 1), (load_v_scales,), (load_v, 0), (load_bytes, 2), (load_v, 1), (load_v, 2), (load_v, 3), (load_bytes, 3), (load_w, 0), (load_slope, TRAIN, [0, 1]),
            (load_bytes, 4), (load_act, QUERY, 0), (load_act, QUERY, 1), (load_act, TRAIN, 0), (load_slope, TRAIN, [2]), (load_w, 1), (load_bytes, 5), (load_act, TRAIN, 1), (load_slope, TRAIN, [3]),
            (load_w, 2), (load_slope, TRAIN, [4, 5]), (load_bytes, 6), (load_err_query, 0), (load_err_query, 1), (load_w, 3), (load_bytes, 7), (load_slope, QUERY, [0, 1]), (load_err_query, 2), (load_err_query, 3), (load_w, 4), (load_w, 6), (load_slope, QUERY, [2, 3]), (load_act, TRAIN, 2), (load_slope, TRAIN, [6, 7]),
            (load_w, 5), (load_w, 7), (load_act, TRAIN, 3)]
        left, right = slice(0, 256), slice(256, N)
        sync += each(store, [1, 0, 2, 4, 3, 5, 6]) + [(store, 7, left), (store, 7, right)]
        tensor = each(turn, et(0)[:1], True) + each(turn, et(0)[1:] + et(1)[:1], True) + [(back, TRAIN, 0, h, slice(0, 1)) for h in range(2)] + each(turn, et(1)[1:], True) + [(back, TRAIN, 0, h, slice(1, 2)) for h in range(2)] + each(turn, et(2)) + [(back, TRAIN, 0, 0, hi), (back, TRAIN, 0, 1, hi)] + both(back, TRAIN, [1])
        vector = each(empty, et(0)[:2]) + apart(et(0)[:1]) + each(empty, et(0)[2:]) + apart(et(0)[1:2]) + each(empty, et(1)[:1]) + apart(et(0)[2:]) + each(empty, et(1)[1:]) + apart(et(1))
        vector += each(empty, et(2)[::-1]) + both(times_slope, TRAIN, [0, 1], (1, 0))
        scalar = each(widen, et(0) + et(1)) + prep(2) + [step for i in (3, 4) for step in each(widen, et(i)) + sorts(et(i)[::-1])]
        held = ["w_laid0", "w_laid0", "w_laid0", "w_laid0", "w_laid1", "w_laid1"]
        gpsimd = [(lay_w, piece, "gpsimd", held[piece], dt(1) if piece == 4 else []) for piece in range(6)]
        tensor += each(turn, et(3)) + each(turn, aq(0), True) + both(back, TRAIN, [2], [0]) + each(turn, aq(1), True) + both(back, TRAIN, [2], [1])
        vector += joined(et(2)) + each(empty, et(3)[::-1]) + apart(aq(0)[::-1]) + joined(et(3)) + [(quantise_w, 0)] + both(times_slope, TRAIN, [2])
        scalar += each(empty, aq(0)) + sorts(at(0)[:1]) + each(empty, aq(1)) + sorts(at(0)[1:])
        for i in (4, 5):
            pair = i - 4
            tensor += turn_err(i) + each(turn, at(pair) + (dt(0) if i == 4 else [])) + both(back, TRAIN, [i - 1]) + each(gram_act, [2 * pair, 2 * pair + 1])
            vector += each(empty, et(i)) + apart(aq(1)[::-1] if i == 4 else []) + joined(at(pair)[:2], at(pair)[2:], et(i)) + apart(dt(0) if i == 4 else []) + [(quantise_w, i - 3)] + both(times_slope, TRAIN, [i - 1], (1, 0)) + each(keep_gram, [2] if i == 5 else [], "vector")
            scalar += each(empty, at(pair) + (dt(0) if i == 4 else [])) + prep(i + 1) + (sorts(at(1)) if i < 5 else sorts_eq(0, 1)) + each(keep_gram, [0, 1] if i == 4 else [3])
        tensor += turn_err(6) + each(turn, eq(0, 1) + dt(1)) + both(back, TRAIN, [5]) + both(back, QUERY, [0, 1], [0])
        vector += each(empty, et(6)) + [(quantise_w, 3)] + joined(eq(0), eq(1), et(6), dt(1)) + both(times_slope, TRAIN, [5], (1, 0)) + both(times_slope, QUERY, [0, 1], [0])
        scalar += each(empty, eq(0, 1)) + each(empty, dt(1), "scalar", "w_laid1") + sorts_eq(2, 3) + each(widen, et(7))
        tensor += each(turn, eq(2, 3) + dt(2) + dq(0, 0)) + both(back, TRAIN, [6]) + both(back, QUERY, [2], [0])
        vector += each(empty, eq(2), "vector") + joined(eq(2), eq(3)) + [(quantise_w, 4)] + both(times_slope, TRAIN, [6], (1, 0)) + both(times_slope, QUERY, [2], [0])
        scalar += each(empty, eq(3) + dt(2) + dq(0, 0)) + sorts(et(7) + at(2))
        three, last = slice(0, 3), slice(3, 4)
        tensor += turn_err(7) + each(turn, at(2) + dt(3, 4)) + both(back, QUERY, [3], [0]) + each(gram_act, [4, 5]) + [(back, QUERY, i, 1, three) for i in range(3)] + [(back, QUERY, i, 1, last) for i in range(3)] + [(back, QUERY, 3, 1)]
        vector += each(empty, et(7)) + joined(at(2)[:2], at(2)[2:]) + [(quantise_w, 5)] + both(times_slope, QUERY, [3], [0]) + [(quantise_w, 6)] + joined(et(7)) + [(quantise_w, 7)] + joined(dt(2, 3)) + both(times_slope, QUERY, range(4), [1])
        scalar += each(empty, at(2)) + [(lay_w, 6, "scalar", "w_laid0"), (lay_w, 7, "scalar")] + each(empty, dt(3, 4)) + each(keep_gram, [4, 5]) + sorts(at(3)[::-1])
        tensor += each(turn, dq(1, 0) + dq(0, 1) + dt(5) + at(3)[:1] + dq(1, 1) + at(3)[1:]) + both(back, TRAIN, [7]) + each(gram_err, [0, 1, 2]) + each(turn, dt(6, 7)) + [(gram_act, 6), (gram_err, 3), (gram_err, 4), (gram_err, 5), (gram_act, 7), (gram_err, 6), (gram_err, 7, slice(0, 2), left), (gram_err, 7, slice(0, 2), right)]
        vector += joined(dq(0, 0) + dq(1, 0), dq(0, 1) + dq(1, 1)) + both(times_slope, TRAIN, [7]) + joined(at(3)[:2], at(3)[2:], dt(4, 5)) + each(finish, [1, 0, 2]) + joined(dt(6, 7)) + each(finish, [4, 3, 5, 6]) + [(finish, 7, left), (finish, 7, right)]
        scalar += each(empty, dq(1, 0) + dq(0, 1) + dq(1, 1) + at(3) + dt(5, 6, 7)) + each(keep_gram, [6, 7])
        with tc.manual_schedule():
            make_identity(nc, ident[:])
            nc.vector.memset(v_planes[:].rearrange("p g n -> p (g n)").bitcast(I32), 0)
            write_out([sync, vector, scalar, gpsimd, tensor])
